import numpy as np
import ml_dtypes


def mxq(x, axis, fmt="e4m3"):
    dtype, down = {"e4m3": (ml_dtypes.float8_e4m3fn, 7), "e5m2": (ml_dtypes.float8_e5m2, 14)}[fmt]
    v = np.moveaxis(np.asarray(x, np.float32).astype(ml_dtypes.bfloat16).astype(np.float64), axis, -1)
    blocks = v.reshape(v.shape[:-1] + (-1, 32))
    amax = np.abs(blocks).max(-1, keepdims=True)
    byte = np.maximum(np.where(amax > 0, np.frexp(amax)[1] - 1 + 127, 0) - down, 1)
    scale = np.exp2(byte - 127.0)
    codes = (blocks / scale).astype(np.float32).astype(dtype).astype(np.float64)
    return np.moveaxis((codes * scale).reshape(v.shape), -1, axis)


WIDE = False


def mx_kscale(k):
    if not WIDE:
        return np.ones(k)
    levels = np.array([10, -10, 5, -5, 0])
    if k % 512:
        return np.exp2(np.random.permutation(np.resize(levels, k // 32))).repeat(32)
    a = np.empty((k // 512, 16))
    for p in range(k // 512):
        a[p, :8] = np.random.permutation(np.resize(levels, 8))
        for g in range(8):
            far = levels[np.abs(levels - a[p, g]) >= 10]
            a[p, g + 8] = far[np.random.randint(len(far))]
    return np.exp2(a.ravel()).repeat(32)


def f64(x):
    return np.asarray(x).astype(np.float64)


def striped(idx):
    return np.tile(idx.reshape(-1, 16).T, (8, 1)).astype(np.uint16)


def unstriped(offs):
    return offs[:16].T.reshape(-1).astype(np.int64)


def pack_weight(w):
    k, n = w.shape
    w = f64(np.asarray(w, np.float32).astype(ml_dtypes.bfloat16)).reshape(k // 32, 32, n)
    amax = np.abs(w).max(1)
    byte = np.clip(np.where(amax > 0, np.frexp(amax)[1] - 1 + 127 - 7, 1), 1, 254)
    scaled = (w * np.exp2(127.0 - byte)[:, None, :]).reshape(k, n).astype(np.float32)
    words = np.ascontiguousarray(scaled.reshape(k // 512, 128, 4, n).transpose(0, 1, 3, 2)).astype(ml_dtypes.float8_e4m3fn).view(np.uint8)
    return words, np.ascontiguousarray(byte.astype(np.uint8).reshape(k // 512, 16, n))


def unpack_weight(words, scales):
    g, p, n, _ = words.shape
    vals = np.ascontiguousarray(words).view(ml_dtypes.float8_e4m3fn).astype(np.float64) * np.repeat(np.exp2(scales.astype(np.float64) - 127.0), 8, axis=1)[..., None]
    return vals.transpose(0, 1, 3, 2).reshape(g * 512, n)


def gelu(v):
    return 0.5 * v * (1.0 + np.tanh(np.sqrt(2.0 / np.pi) * (v + 0.044715 * v**3)))


K, T, E, C, N = 512, 1024, 8, 128, 512


def by_expert(wq, xq):
    return np.concatenate([wq[e].T @ xq[:, e * C:(e + 1) * C] for e in range(E)], axis=1)


def setup_inputs():
    n = np.random.standard_normal
    s = mx_kscale(K)[:, None]
    packed = [pack_weight(m) for m in n((E, K, N)) / np.sqrt(K) / s[None]]
    return {
        "xT": (n((K, T)) * s).astype(np.float32),
        "w_words": np.stack([m[0] for m in packed]),
        "w_scales": np.stack([m[1] for m in packed]),
        "b": (0.3 * n((N, E))).astype(np.float32),
        "gate": np.tile(np.random.uniform(0.2, 1.0, E * C), (N, 1)).astype(np.float32),
        "offs": striped(np.random.permutation(T)[:E * C]),
    }


def reference(xT, w_words, w_scales, b, gate, offs):
    idx = unstriped(offs)
    xq = mxq(f64(xT)[:, idx], 0, "e4m3")
    w = np.stack([unpack_weight(w_words[e], w_scales[e]) for e in range(E)])
    y = by_expert(w, xq)
    y = gelu(y + np.repeat(f64(b), C, axis=1))
    out = np.zeros((N, T))
    out[:, idx] = f64(gate) * y
    return out

@@ -1,0 +1,152 @@
+from contextlib import ExitStack
+
+import concourse.mybir as mybir
+
+K, T, E, C, N = 512, 1024, 8, 128, 512
+P = 128
+PACK = 4
+SLOTS = E * C
+BLOCKS = N // P
+HALF = SLOTS // 2
+
+F32 = mybir.dt.float32
+BF16 = mybir.dt.bfloat16
+U32 = mybir.dt.uint32
+I32 = mybir.dt.int32
+U16 = mybir.dt.uint16
+U8 = mybir.dt.uint8
+FP8X4 = mybir.dt.float8_e4m3fn_x4
+MULT = mybir.AluOpType.mult
+GELU = mybir.ActivationFunctionType.Gelu_apprx_tanh
+
+FLOPS = 2 * K * N * SLOTS
+BYTES = 4 * K * T + E * K * N + E * (K // 32) * N + 4 * N * E + 4 * SLOTS + 2 * 128 * SLOTS // 16 + 4 * N * T
+
+ORDER = (2, 0, 1, 3)
+COPY = mybir.ActivationFunctionType.Copy
+
+
+def tile_routed_moe_kernel(tc, xT, w_words, w_scales, b, gate, offs, out):
+    nc = tc.nc
+    with ExitStack() as ctx:
+        keep = ctx.enter_context(tc.tile_pool(name="keep", bufs=1))
+        stage = ctx.enter_context(tc.tile_pool(name="stage", bufs=1))
+        ring = ctx.enter_context(tc.tile_pool(name="ring", bufs=3))
+        psum = ctx.enter_context(tc.psum_pool(name="psum", bufs=1))
+
+        offsets = keep.tile([P, SLOTS // 16], U16, name="offsets")
+        bias = keep.tile([P, BLOCKS, E], F32, name="bias")
+        bias_first = stage.tile([P, PACK], F32, name="bias_first", tag="grouped", align_bytes=64)
+        gates = keep.tile([P, SLOTS], F32, name="gates")
+        warm = keep.tile([P, 1], F32, name="warm")
+        planes = [keep.tile([P, N], U8, name=f"planes{h}", align_bytes=64) for h in range(2)]
+
+        for h in range(2):
+            nc.gpsimd.memset(planes[h][:].bitcast(I32), 0)
+        nc.vector.memset(warm[:], 0.0)
+        nc.scalar.activation(warm[:], warm[:], GELU)
+
+        x_rows = xT.rearrange("(p j) t -> p j t", j=PACK)
+
+        def load_scales(h):
+            for q in range(4):
+                nc.sync.dma_start(
+                    planes[h][32 * q : 32 * q + 16, :].bitcast(I32),
+                    w_scales[4 * h : 4 * h + 4, 0, 4 * q : 4 * q + 4, :].bitcast(I32),
+                )
+
+        nc.sync.dma_start(offsets[:], offs)
+        raws = [keep.tile([P, T], F32, name=f"raw{j}") for j in range(PACK)]
+        for j in ORDER:
+            nc.sync.dma_start(raws[j][:], x_rows[:, j, :])
+        load_scales(0)
+        nc.sync.dma_start(bias_first[:], b[0:P, 0:PACK])
+        words = []
+        for e in range(0, E, 2):
+            w_pair = keep.tile([P, 2, N], U32, name=f"words{e}", align_bytes=64)
+            nc.sync.dma_start(w_pair[:].bitcast(I32), w_words[e : e + 2].rearrange("e a p n r -> p (e a) (n r)").bitcast(I32))
+            words.append(w_pair)
+            if e == 0:
+                nc.sync.dma_start(gates[:, 0:256], gate[0:P, 0:256])
+                nc.sync.dma_start(bias[:], b.rearrange("(c p) e -> p c e", p=P))
+            if e == 2:
+                nc.sync.dma_start(gates[:, 256:512], gate[0:P, 256:512])
+                load_scales(1)
+                nc.sync.dma_start(gates[:, 512:SLOTS], gate[0:P, 512:SLOTS])
+
+        rounded = [keep.tile([P, T], BF16, name=f"rounded{j}") for j in range(PACK)]
+        banks = [[psum.tile([P, PACK, C], F32, name=f"bank{n}{h}") for h in range(2)] for n in range(BLOCKS)]
+        windows = [keep.tile([P, T], F32, name=f"window{n}") for n in range(BLOCKS)]
+
+        def vector_gather(grouped, s0, s1, j):
+            nc.vector.tensor_copy(grouped[:, s0:s1, j], raws[j][:].indirect(offsets[:, s0 // 16 : s1 // 16]))
+
+        def scalar_gather(grouped, s0, s1, j):
+            nc.scalar.activation(grouped[:, s0 % HALF : s0 % HALF + s1 - s0, j], rounded[j][:].indirect(offsets[:, s0 // 16 : s1 // 16]), COPY)
+
+        def multiply(s0, s1, grouped):
+            codes = keep.tile([P, s1 - s0], U32, name=f"codes{s0}", align_bytes=64)
+            scales = keep.tile([P, s1 - s0], U8, name=f"scales{s0}", align_bytes=64)
+            nc.vector.quantize_mx(out=codes[:].bitcast(FP8X4), scales=scales[:], in_=grouped[:, s0 % HALF : s0 % HALF + s1 - s0].rearrange("p s j -> p (s j)"))
+            for n in range(BLOCKS):
+                feats = slice(n * P, (n + 1) * P)
+                for e in range(s0 // C, s1 // C):
+                    cols = slice(e * C - s0, (e + 1) * C - s0)
+                    nc.tensor.matmul_mx(
+                        out=banks[n][e // PACK][:, e % PACK, :],
+                        lhsT=words[e // 2][:, e % 2, feats].bitcast(FP8X4),
+                        lhsT_scale=planes[e // PACK][4 * (e % PACK) : P, feats],
+                        rhs=codes[:, cols].bitcast(FP8X4),
+                        rhs_scale=scales[:, cols],
+                        start=True,
+                        stop=True,
+                    )
+
+        def activate(y, n, e):
+            column = bias_first[:, e : e + 1] if n == 0 and e < PACK else bias[:, n, e : e + 1]
+            nc.scalar.activation(y[:, (e % PACK) * C : (e % PACK + 1) * C], banks[n][e // PACK][:, e % PACK, :], GELU, bias=column)
+
+        def scatter(y, n, s0, s1):
+            nc.vector.tensor_tensor(
+                windows[n][:].indirect(offsets[:, s0 // 16 : s1 // 16]),
+                y[:, s0 % HALF : s0 % HALF + s1 - s0],
+                gates[:, s0:s1],
+                MULT,
+            )
+
+        def finish(y, n, s0, s1):
+            for e in range(s0 // C, s1 // C):
+                activate(y, n, e)
+            scatter(y, n, s0, s1)
+
+        def new_y(n, h):
+            return ring.tile([P, HALF], F32, name=f"y{n}{h}", tag="y")
+
+        part_a = keep.tile([P, HALF, PACK], BF16, name="part_a", align_bytes=64)
+        nc.scalar.copy(rounded[2][:], raws[2][:])
+        vector_gather(part_a, 0, 256, 2)
+        for j in range(2):
+            nc.vector.tensor_copy(rounded[j][:], raws[j][:])
+            scalar_gather(part_a, 0, 256, j)
+            scalar_gather(part_a, 256, 384, j)
+            vector_gather(part_a, 384, HALF, j)
+        vector_gather(part_a, 0, 256, 3)
+        nc.vector.tensor_copy(rounded[3][:], raws[3][:])
+        for j in range(2, PACK):
+            scalar_gather(part_a, 256, HALF, j)
+        multiply(0, 256, part_a)
+        y = new_y(0, 0)
+        finish(y, 0, 0, 256)
+        multiply(256, HALF, part_a)
+
+        finish(y, 0, 256, HALF)
+        finish(new_y(1, 0), 1, 0, HALF)
+        finish(new_y(2, 0), 2, 0, HALF)
+        part_c = stage.tile([P, HALF, PACK], BF16, name="part_c", tag="grouped", align_bytes=64)
+        for j in range(PACK):
+            scalar_gather(part_c, HALF, SLOTS, j)
+        multiply(HALF, SLOTS, part_c)
+        finish(new_y(3, 0), 3, 0, HALF)
+        for n in range(BLOCKS):
+            finish(new_y(n, 1), n, HALF, SLOTS)
+            nc.sync.dma_start(out[n * P : (n + 1) * P, :], windows[n][:])

@@ -7,7 +7,6 @@ P = 128
 PACK = 4
 SLOTS = E * C
 BLOCKS = N // P
-HALF = SLOTS // 2
 
 F32 = mybir.dt.float32
 BF16 = mybir.dt.bfloat16
@@ -18,25 +17,23 @@ U8 = mybir.dt.uint8
 FP8X4 = mybir.dt.float8_e4m3fn_x4
 MULT = mybir.AluOpType.mult
 GELU = mybir.ActivationFunctionType.Gelu_apprx_tanh
+COPY = mybir.ActivationFunctionType.Copy
 
 FLOPS = 2 * K * N * SLOTS
 BYTES = 4 * K * T + E * K * N + E * (K // 32) * N + 4 * N * E + 4 * SLOTS + 2 * 128 * SLOTS // 16 + 4 * N * T
 
-ORDER = (2, 0, 1, 3)
-COPY = mybir.ActivationFunctionType.Copy
+PHASES = ((0, 1), (1, 4), (4, 6), (6, 8))
 
 
 def tile_routed_moe_kernel(tc, xT, w_words, w_scales, b, gate, offs, out):
     nc = tc.nc
     with ExitStack() as ctx:
         keep = ctx.enter_context(tc.tile_pool(name="keep", bufs=1))
-        stage = ctx.enter_context(tc.tile_pool(name="stage", bufs=1))
         ring = ctx.enter_context(tc.tile_pool(name="ring", bufs=3))
         psum = ctx.enter_context(tc.psum_pool(name="psum", bufs=1))
 
         offsets = keep.tile([P, SLOTS // 16], U16, name="offsets")
         bias = keep.tile([P, BLOCKS, E], F32, name="bias")
-        bias_first = stage.tile([P, PACK], F32, name="bias_first", tag="grouped", align_bytes=64)
         gates = keep.tile([P, SLOTS], F32, name="gates")
         warm = keep.tile([P, 1], F32, name="warm")
         planes = [keep.tile([P, N], U8, name=f"planes{h}", align_bytes=64) for h in range(2)]
@@ -57,96 +54,95 @@ def tile_routed_moe_kernel(tc, xT, w_words, w_scales, b, gate, offs, out):
 
         nc.sync.dma_start(offsets[:], offs)
         raws = [keep.tile([P, T], F32, name=f"raw{j}") for j in range(PACK)]
-        for j in ORDER:
+        for j in range(PACK):
             nc.sync.dma_start(raws[j][:], x_rows[:, j, :])
-        load_scales(0)
-        nc.sync.dma_start(bias_first[:], b[0:P, 0:PACK])
+        w_rows = w_words.rearrange("e a p n r -> p (e a) (n r)").bitcast(I32)
         words = []
-        for e in range(0, E, 2):
-            w_pair = keep.tile([P, 2, N], U32, name=f"words{e}", align_bytes=64)
-            nc.sync.dma_start(w_pair[:].bitcast(I32), w_words[e : e + 2].rearrange("e a p n r -> p (e a) (n r)").bitcast(I32))
-            words.append(w_pair)
-            if e == 0:
-                nc.sync.dma_start(gates[:, 0:256], gate[0:P, 0:256])
+        for i, (e0, e1) in enumerate(PHASES):
+            if e0 % 4 == 0:
+                load_scales(e0 // 4)
+            w = keep.tile([P, e1 - e0, N], U32, name=f"words{i}", align_bytes=64)
+            nc.sync.dma_start(w[:].bitcast(I32), w_rows[:, e0:e1, :])
+            words.append(w)
+            if i == 0:
                 nc.sync.dma_start(bias[:], b.rearrange("(c p) e -> p c e", p=P))
-            if e == 2:
-                nc.sync.dma_start(gates[:, 256:512], gate[0:P, 256:512])
-                load_scales(1)
-                nc.sync.dma_start(gates[:, 512:SLOTS], gate[0:P, 512:SLOTS])
+            nc.sync.dma_start(gates[:, e0 * C : e1 * C], gate[0:P, e0 * C : e1 * C])
 
-        rounded = [keep.tile([P, T], BF16, name=f"rounded{j}") for j in range(PACK)]
-        banks = [[psum.tile([P, PACK, C], F32, name=f"bank{n}{h}") for h in range(2)] for n in range(BLOCKS)]
+        banks = [psum.tile([P, 4 * C], F32, name=f"bank{i}") for i in range(8)]
         windows = [keep.tile([P, T], F32, name=f"window{n}") for n in range(BLOCKS)]
 
-        def vector_gather(grouped, s0, s1, j):
-            nc.vector.tensor_copy(grouped[:, s0:s1, j], raws[j][:].indirect(offsets[:, s0 // 16 : s1 // 16]))
+        def listed(e0, e1):
+            return offsets[:, e0 * C // 16 : e1 * C // 16]
 
-        def scalar_gather(grouped, s0, s1, j):
-            nc.scalar.activation(grouped[:, s0 % HALF : s0 % HALF + s1 - s0, j], rounded[j][:].indirect(offsets[:, s0 // 16 : s1 // 16]), COPY)
+        def sums(n, e):
+            if e < 4:
+                return banks[n][:, e * C : (e + 1) * C]
+            i = 4 + 2 * ((e - 4) // 2) + n // 2
+            c0 = (2 * (n % 2) + e % 2) * C
+            return banks[i][:, c0 : c0 + C]
 
-        def multiply(s0, s1, grouped):
-            codes = keep.tile([P, s1 - s0], U32, name=f"codes{s0}", align_bytes=64)
-            scales = keep.tile([P, s1 - s0], U8, name=f"scales{s0}", align_bytes=64)
-            nc.vector.quantize_mx(out=codes[:].bitcast(FP8X4), scales=scales[:], in_=grouped[:, s0 % HALF : s0 % HALF + s1 - s0].rearrange("p s j -> p (s j)"))
+        def new_grouped(i, tag):
+            e0, e1 = PHASES[i]
+            return keep.tile([P, (e1 - e0) * C, PACK], BF16, name=f"grouped{i}", tag=tag, align_bytes=64)
+
+        def multiply(i, grouped):
+            e0, e1 = PHASES[i]
+            codes = keep.tile([P, (e1 - e0) * C], U32, name=f"codes{i}", tag=f"codes{i}", align_bytes=64)
+            scales = keep.tile([P, (e1 - e0) * C], U8, name=f"scales{i}", align_bytes=64)
+            cuts = [0, C, 3 * C] if e1 - e0 == 3 else [0, (e1 - e0) * C]
+            for s0, s1 in zip(cuts, cuts[1:]):
+                nc.vector.quantize_mx(out=codes[:, s0:s1].bitcast(FP8X4), scales=scales[:, s0:s1], in_=grouped[:, s0:s1].rearrange("p s j -> p (s j)"))
             for n in range(BLOCKS):
                 feats = slice(n * P, (n + 1) * P)
-                for e in range(s0 // C, s1 // C):
-                    cols = slice(e * C - s0, (e + 1) * C - s0)
+                for e in range(e0, e1):
+                    cols = slice((e - e0) * C, (e - e0 + 1) * C)
                     nc.tensor.matmul_mx(
-                        out=banks[n][e // PACK][:, e % PACK, :],
-                        lhsT=words[e // 2][:, e % 2, feats].bitcast(FP8X4),
-                        lhsT_scale=planes[e // PACK][4 * (e % PACK) : P, feats],
+                        out=sums(n, e),
+                        lhsT=words[i][:, e - e0, feats].bitcast(FP8X4),
+                        lhsT_scale=planes[e // 4][4 * (e % 4) : P, feats],
                         rhs=codes[:, cols].bitcast(FP8X4),
                         rhs_scale=scales[:, cols],
                         start=True,
                         stop=True,
                     )
 
-        def activate(y, n, e):
-            column = bias_first[:, e : e + 1] if n == 0 and e < PACK else bias[:, n, e : e + 1]
-            nc.scalar.activation(y[:, (e % PACK) * C : (e % PACK + 1) * C], banks[n][e // PACK][:, e % PACK, :], GELU, bias=column)
+        def finish(i, n):
+            e0, e1 = PHASES[i]
+            y = ring.tile([P, (e1 - e0) * C], F32, name=f"y{i}{n}", tag="y")
+            for e in range(e0, e1):
+                nc.scalar.activation(y[:, (e - e0) * C : (e - e0 + 1) * C], sums(n, e), GELU, bias=bias[:, n, e : e + 1])
+            nc.vector.tensor_tensor(windows[n][:].indirect(listed(e0, e1)), y[:], gates[:, e0 * C : e1 * C], MULT)
+            if e1 == E:
+                nc.sync.dma_start(out[n * P : (n + 1) * P, :], windows[n][:])
 
-        def scatter(y, n, s0, s1):
-            nc.vector.tensor_tensor(
-                windows[n][:].indirect(offsets[:, s0 // 16 : s1 // 16]),
-                y[:, s0 % HALF : s0 % HALF + s1 - s0],
-                gates[:, s0:s1],
-                MULT,
-            )
+        def scalar_gather(i, grouped, j):
+            nc.scalar.activation(grouped[:, :, j], rounded[j][:].indirect(listed(*PHASES[i])), COPY)
 
-        def finish(y, n, s0, s1):
-            for e in range(s0 // C, s1 // C):
-                activate(y, n, e)
-            scatter(y, n, s0, s1)
-
-        def new_y(n, h):
-            return ring.tile([P, HALF], F32, name=f"y{n}{h}", tag="y")
-
-        part_a = keep.tile([P, HALF, PACK], BF16, name="part_a", align_bytes=64)
-        nc.scalar.copy(rounded[2][:], raws[2][:])
-        vector_gather(part_a, 0, 256, 2)
-        for j in range(2):
+        first = new_grouped(0, "first")
+        second = new_grouped(1, "second")
+        rounded = []
+        for j in range(PACK - 1):
+            rounded.append(keep.tile([P, T], BF16, name=f"rounded{j}"))
             nc.vector.tensor_copy(rounded[j][:], raws[j][:])
-            scalar_gather(part_a, 0, 256, j)
-            scalar_gather(part_a, 256, 384, j)
-            vector_gather(part_a, 384, HALF, j)
-        vector_gather(part_a, 0, 256, 3)
-        nc.vector.tensor_copy(rounded[3][:], raws[3][:])
-        for j in range(2, PACK):
-            scalar_gather(part_a, 256, HALF, j)
-        multiply(0, 256, part_a)
-        y = new_y(0, 0)
-        finish(y, 0, 0, 256)
-        multiply(256, HALF, part_a)
-
-        finish(y, 0, 256, HALF)
-        finish(new_y(1, 0), 1, 0, HALF)
-        finish(new_y(2, 0), 2, 0, HALF)
-        part_c = stage.tile([P, HALF, PACK], BF16, name="part_c", tag="grouped", align_bytes=64)
-        for j in range(PACK):
-            scalar_gather(part_c, HALF, SLOTS, j)
-        multiply(HALF, SLOTS, part_c)
-        finish(new_y(3, 0), 3, 0, HALF)
-        for n in range(BLOCKS):
-            finish(new_y(n, 1), n, HALF, SLOTS)
-            nc.sync.dma_start(out[n * P : (n + 1) * P, :], windows[n][:])
+            nc.vector.tensor_copy(first[:, :, j], raws[j][:].indirect(listed(0, 1)))
+            scalar_gather(1, second, j)
+        last = PACK - 1
+        nc.vector.tensor_copy(first[:, :, last], raws[last][:].indirect(listed(0, 1)))
+        multiply(0, first)
+        rounded.append(keep.tile([P, T], BF16, name="rounded_last", tag="first", align_bytes=64))
+        nc.vector.tensor_copy(rounded[last][:], raws[last][:])
+        for n in range(BLOCKS - 1):
+            finish(0, n)
+        scalar_gather(1, second, last)
+        finish(0, BLOCKS - 1)
+        multiply(1, second)
+        for i in range(1, len(PHASES)):
+            finish(i, 0)
+            finish(i, 1)
+            if i + 1 < len(PHASES):
+                grouped = new_grouped(i + 1, f"codes{i}")
+                for j in range(PACK):
+                    scalar_gather(i + 1, grouped, j)
+                multiply(i + 1, grouped)
+            finish(i, 2)
+            finish(i, 3)

@@ -22,14 +22,11 @@ COPY = mybir.ActivationFunctionType.Copy
 FLOPS = 2 * K * N * SLOTS
 BYTES = 4 * K * T + E * K * N + E * (K // 32) * N + 4 * N * E + 4 * SLOTS + 2 * 128 * SLOTS // 16 + 4 * N * T
 
-PHASES = ((0, 1), (1, 4), (4, 6), (6, 8))
-
 
 def tile_routed_moe_kernel(tc, xT, w_words, w_scales, b, gate, offs, out):
     nc = tc.nc
     with ExitStack() as ctx:
         keep = ctx.enter_context(tc.tile_pool(name="keep", bufs=1))
-        ring = ctx.enter_context(tc.tile_pool(name="ring", bufs=3))
         psum = ctx.enter_context(tc.psum_pool(name="psum", bufs=1))
 
         offsets = keep.tile([P, SLOTS // 16], U16, name="offsets")
@@ -44,6 +41,8 @@ def tile_routed_moe_kernel(tc, xT, w_words, w_scales, b, gate, offs, out):
         nc.scalar.activation(warm[:], warm[:], GELU)
 
         x_rows = xT.rearrange("(p j) t -> p j t", j=PACK)
+        w_rows = w_words.rearrange("e a p n r -> p (e a) (n r)").bitcast(I32)
+        words = keep.tile([P, E, N], U32, name="words", align_bytes=64)
 
         def load_scales(h):
             for q in range(4):
@@ -52,97 +51,98 @@ def tile_routed_moe_kernel(tc, xT, w_words, w_scales, b, gate, offs, out):
                     w_scales[4 * h : 4 * h + 4, 0, 4 * q : 4 * q + 4, :].bitcast(I32),
                 )
 
+        def load_words(e0, e1):
+            nc.sync.dma_start(words[:, e0:e1, :].bitcast(I32), w_rows[:, e0:e1, :])
+
+        def load_gates(e0, e1):
+            nc.sync.dma_start(gates[:, e0 * C : e1 * C], gate[0:P, e0 * C : e1 * C])
+
         nc.sync.dma_start(offsets[:], offs)
         raws = [keep.tile([P, T], F32, name=f"raw{j}") for j in range(PACK)]
         for j in range(PACK):
             nc.sync.dma_start(raws[j][:], x_rows[:, j, :])
-        w_rows = w_words.rearrange("e a p n r -> p (e a) (n r)").bitcast(I32)
-        words = []
-        for i, (e0, e1) in enumerate(PHASES):
-            if e0 % 4 == 0:
-                load_scales(e0 // 4)
-            w = keep.tile([P, e1 - e0, N], U32, name=f"words{i}", align_bytes=64)
-            nc.sync.dma_start(w[:].bitcast(I32), w_rows[:, e0:e1, :])
-            words.append(w)
-            if i == 0:
-                nc.sync.dma_start(bias[:], b.rearrange("(c p) e -> p c e", p=P))
-            nc.sync.dma_start(gates[:, e0 * C : e1 * C], gate[0:P, e0 * C : e1 * C])
+        load_scales(0)
+        load_words(0, 1)
+        nc.sync.dma_start(bias[:], b.rearrange("(c p) e -> p c e", p=P))
+        load_gates(0, 1)
+        load_words(1, 4)
+        load_gates(1, 4)
+        load_scales(1)
+        load_words(4, 8)
+        load_gates(4, 8)
 
-        banks = [psum.tile([P, 4 * C], F32, name=f"bank{i}") for i in range(8)]
-        windows = [keep.tile([P, T], F32, name=f"window{n}") for n in range(BLOCKS)]
+        banks = [[psum.tile([P, PACK, C], F32, name=f"bank{n}{h}") for h in range(2)] for n in range(BLOCKS)]
+        scales = keep.tile([P, SLOTS], U8, name="scales", align_bytes=64)
 
         def listed(e0, e1):
             return offsets[:, e0 * C // 16 : e1 * C // 16]
 
-        def sums(n, e):
-            if e < 4:
-                return banks[n][:, e * C : (e + 1) * C]
-            i = 4 + 2 * ((e - 4) // 2) + n // 2
-            c0 = (2 * (n % 2) + e % 2) * C
-            return banks[i][:, c0 : c0 + C]
-
-        def new_grouped(i, tag):
-            e0, e1 = PHASES[i]
-            return keep.tile([P, (e1 - e0) * C, PACK], BF16, name=f"grouped{i}", tag=tag, align_bytes=64)
-
-        def multiply(i, grouped):
-            e0, e1 = PHASES[i]
-            codes = keep.tile([P, (e1 - e0) * C], U32, name=f"codes{i}", tag=f"codes{i}", align_bytes=64)
-            scales = keep.tile([P, (e1 - e0) * C], U8, name=f"scales{i}", align_bytes=64)
-            cuts = [0, C, 3 * C] if e1 - e0 == 3 else [0, (e1 - e0) * C]
+        def multiply(e0, e1, grouped, tag, blocks):
+            codes = keep.tile([P, (e1 - e0) * C], U32, name=f"codes{e0}", tag=tag, align_bytes=64)
+            cuts = (0, C, 3 * C) if e1 - e0 == 3 else (0, (e1 - e0) * C)
             for s0, s1 in zip(cuts, cuts[1:]):
-                nc.vector.quantize_mx(out=codes[:, s0:s1].bitcast(FP8X4), scales=scales[:, s0:s1], in_=grouped[:, s0:s1].rearrange("p s j -> p (s j)"))
-            for n in range(BLOCKS):
+                nc.vector.quantize_mx(
+                    out=codes[:, s0:s1].bitcast(FP8X4),
+                    scales=scales[:, e0 * C + s0 : e0 * C + s1],
+                    in_=grouped[:, s0:s1].rearrange("p s j -> p (s j)"),
+                )
+            for n in blocks:
                 feats = slice(n * P, (n + 1) * P)
                 for e in range(e0, e1):
-                    cols = slice((e - e0) * C, (e - e0 + 1) * C)
+                    slots = slice(e * C, (e + 1) * C)
                     nc.tensor.matmul_mx(
-                        out=sums(n, e),
-                        lhsT=words[i][:, e - e0, feats].bitcast(FP8X4),
+                        out=banks[n][e // 4][:, e % 4, :],
+                        lhsT=words[:, e, feats].bitcast(FP8X4),
                         lhsT_scale=planes[e // 4][4 * (e % 4) : P, feats],
-                        rhs=codes[:, cols].bitcast(FP8X4),
-                        rhs_scale=scales[:, cols],
+                        rhs=codes[:, (e - e0) * C : (e - e0 + 1) * C].bitcast(FP8X4),
+                        rhs_scale=scales[:, slots],
                         start=True,
                         stop=True,
                     )
 
-        def finish(i, n):
-            e0, e1 = PHASES[i]
-            y = ring.tile([P, (e1 - e0) * C], F32, name=f"y{i}{n}", tag="y")
+        def finish(window, n, e0, e1, y):
             for e in range(e0, e1):
-                nc.scalar.activation(y[:, (e - e0) * C : (e - e0 + 1) * C], sums(n, e), GELU, bias=bias[:, n, e : e + 1])
-            nc.vector.tensor_tensor(windows[n][:].indirect(listed(e0, e1)), y[:], gates[:, e0 * C : e1 * C], MULT)
-            if e1 == E:
-                nc.sync.dma_start(out[n * P : (n + 1) * P, :], windows[n][:])
+                nc.scalar.activation(y[:, (e - e0) * C : (e - e0 + 1) * C], banks[n][e // 4][:, e % 4, :], GELU, bias=bias[:, n, e : e + 1])
+            nc.vector.tensor_tensor(window[:].indirect(listed(e0, e1)), y, gates[:, e0 * C : e1 * C], MULT)
 
-        def scalar_gather(i, grouped, j):
-            nc.scalar.activation(grouped[:, :, j], rounded[j][:].indirect(listed(*PHASES[i])), COPY)
+        def new_y(n, e0, e1, tag):
+            return keep.tile([P, (e1 - e0) * C], F32, name=f"y{n}{e0}", tag=tag)[:]
 
-        first = new_grouped(0, "first")
-        second = new_grouped(1, "second")
-        rounded = []
+        def vector_gather(grouped, e0, e1, j):
+            nc.vector.tensor_copy(grouped[:, :, j], raws[j][:].indirect(listed(e0, e1)))
+
+        def scalar_gather(grouped, e0, e1, j):
+            nc.scalar.activation(grouped[:, :, j], rounded[j][:].indirect(listed(e0, e1)), COPY)
+
+        first = keep.tile([P, C, PACK], BF16, name="first", tag="first", align_bytes=64)
+        second = keep.tile([P, 3 * C, PACK], BF16, name="second", tag="second", align_bytes=64)
+        rounded = {}
         for j in range(PACK - 1):
-            rounded.append(keep.tile([P, T], BF16, name=f"rounded{j}"))
+            rounded[j] = keep.tile([P, T], BF16, name=f"rounded{j}")
             nc.vector.tensor_copy(rounded[j][:], raws[j][:])
-            nc.vector.tensor_copy(first[:, :, j], raws[j][:].indirect(listed(0, 1)))
-            scalar_gather(1, second, j)
-        last = PACK - 1
-        nc.vector.tensor_copy(first[:, :, last], raws[last][:].indirect(listed(0, 1)))
-        multiply(0, first)
-        rounded.append(keep.tile([P, T], BF16, name="rounded_last", tag="first", align_bytes=64))
-        nc.vector.tensor_copy(rounded[last][:], raws[last][:])
-        for n in range(BLOCKS - 1):
-            finish(0, n)
-        scalar_gather(1, second, last)
-        finish(0, BLOCKS - 1)
-        multiply(1, second)
-        for i in range(1, len(PHASES)):
-            finish(i, 0)
-            finish(i, 1)
-            if i + 1 < len(PHASES):
-                grouped = new_grouped(i + 1, f"codes{i}")
-                for j in range(PACK):
-                    scalar_gather(i + 1, grouped, j)
-                multiply(i + 1, grouped)
-            finish(i, 2)
-            finish(i, 3)
+            vector_gather(first[:], 0, 1, j)
+            scalar_gather(second[:], 1, 4, j)
+        vector_gather(first[:], 0, 1, 3)
+        multiply(0, 1, first[:], "codes0", range(BLOCKS))
+        rounded[3] = keep.tile([P, T], BF16, name="rounded3", tag="first", align_bytes=64)
+        nc.vector.tensor_copy(rounded[3][:], raws[3][:])
+        windows = [keep.tile([P, T], F32, name=f"window{n}") for n in range(3)]
+        for n in range(3):
+            finish(windows[n], n, 0, 1, new_y(n, 0, 1, f"x{n}"))
+        y3 = new_y(3, 0, 1, "x3")
+        nc.scalar.activation(y3, banks[3][0][:, 0, :], GELU, bias=bias[:, 3, 0:1])
+        scalar_gather(second[:], 1, 4, 3)
+        multiply(1, 4, second[:], "third", range(BLOCKS))
+        windows.append(keep.tile([P, T], F32, name="window3", tag="second", align_bytes=64))
+        nc.vector.tensor_tensor(windows[3][:].indirect(listed(0, 1)), y3, gates[:, 0:C], MULT)
+        for n in range(3):
+            finish(windows[n], n, 1, 4, new_y(n, 1, 4, f"y{n}"))
+        third = keep.tile([P, 4 * C, PACK], BF16, name="third", tag="third", align_bytes=64)
+        for j in range(PACK):
+            scalar_gather(third[:], 4, 8, j)
+        multiply(4, 8, third[:], "codes4", range(BLOCKS))
+        y_late = keep.tile([P, 3 * C], F32, name="y_late", tag="first", align_bytes=64)
+        finish(windows[3], 3, 1, 4, y_late[:])
+        for n in range(BLOCKS):
+            finish(windows[n], n, 4, 8, new_y(n, 4, 8, f"z{n}"))
+            nc.sync.dma_start(out[n * P : (n + 1) * P, :], windows[n][:])

@@ -65,36 +65,31 @@ def tile_routed_moe_kernel(tc, xT, w_words, w_scales, b, gate, offs, out):
         load_words(0, 1)
         nc.sync.dma_start(bias[:], b.rearrange("(c p) e -> p c e", p=P))
         load_gates(0, 1)
-        load_words(1, 4)
+        load_words(1, 2)
         load_gates(1, 4)
+        load_words(2, 4)
         load_scales(1)
         load_words(4, 8)
         load_gates(4, 8)
 
         banks = [[psum.tile([P, PACK, C], F32, name=f"bank{n}{h}") for h in range(2)] for n in range(BLOCKS)]
-        scales = keep.tile([P, SLOTS], U8, name="scales", align_bytes=64)
 
         def listed(e0, e1):
             return offsets[:, e0 * C // 16 : e1 * C // 16]
 
-        def multiply(e0, e1, grouped, tag, blocks):
-            codes = keep.tile([P, (e1 - e0) * C], U32, name=f"codes{e0}", tag=tag, align_bytes=64)
-            cuts = (0, C, 3 * C) if e1 - e0 == 3 else (0, (e1 - e0) * C)
-            for s0, s1 in zip(cuts, cuts[1:]):
-                nc.vector.quantize_mx(
-                    out=codes[:, s0:s1].bitcast(FP8X4),
-                    scales=scales[:, e0 * C + s0 : e0 * C + s1],
-                    in_=grouped[:, s0:s1].rearrange("p s j -> p (s j)"),
-                )
-            for n in blocks:
+        def multiply(e0, e1, grouped):
+            codes = keep.tile([P, (e1 - e0) * C], U32, name=f"codes{e0}", tag=f"codes{e0}", align_bytes=64)
+            scales = keep.tile([P, (e1 - e0) * C], U8, name=f"scales{e0}", tag=f"scales{e0}", align_bytes=64)
+            nc.vector.quantize_mx(out=codes[:].bitcast(FP8X4), scales=scales[:], in_=grouped[:].rearrange("p s j -> p (s j)"))
+            for n in range(BLOCKS):
                 feats = slice(n * P, (n + 1) * P)
                 for e in range(e0, e1):
-                    slots = slice(e * C, (e + 1) * C)
+                    slots = slice((e - e0) * C, (e - e0 + 1) * C)
                     nc.tensor.matmul_mx(
                         out=banks[n][e // 4][:, e % 4, :],
                         lhsT=words[:, e, feats].bitcast(FP8X4),
                         lhsT_scale=planes[e // 4][4 * (e % 4) : P, feats],
-                        rhs=codes[:, (e - e0) * C : (e - e0 + 1) * C].bitcast(FP8X4),
+                        rhs=codes[:, slots].bitcast(FP8X4),
                         rhs_scale=scales[:, slots],
                         start=True,
                         stop=True,
@@ -114,35 +109,53 @@ def tile_routed_moe_kernel(tc, xT, w_words, w_scales, b, gate, offs, out):
         def scalar_gather(grouped, e0, e1, j):
             nc.scalar.activation(grouped[:, :, j], rounded[j][:].indirect(listed(e0, e1)), COPY)
 
-        first = keep.tile([P, C, PACK], BF16, name="first", tag="first", align_bytes=64)
-        second = keep.tile([P, 3 * C, PACK], BF16, name="second", tag="second", align_bytes=64)
+        def new_grouped(e0, e1, tag):
+            return keep.tile([P, (e1 - e0) * C, PACK], BF16, name=f"grouped{e0}", tag=tag, align_bytes=64)
+
+        def new_window(n, tag):
+            return keep.tile([P, T], F32, name=f"window{n}", tag=tag, align_bytes=64)
+
+        grouped0 = new_grouped(0, 1, "grouped0")
+        grouped1 = new_grouped(1, 2, "grouped1")
+        grouped2 = new_grouped(2, 4, "grouped2")
         rounded = {}
         for j in range(PACK - 1):
             rounded[j] = keep.tile([P, T], BF16, name=f"rounded{j}")
             nc.vector.tensor_copy(rounded[j][:], raws[j][:])
-            vector_gather(first[:], 0, 1, j)
-            scalar_gather(second[:], 1, 4, j)
-        vector_gather(first[:], 0, 1, 3)
-        multiply(0, 1, first[:], "codes0", range(BLOCKS))
-        rounded[3] = keep.tile([P, T], BF16, name="rounded3", tag="first", align_bytes=64)
+            vector_gather(grouped0, 0, 1, j)
+            scalar_gather(grouped1, 1, 2, j)
+            scalar_gather(grouped2, 2, 4, j)
+        vector_gather(grouped0, 0, 1, 3)
+        multiply(0, 1, grouped0)
+        rounded[3] = keep.tile([P, T], BF16, name="rounded3", tag="grouped0", align_bytes=64)
         nc.vector.tensor_copy(rounded[3][:], raws[3][:])
-        windows = [keep.tile([P, T], F32, name=f"window{n}") for n in range(3)]
-        for n in range(3):
-            finish(windows[n], n, 0, 1, new_y(n, 0, 1, f"x{n}"))
-        y3 = new_y(3, 0, 1, "x3")
-        nc.scalar.activation(y3, banks[3][0][:, 0, :], GELU, bias=bias[:, 3, 0:1])
-        scalar_gather(second[:], 1, 4, 3)
-        multiply(1, 4, second[:], "third", range(BLOCKS))
-        windows.append(keep.tile([P, T], F32, name="window3", tag="second", align_bytes=64))
-        nc.vector.tensor_tensor(windows[3][:].indirect(listed(0, 1)), y3, gates[:, 0:C], MULT)
-        for n in range(3):
-            finish(windows[n], n, 1, 4, new_y(n, 1, 4, f"y{n}"))
-        third = keep.tile([P, 4 * C, PACK], BF16, name="third", tag="third", align_bytes=64)
-        for j in range(PACK):
-            scalar_gather(third[:], 4, 8, j)
-        multiply(4, 8, third[:], "codes4", range(BLOCKS))
-        y_late = keep.tile([P, 3 * C], F32, name="y_late", tag="first", align_bytes=64)
-        finish(windows[3], 3, 1, 4, y_late[:])
+        windows = [new_window(n, f"window{n}") for n in range(2)]
+        for n in range(2):
+            finish(windows[n], n, 0, 1, new_y(n, 0, 1, f"y0{n}"))
+        scalar_gather(grouped1, 1, 2, 3)
+        late = [new_y(n, 0, 1, f"y0{n}") for n in (2, 3)]
+        for n in (2, 3):
+            nc.scalar.activation(late[n - 2], banks[n][0][:, 0, :], GELU, bias=bias[:, n, 0:1])
+        multiply(1, 2, grouped1)
+        scalar_gather(grouped2, 2, 4, 3)
+        windows += [new_window(2, "grouped1"), new_window(3, "codes1")]
+        for n in (2, 3):
+            nc.vector.tensor_tensor(windows[n][:].indirect(listed(0, 1)), late[n - 2], gates[:, 0:C], MULT)
         for n in range(BLOCKS):
-            finish(windows[n], n, 4, 8, new_y(n, 4, 8, f"z{n}"))
+            finish(windows[n], n, 1, 2, new_y(n, 1, 2, f"y1{n}"))
+        multiply(2, 4, grouped2)
+        grouped4 = new_grouped(4, 6, "scales1")
+        for j in range(PACK):
+            scalar_gather(grouped4, 4, 6, j)
+        multiply(4, 6, grouped4)
+        for n in range(3):
+            finish(windows[n], n, 2, 4, new_y(n, 2, 4, f"y2{n}"))
+        grouped6 = new_grouped(6, 8, "codes2")
+        for j in range(PACK):
+            scalar_gather(grouped6, 6, 8, j)
+        multiply(6, 8, grouped6)
+        y_late = keep.tile([P, 2 * C], F32, name="y_late", tag="grouped0", align_bytes=64)
+        finish(windows[3], 3, 2, 4, y_late[:])
+        for n in range(BLOCKS):
+            finish(windows[n], n, 4, 8, new_y(n, 4, 8, f"y4{n}"))
             nc.sync.dma_start(out[n * P : (n + 1) * P, :], windows[n][:])

@@ -22,6 +22,8 @@ COPY = mybir.ActivationFunctionType.Copy
 FLOPS = 2 * K * N * SLOTS
 BYTES = 4 * K * T + E * K * N + E * (K // 32) * N + 4 * N * E + 4 * SLOTS + 2 * 128 * SLOTS // 16 + 4 * N * T
 
+LOAD_ORDER = (2, 0, 1, 3)
+
 
 def tile_routed_moe_kernel(tc, xT, w_words, w_scales, b, gate, offs, out):
     nc = tc.nc
@@ -51,43 +53,40 @@ def tile_routed_moe_kernel(tc, xT, w_words, w_scales, b, gate, offs, out):
                     w_scales[4 * h : 4 * h + 4, 0, 4 * q : 4 * q + 4, :].bitcast(I32),
                 )
 
-        def load_words(e0, e1):
-            nc.sync.dma_start(words[:, e0:e1, :].bitcast(I32), w_rows[:, e0:e1, :])
-
-        def load_gates(e0, e1):
-            nc.sync.dma_start(gates[:, e0 * C : e1 * C], gate[0:P, e0 * C : e1 * C])
+        def load_words(e0, e1, n0, n1):
+            nc.sync.dma_start(words[:, e0:e1, n0 * P : n1 * P].bitcast(I32), w_rows[:, e0:e1, n0 * P : n1 * P])
 
         nc.sync.dma_start(offsets[:], offs)
         raws = [keep.tile([P, T], F32, name=f"raw{j}") for j in range(PACK)]
-        for j in range(PACK):
+        for j in LOAD_ORDER:
             nc.sync.dma_start(raws[j][:], x_rows[:, j, :])
         load_scales(0)
-        load_words(0, 1)
         nc.sync.dma_start(bias[:], b.rearrange("(c p) e -> p c e", p=P))
-        load_gates(0, 1)
-        load_words(1, 2)
-        load_gates(1, 4)
-        load_words(2, 4)
+        words_first = keep.tile([P, 2 * P], U32, name="words_first", tag="early", align_bytes=64)
+        nc.sync.dma_start(words_first[:].bitcast(I32), w_rows[:, 0, 0 : 2 * P])
+        load_words(0, 4, 2, 4)
+        nc.sync.dma_start(gates[:, 0 : 2 * C], gate[0:P, 0 : 2 * C])
+        nc.sync.dma_start(gates[:, 2 * C : SLOTS], gate[0:P, 2 * C : SLOTS])
+        load_words(1, 4, 0, 2)
         load_scales(1)
-        load_words(4, 8)
-        load_gates(4, 8)
+        load_words(4, 8, 0, 4)
 
         banks = [[psum.tile([P, PACK, C], F32, name=f"bank{n}{h}") for h in range(2)] for n in range(BLOCKS)]
 
         def listed(e0, e1):
             return offsets[:, e0 * C // 16 : e1 * C // 16]
 
-        def multiply(e0, e1, grouped):
+        def multiply(e0, e1, grouped, blocks, scales_tag):
             codes = keep.tile([P, (e1 - e0) * C], U32, name=f"codes{e0}", tag=f"codes{e0}", align_bytes=64)
-            scales = keep.tile([P, (e1 - e0) * C], U8, name=f"scales{e0}", tag=f"scales{e0}", align_bytes=64)
-            nc.vector.quantize_mx(out=codes[:].bitcast(FP8X4), scales=scales[:], in_=grouped[:].rearrange("p s j -> p (s j)"))
-            for n in range(BLOCKS):
+            scales = keep.tile([P, (e1 - e0) * C], U8, name=f"scales{e0}", tag=scales_tag, align_bytes=64)
+            nc.vector.quantize_mx(out=codes[:].bitcast(FP8X4), scales=scales[:], in_=grouped.rearrange("p s j -> p (s j)"))
+            for n in blocks:
                 feats = slice(n * P, (n + 1) * P)
                 for e in range(e0, e1):
                     slots = slice((e - e0) * C, (e - e0 + 1) * C)
                     nc.tensor.matmul_mx(
                         out=banks[n][e // 4][:, e % 4, :],
-                        lhsT=words[:, e, feats].bitcast(FP8X4),
+                        lhsT=(words_first[:, feats] if e == 0 and n < 2 else words[:, e, feats]).bitcast(FP8X4),
                         lhsT_scale=planes[e // 4][4 * (e % 4) : P, feats],
                         rhs=codes[:, slots].bitcast(FP8X4),
                         rhs_scale=scales[:, slots],
@@ -95,13 +94,19 @@ def tile_routed_moe_kernel(tc, xT, w_words, w_scales, b, gate, offs, out):
                         stop=True,
                     )
 
-        def finish(window, n, e0, e1, y):
+        def activate(y, n, e0, e1):
             for e in range(e0, e1):
                 nc.scalar.activation(y[:, (e - e0) * C : (e - e0 + 1) * C], banks[n][e // 4][:, e % 4, :], GELU, bias=bias[:, n, e : e + 1])
+
+        def scatter(window, e0, e1, y):
             nc.vector.tensor_tensor(window[:].indirect(listed(e0, e1)), y, gates[:, e0 * C : e1 * C], MULT)
 
+        def finish(window, n, e0, e1, y):
+            activate(y, n, e0, e1)
+            scatter(window, e0, e1, y)
+
         def new_y(n, e0, e1, tag):
-            return keep.tile([P, (e1 - e0) * C], F32, name=f"y{n}{e0}", tag=tag)[:]
+            return keep.tile([P, (e1 - e0) * C], F32, name=f"y{n}{e0}", tag=tag, align_bytes=64)[:]
 
         def vector_gather(grouped, e0, e1, j):
             nc.vector.tensor_copy(grouped[:, :, j], raws[j][:].indirect(listed(e0, e1)))
@@ -115,47 +120,42 @@ def tile_routed_moe_kernel(tc, xT, w_words, w_scales, b, gate, offs, out):
         def new_window(n, tag):
             return keep.tile([P, T], F32, name=f"window{n}", tag=tag, align_bytes=64)
 
-        grouped0 = new_grouped(0, 1, "grouped0")
-        grouped1 = new_grouped(1, 2, "grouped1")
-        grouped2 = new_grouped(2, 4, "grouped2")
-        rounded = {}
-        for j in range(PACK - 1):
-            rounded[j] = keep.tile([P, T], BF16, name=f"rounded{j}")
+        first = new_grouped(0, 2, "first")
+        second = new_grouped(2, 4, "second")
+        rounded = {j: keep.tile([P, T], BF16, name=f"rounded{j}") for j in range(3)}
+        vector_gather(first, 0, 2, 2)
+        nc.scalar.copy(rounded[2][:], raws[2][:])
+        scalar_gather(second, 2, 4, 2)
+        for j in range(2):
             nc.vector.tensor_copy(rounded[j][:], raws[j][:])
-            vector_gather(grouped0, 0, 1, j)
-            scalar_gather(grouped1, 1, 2, j)
-            scalar_gather(grouped2, 2, 4, j)
-        vector_gather(grouped0, 0, 1, 3)
-        multiply(0, 1, grouped0)
-        rounded[3] = keep.tile([P, T], BF16, name="rounded3", tag="grouped0", align_bytes=64)
-        nc.vector.tensor_copy(rounded[3][:], raws[3][:])
-        windows = [new_window(n, f"window{n}") for n in range(2)]
+            vector_gather(first[:, 0:C], 0, 1, j)
+            scalar_gather(first[:, C : 2 * C], 1, 2, j)
+            scalar_gather(second, 2, 4, j)
+        for e in range(2):
+            vector_gather(first[:, e * C : (e + 1) * C], e, e + 1, 3)
+        multiply(0, 1, first[:, 0:C], range(BLOCKS), "scales0")
+        windows = {n: new_window(n, f"window{n}") for n in (0, 1, 3)}
         for n in range(2):
-            finish(windows[n], n, 0, 1, new_y(n, 0, 1, f"y0{n}"))
-        scalar_gather(grouped1, 1, 2, 3)
-        late = [new_y(n, 0, 1, f"y0{n}") for n in (2, 3)]
-        for n in (2, 3):
-            nc.scalar.activation(late[n - 2], banks[n][0][:, 0, :], GELU, bias=bias[:, n, 0:1])
-        multiply(1, 2, grouped1)
-        scalar_gather(grouped2, 2, 4, 3)
-        windows += [new_window(2, "grouped1"), new_window(3, "codes1")]
-        for n in (2, 3):
-            nc.vector.tensor_tensor(windows[n][:].indirect(listed(0, 1)), late[n - 2], gates[:, 0:C], MULT)
-        for n in range(BLOCKS):
-            finish(windows[n], n, 1, 2, new_y(n, 1, 2, f"y1{n}"))
-        multiply(2, 4, grouped2)
-        grouped4 = new_grouped(4, 6, "scales1")
+            finish(windows[n], n, 0, 1, new_y(n, 0, 1, f"y{n}0"))
+        multiply(1, 2, first[:, C : 2 * C], (2, 3, 0, 1), "scales1")
+        rounded[3] = keep.tile([P, T], BF16, name="rounded3", tag="early", align_bytes=64)
+        nc.vector.tensor_copy(rounded[3][:], raws[3][:])
+        scalar_gather(second, 2, 4, 3)
+        held = keep.tile([P, 12 * C], F32, name="held", tag="y00", align_bytes=64)
+        y2 = held[:, 0 : 2 * C]
+        activate(y2, 2, 0, 2)
+        multiply(2, 4, second[:], (3, 0, 1, 2), "scales2")
+        windows[2] = new_window(2, "window2")
+        scatter(windows[2], 0, 2, y2)
+        finish(windows[3], 3, 0, 4, held[:, 2 * C : 6 * C])
+        finish(windows[0], 0, 1, 4, held[:, 6 * C : 9 * C])
+        finish(windows[1], 1, 1, 4, held[:, 9 * C : 12 * C])
+        third = new_grouped(4, 8, "codes2")
         for j in range(PACK):
-            scalar_gather(grouped4, 4, 6, j)
-        multiply(4, 6, grouped4)
-        for n in range(3):
-            finish(windows[n], n, 2, 4, new_y(n, 2, 4, f"y2{n}"))
-        grouped6 = new_grouped(6, 8, "codes2")
-        for j in range(PACK):
-            scalar_gather(grouped6, 6, 8, j)
-        multiply(6, 8, grouped6)
-        y_late = keep.tile([P, 2 * C], F32, name="y_late", tag="grouped0", align_bytes=64)
-        finish(windows[3], 3, 2, 4, y_late[:])
+            scalar_gather(third, 4, 8, j)
+        multiply(4, 8, third[:], range(BLOCKS), "scales4")
+        y_late = keep.tile([P, 2 * C], F32, name="y_late", tag="early", align_bytes=64)
+        finish(windows[2], 2, 2, 4, y_late[:])
         for n in range(BLOCKS):
-            finish(windows[n], n, 4, 8, new_y(n, 4, 8, f"y4{n}"))
+            finish(windows[n], n, 4, 8, new_y(n, 4, 8, f"y{n}4"))
             nc.sync.dma_start(out[n * P : (n + 1) * P, :], windows[n][:])

@@ -64,8 +64,8 @@ def tile_routed_moe_kernel(tc, xT, w_words, w_scales, b, gate, offs, out):
         nc.sync.dma_start(bias[:], b.rearrange("(c p) e -> p c e", p=P))
         words_first = keep.tile([P, 2 * P], U32, name="words_first", tag="early", align_bytes=64)
         nc.sync.dma_start(words_first[:].bitcast(I32), w_rows[:, 0, 0 : 2 * P])
-        load_words(0, 4, 2, 4)
         nc.sync.dma_start(gates[:, 0 : 2 * C], gate[0:P, 0 : 2 * C])
+        load_words(0, 4, 2, 4)
         nc.sync.dma_start(gates[:, 2 * C : SLOTS], gate[0:P, 2 * C : SLOTS])
         load_words(1, 4, 0, 2)
         load_scales(1)
@@ -139,7 +139,8 @@ def tile_routed_moe_kernel(tc, xT, w_words, w_scales, b, gate, offs, out):
             finish(windows[n], n, 0, 1, new_y(n, 0, 1, f"y{n}0"))
         multiply(1, 2, first[:, C : 2 * C], (2, 3, 0, 1), "scales1")
         rounded[3] = keep.tile([P, T], BF16, name="rounded3", tag="early", align_bytes=64)
-        nc.vector.tensor_copy(rounded[3][:], raws[3][:])
+        nc.vector.tensor_copy(rounded[3][:, 0 : T // 2], raws[3][:, 0 : T // 2])
+        nc.scalar.copy(rounded[3][:, T // 2 : T], raws[3][:, T // 2 : T])
         scalar_gather(second, 2, 4, 3)
         held = keep.tile([P, 12 * C], F32, name="held", tag="y00", align_bytes=64)
         y2 = held[:, 0 : 2 * C]

@@ -7,6 +7,7 @@ P = 128
 PACK = 4
 SLOTS = E * C
 BLOCKS = N // P
+PER_BANK = 4
 
 F32 = mybir.dt.float32
 BF16 = mybir.dt.bfloat16
@@ -23,6 +24,7 @@ FLOPS = 2 * K * N * SLOTS
 BYTES = 4 * K * T + E * K * N + E * (K // 32) * N + 4 * N * E + 4 * SLOTS + 2 * 128 * SLOTS // 16 + 4 * N * T
 
 LOAD_ORDER = (2, 0, 1, 3)
+LAST_PLANE = LOAD_ORDER[-1]
 
 
 def tile_routed_moe_kernel(tc, xT, w_words, w_scales, b, gate, offs, out):
@@ -35,10 +37,10 @@ def tile_routed_moe_kernel(tc, xT, w_words, w_scales, b, gate, offs, out):
         bias = keep.tile([P, BLOCKS, E], F32, name="bias")
         gates = keep.tile([P, SLOTS], F32, name="gates")
         warm = keep.tile([P, 1], F32, name="warm")
-        planes = [keep.tile([P, N], U8, name=f"planes{h}", align_bytes=64) for h in range(2)]
+        w_scale_rows = [keep.tile([P, N], U8, name=f"w_scale_rows{h}", align_bytes=64) for h in range(E // PER_BANK)]
 
-        for h in range(2):
-            nc.gpsimd.memset(planes[h][:].bitcast(I32), 0)
+        for tile in w_scale_rows:
+            nc.gpsimd.memset(tile[:].bitcast(I32), 0)
         nc.vector.memset(warm[:], 0.0)
         nc.scalar.activation(warm[:], warm[:], GELU)
 
@@ -47,47 +49,56 @@ def tile_routed_moe_kernel(tc, xT, w_words, w_scales, b, gate, offs, out):
         words = keep.tile([P, E, N], U32, name="words", align_bytes=64)
 
         def load_scales(h):
-            for q in range(4):
+            for quad in range(4):
                 nc.sync.dma_start(
-                    planes[h][32 * q : 32 * q + 16, :].bitcast(I32),
-                    w_scales[4 * h : 4 * h + 4, 0, 4 * q : 4 * q + 4, :].bitcast(I32),
+                    w_scale_rows[h][32 * quad : 32 * quad + 16, :].bitcast(I32),
+                    w_scales[PER_BANK * h : PER_BANK * (h + 1), 0, 4 * quad : 4 * quad + 4, :].bitcast(I32),
                 )
 
         def load_words(e0, e1, n0, n1):
             nc.sync.dma_start(words[:, e0:e1, n0 * P : n1 * P].bitcast(I32), w_rows[:, e0:e1, n0 * P : n1 * P])
 
         nc.sync.dma_start(offsets[:], offs)
-        raws = [keep.tile([P, T], F32, name=f"raw{j}") for j in range(PACK)]
+        planes = [keep.tile([P, T], F32, name=f"plane{j}") for j in range(PACK)]
         for j in LOAD_ORDER:
-            nc.sync.dma_start(raws[j][:], x_rows[:, j, :])
+            nc.sync.dma_start(planes[j][:], x_rows[:, j, :])
         load_scales(0)
         nc.sync.dma_start(bias[:], b.rearrange("(c p) e -> p c e", p=P))
-        words_first = keep.tile([P, 2 * P], U32, name="words_first", tag="early", align_bytes=64)
+        words_first = keep.tile([P, 2 * P], U32, name="words_first", tag="words_first", align_bytes=64)
         nc.sync.dma_start(words_first[:].bitcast(I32), w_rows[:, 0, 0 : 2 * P])
         nc.sync.dma_start(gates[:, 0 : 2 * C], gate[0:P, 0 : 2 * C])
         load_words(0, 4, 2, 4)
-        nc.sync.dma_start(gates[:, 2 * C : SLOTS], gate[0:P, 2 * C : SLOTS])
         load_words(1, 4, 0, 2)
+        nc.sync.dma_start(gates[:, 2 * C : SLOTS], gate[0:P, 2 * C : SLOTS])
         load_scales(1)
         load_words(4, 8, 0, 4)
 
-        banks = [[psum.tile([P, PACK, C], F32, name=f"bank{n}{h}") for h in range(2)] for n in range(BLOCKS)]
+        banks = [[psum.tile([P, PER_BANK, C], F32, name=f"bank{n}{h}") for h in range(E // PER_BANK)] for n in range(BLOCKS)]
 
         def listed(e0, e1):
             return offsets[:, e0 * C // 16 : e1 * C // 16]
 
-        def multiply(e0, e1, grouped, blocks, scales_tag):
+        def sums(n, e):
+            return banks[n][e // PER_BANK][:, e % PER_BANK, :]
+
+        def vector_gather(grouped, e0, e1, j):
+            nc.vector.tensor_copy(grouped[:, :, j], planes[j][:].indirect(listed(e0, e1)))
+
+        def scalar_gather(grouped, e0, e1, j):
+            nc.scalar.activation(grouped[:, :, j], rounded[j][:].indirect(listed(e0, e1)), COPY)
+
+        def multiply(e0, e1, grouped, blocks):
             codes = keep.tile([P, (e1 - e0) * C], U32, name=f"codes{e0}", tag=f"codes{e0}", align_bytes=64)
-            scales = keep.tile([P, (e1 - e0) * C], U8, name=f"scales{e0}", tag=scales_tag, align_bytes=64)
+            scales = keep.tile([P, (e1 - e0) * C], U8, name=f"scales{e0}", align_bytes=64)
             nc.vector.quantize_mx(out=codes[:].bitcast(FP8X4), scales=scales[:], in_=grouped.rearrange("p s j -> p (s j)"))
             for n in blocks:
                 feats = slice(n * P, (n + 1) * P)
                 for e in range(e0, e1):
                     slots = slice((e - e0) * C, (e - e0 + 1) * C)
                     nc.tensor.matmul_mx(
-                        out=banks[n][e // 4][:, e % 4, :],
+                        out=sums(n, e),
                         lhsT=(words_first[:, feats] if e == 0 and n < 2 else words[:, e, feats]).bitcast(FP8X4),
-                        lhsT_scale=planes[e // 4][4 * (e % 4) : P, feats],
+                        lhsT_scale=w_scale_rows[e // PER_BANK][4 * (e % PER_BANK) : P, feats],
                         rhs=codes[:, slots].bitcast(FP8X4),
                         rhs_scale=scales[:, slots],
                         start=True,
@@ -96,67 +107,68 @@ def tile_routed_moe_kernel(tc, xT, w_words, w_scales, b, gate, offs, out):
 
         def activate(y, n, e0, e1):
             for e in range(e0, e1):
-                nc.scalar.activation(y[:, (e - e0) * C : (e - e0 + 1) * C], banks[n][e // 4][:, e % 4, :], GELU, bias=bias[:, n, e : e + 1])
+                nc.scalar.activation(y[:, (e - e0) * C : (e - e0 + 1) * C], sums(n, e), GELU, bias=bias[:, n, e : e + 1])
 
-        def scatter(window, e0, e1, y):
-            nc.vector.tensor_tensor(window[:].indirect(listed(e0, e1)), y, gates[:, e0 * C : e1 * C], MULT)
+        def scatter(y, n, e0, e1):
+            nc.vector.tensor_tensor(windows[n][:].indirect(listed(e0, e1)), y, gates[:, e0 * C : e1 * C], MULT)
 
-        def finish(window, n, e0, e1, y):
+        def finish(y, n, e0, e1):
             activate(y, n, e0, e1)
-            scatter(window, e0, e1, y)
-
-        def new_y(n, e0, e1, tag):
-            return keep.tile([P, (e1 - e0) * C], F32, name=f"y{n}{e0}", tag=tag, align_bytes=64)[:]
-
-        def vector_gather(grouped, e0, e1, j):
-            nc.vector.tensor_copy(grouped[:, :, j], raws[j][:].indirect(listed(e0, e1)))
-
-        def scalar_gather(grouped, e0, e1, j):
-            nc.scalar.activation(grouped[:, :, j], rounded[j][:].indirect(listed(e0, e1)), COPY)
+            scatter(y, n, e0, e1)
 
         def new_grouped(e0, e1, tag):
             return keep.tile([P, (e1 - e0) * C, PACK], BF16, name=f"grouped{e0}", tag=tag, align_bytes=64)
 
-        def new_window(n, tag):
-            return keep.tile([P, T], F32, name=f"window{n}", tag=tag, align_bytes=64)
+        def new_y(name, experts, tag):
+            return keep.tile([P, experts * C], F32, name=name, tag=tag, align_bytes=64)[:]
 
-        first = new_grouped(0, 2, "first")
-        second = new_grouped(2, 4, "second")
-        rounded = {j: keep.tile([P, T], BF16, name=f"rounded{j}") for j in range(3)}
-        vector_gather(first, 0, 2, 2)
-        nc.scalar.copy(rounded[2][:], raws[2][:])
-        scalar_gather(second, 2, 4, 2)
-        for j in range(2):
-            nc.vector.tensor_copy(rounded[j][:], raws[j][:])
-            vector_gather(first[:, 0:C], 0, 1, j)
-            scalar_gather(first[:, C : 2 * C], 1, 2, j)
-            scalar_gather(second, 2, 4, j)
-        for e in range(2):
-            vector_gather(first[:, e * C : (e + 1) * C], e, e + 1, 3)
-        multiply(0, 1, first[:, 0:C], range(BLOCKS), "scales0")
-        windows = {n: new_window(n, f"window{n}") for n in (0, 1, 3)}
-        for n in range(2):
-            finish(windows[n], n, 0, 1, new_y(n, 0, 1, f"y{n}0"))
-        multiply(1, 2, first[:, C : 2 * C], (2, 3, 0, 1), "scales1")
-        rounded[3] = keep.tile([P, T], BF16, name="rounded3", tag="early", align_bytes=64)
-        nc.vector.tensor_copy(rounded[3][:, 0 : T // 2], raws[3][:, 0 : T // 2])
-        nc.scalar.copy(rounded[3][:, T // 2 : T], raws[3][:, T // 2 : T])
-        scalar_gather(second, 2, 4, 3)
-        held = keep.tile([P, 12 * C], F32, name="held", tag="y00", align_bytes=64)
-        y2 = held[:, 0 : 2 * C]
-        activate(y2, 2, 0, 2)
-        multiply(2, 4, second[:], (3, 0, 1, 2), "scales2")
-        windows[2] = new_window(2, "window2")
-        scatter(windows[2], 0, 2, y2)
-        finish(windows[3], 3, 0, 4, held[:, 2 * C : 6 * C])
-        finish(windows[0], 0, 1, 4, held[:, 6 * C : 9 * C])
-        finish(windows[1], 1, 1, 4, held[:, 9 * C : 12 * C])
-        third = new_grouped(4, 8, "codes2")
+        grouped01 = new_grouped(0, 2, "grouped01")
+        grouped23 = new_grouped(2, 4, "grouped23")
+        grouped0, grouped1 = grouped01[:, 0:C], grouped01[:, C : 2 * C]
+        rounded = {j: keep.tile([P, T], BF16, name=f"rounded{j}") for j in range(PACK) if j != LAST_PLANE}
+        vector_gather(grouped01, 0, 2, 2)
+        nc.scalar.copy(rounded[2][:], planes[2][:])
+        scalar_gather(grouped23, 2, 4, 2)
+        for j in (0, 1):
+            nc.vector.tensor_copy(rounded[j][:], planes[j][:])
+            vector_gather(grouped0, 0, 1, j)
+            scalar_gather(grouped1, 1, 2, j)
+            scalar_gather(grouped23, 2, 4, j)
+
+        vector_gather(grouped0, 0, 1, LAST_PLANE)
+        vector_gather(grouped1, 1, 2, LAST_PLANE)
+        multiply(0, 1, grouped0, range(BLOCKS))
+        windows = [keep.tile([P, T], F32, name=f"window{n}") for n in range(BLOCKS)]
+        for n in (0, 1):
+            finish(new_y(f"y_first{n}", 1, f"y_first{n}"), n, 0, 1)
+        multiply(1, 2, grouped1, (2, 3, 0, 1))
+
+        rounded[LAST_PLANE] = keep.tile([P, T], BF16, name="rounded_last", tag="words_first", align_bytes=64)
+        nc.vector.tensor_copy(rounded[LAST_PLANE][:, 0 : T // 2], planes[LAST_PLANE][:, 0 : T // 2])
+        nc.scalar.copy(rounded[LAST_PLANE][:, T // 2 : T], planes[LAST_PLANE][:, T // 2 : T])
+        scalar_gather(grouped23, 2, 4, LAST_PLANE)
+
+        middle = ((2, 0, 2), (3, 0, 2), (0, 1, 4), (2, 2, 4), (3, 2, 4))
+        y_middle = new_y("y_middle", sum(e1 - e0 for n, e0, e1 in middle), "y_first0")
+        parts, start = [], 0
+        for n, e0, e1 in middle:
+            parts.append((y_middle[:, start : start + (e1 - e0) * C], n, e0, e1))
+            start += (e1 - e0) * C
+        for part in parts[:2]:
+            activate(*part)
+        multiply(2, 4, grouped23[:], (0, 2, 3, 1))
+        for part in parts[:2]:
+            scatter(*part)
+        for part in parts[2:]:
+            finish(*part)
+
+        grouped47 = new_grouped(4, 8, "codes2")
         for j in range(PACK):
-            scalar_gather(third, 4, 8, j)
-        multiply(4, 8, third[:], range(BLOCKS), "scales4")
-        y_late = keep.tile([P, 2 * C], F32, name="y_late", tag="early", align_bytes=64)
-        finish(windows[2], 2, 2, 4, y_late[:])
+            scalar_gather(grouped47, 4, 8, j)
+        multiply(4, 8, grouped47[:], range(BLOCKS))
+
+        finish(new_y("y_kept", 3, "words_first"), 1, 1, 4)
+
         for n in range(BLOCKS):
-            finish(windows[n], n, 4, 8, new_y(n, 4, 8, f"y{n}4"))
+            finish(new_y(f"y_last{n}", 4, f"y_last{n}"), n, 4, 8)
             nc.sync.dma_start(out[n * P : (n + 1) * P, :], windows[n][:])

@@ -59,17 +59,19 @@ def tile_routed_moe_kernel(tc, xT, w_words, w_scales, b, gate, offs, out):
             nc.sync.dma_start(words[:, e0:e1, n0 * P : n1 * P].bitcast(I32), w_rows[:, e0:e1, n0 * P : n1 * P])
 
         nc.sync.dma_start(offsets[:], offs)
-        planes = [keep.tile([P, T], F32, name=f"plane{j}") for j in range(PACK)]
+        last_and_first = keep.tile([P, T + C], F32, name="last_and_first", align_bytes=64)
+        planes = {j: keep.tile([P, T], F32, name=f"plane{j}") for j in LOAD_ORDER[:-1]}
+        planes[LAST_PLANE] = last_and_first[:, 0:T]
         for j in LOAD_ORDER:
             nc.sync.dma_start(planes[j][:], x_rows[:, j, :])
         load_scales(0)
         nc.sync.dma_start(bias[:], b.rearrange("(c p) e -> p c e", p=P))
         words_first = keep.tile([P, 2 * P], U32, name="words_first", tag="words_first", align_bytes=64)
         nc.sync.dma_start(words_first[:].bitcast(I32), w_rows[:, 0, 0 : 2 * P])
-        nc.sync.dma_start(gates[:, 0 : 2 * C], gate[0:P, 0 : 2 * C])
+        nc.sync.dma_start(gates[:, 0:C], gate[0:P, 0:C])
         load_words(0, 4, 2, 4)
         load_words(1, 4, 0, 2)
-        nc.sync.dma_start(gates[:, 2 * C : SLOTS], gate[0:P, 2 * C : SLOTS])
+        nc.sync.dma_start(gates[:, C:SLOTS], gate[0:P, C:SLOTS])
         load_scales(1)
         load_words(4, 8, 0, 4)
 
@@ -81,16 +83,24 @@ def tile_routed_moe_kernel(tc, xT, w_words, w_scales, b, gate, offs, out):
         def sums(n, e):
             return banks[n][e // PER_BANK][:, e % PER_BANK, :]
 
-        def vector_gather(grouped, e0, e1, j):
-            nc.vector.tensor_copy(grouped[:, :, j], planes[j][:].indirect(listed(e0, e1)))
+        def vector_gather(grouped, e0, e1, j, window=None):
+            window = planes[j] if window is None else window
+            nc.vector.tensor_copy(grouped[:, :, j], window[:].indirect(listed(e0, e1)))
 
         def scalar_gather(grouped, e0, e1, j):
             nc.scalar.activation(grouped[:, :, j], rounded[j][:].indirect(listed(e0, e1)), COPY)
 
-        def multiply(e0, e1, grouped, blocks):
+        def quantise(e0, e1, grouped):
             codes = keep.tile([P, (e1 - e0) * C], U32, name=f"codes{e0}", tag=f"codes{e0}", align_bytes=64)
             scales = keep.tile([P, (e1 - e0) * C], U8, name=f"scales{e0}", align_bytes=64)
             nc.vector.quantize_mx(out=codes[:].bitcast(FP8X4), scales=scales[:], in_=grouped.rearrange("p s j -> p (s j)"))
+            return codes, scales
+
+        def multiply(e0, e1, grouped, blocks):
+            matmuls(e0, e1, quantise(e0, e1, grouped), blocks)
+
+        def matmuls(e0, e1, operand, blocks):
+            codes, scales = operand
             for n in blocks:
                 feats = slice(n * P, (n + 1) * P)
                 for e in range(e0, e1):
@@ -122,47 +132,41 @@ def tile_routed_moe_kernel(tc, xT, w_words, w_scales, b, gate, offs, out):
         def new_y(name, experts, tag):
             return keep.tile([P, experts * C], F32, name=name, tag=tag, align_bytes=64)[:]
 
-        grouped01 = new_grouped(0, 2, "grouped01")
-        grouped23 = new_grouped(2, 4, "grouped23")
-        grouped0, grouped1 = grouped01[:, 0:C], grouped01[:, C : 2 * C]
+        grouped0 = new_grouped(0, 1, "grouped0")[:]
+        grouped13 = new_grouped(1, 4, "grouped13")
+        grouped12, grouped3 = grouped13[:, 0 : 2 * C], grouped13[:, 2 * C : 3 * C]
         rounded = {j: keep.tile([P, T], BF16, name=f"rounded{j}") for j in range(PACK) if j != LAST_PLANE}
-        vector_gather(grouped01, 0, 2, 2)
+        vector_gather(grouped0, 0, 1, 2)
+        vector_gather(grouped12, 1, 3, 2)
         nc.scalar.copy(rounded[2][:], planes[2][:])
-        scalar_gather(grouped23, 2, 4, 2)
+        scalar_gather(grouped3, 3, 4, 2)
         for j in (0, 1):
             nc.vector.tensor_copy(rounded[j][:], planes[j][:])
             vector_gather(grouped0, 0, 1, j)
-            scalar_gather(grouped1, 1, 2, j)
-            scalar_gather(grouped23, 2, 4, j)
+            scalar_gather(grouped13, 1, 4, j)
 
         vector_gather(grouped0, 0, 1, LAST_PLANE)
-        vector_gather(grouped1, 1, 2, LAST_PLANE)
+        last3 = last_and_first[:, T : T + C]
+        nc.vector.tensor_copy(last3, planes[LAST_PLANE].indirect(listed(3, 4)))
+        nc.scalar.copy(grouped3[:, :, LAST_PLANE], last3)
         multiply(0, 1, grouped0, range(BLOCKS))
+        vector_gather(grouped12, 1, 3, LAST_PLANE, last_and_first[:, 0 : T + 8])
         windows = [keep.tile([P, T], F32, name=f"window{n}") for n in range(BLOCKS)]
-        for n in (0, 1):
-            finish(new_y(f"y_first{n}", 1, f"y_first{n}"), n, 0, 1)
-        multiply(1, 2, grouped1, (2, 3, 0, 1))
-
+        firsts = [new_y(f"y_first{n}", 1, f"y_first{n}") for n in range(BLOCKS)]
+        for n in range(BLOCKS):
+            activate(firsts[n], n, 0, 1)
         rounded[LAST_PLANE] = keep.tile([P, T], BF16, name="rounded_last", tag="words_first", align_bytes=64)
-        nc.vector.tensor_copy(rounded[LAST_PLANE][:, 0 : T // 2], planes[LAST_PLANE][:, 0 : T // 2])
-        nc.scalar.copy(rounded[LAST_PLANE][:, T // 2 : T], planes[LAST_PLANE][:, T // 2 : T])
-        scalar_gather(grouped23, 2, 4, LAST_PLANE)
+        nc.scalar.copy(rounded[LAST_PLANE][:], planes[LAST_PLANE])
+        quantised = [(1, 3, quantise(1, 3, grouped12)), (3, 4, quantise(3, 4, grouped3))]
+        for n in range(BLOCKS):
+            scatter(firsts[n], n, 0, 1)
+        for n in (2, 3, 0, 1):
+            for e0, e1, operand in quantised:
+                matmuls(e0, e1, operand, (n,))
+        for n in (2, 3, 0):
+            finish(new_y(f"y_middle{n}", 3, f"y_middle{n}"), n, 1, 4)
 
-        middle = ((2, 0, 2), (3, 0, 2), (0, 1, 4), (2, 2, 4), (3, 2, 4))
-        y_middle = new_y("y_middle", sum(e1 - e0 for n, e0, e1 in middle), "y_first0")
-        parts, start = [], 0
-        for n, e0, e1 in middle:
-            parts.append((y_middle[:, start : start + (e1 - e0) * C], n, e0, e1))
-            start += (e1 - e0) * C
-        for part in parts[:2]:
-            activate(*part)
-        multiply(2, 4, grouped23[:], (0, 2, 3, 1))
-        for part in parts[:2]:
-            scatter(*part)
-        for part in parts[2:]:
-            finish(*part)
-
-        grouped47 = new_grouped(4, 8, "codes2")
+        grouped47 = new_grouped(4, 8, "codes3")
         for j in range(PACK):
             scalar_gather(grouped47, 4, 8, j)
         multiply(4, 8, grouped47[:], range(BLOCKS))

@@ -66,11 +66,11 @@ def tile_routed_moe_kernel(tc, xT, w_words, w_scales, b, gate, offs, out):
             nc.sync.dma_start(planes[j][:], x_rows[:, j, :])
         load_scales(0)
         nc.sync.dma_start(bias[:], b.rearrange("(c p) e -> p c e", p=P))
-        words_first = keep.tile([P, 2 * P], U32, name="words_first", tag="words_first", align_bytes=64)
-        nc.sync.dma_start(words_first[:].bitcast(I32), w_rows[:, 0, 0 : 2 * P])
+        words_first = keep.tile([P, N], U32, name="words_first", tag="words_first", align_bytes=64)
+        nc.sync.dma_start(words_first[:].bitcast(I32), w_rows[:, 0, :])
         nc.sync.dma_start(gates[:, 0:C], gate[0:P, 0:C])
-        load_words(0, 4, 2, 4)
         load_words(1, 4, 0, 2)
+        load_words(1, 4, 2, 4)
         nc.sync.dma_start(gates[:, C:SLOTS], gate[0:P, C:SLOTS])
         load_scales(1)
         load_words(4, 8, 0, 4)
@@ -107,7 +107,7 @@ def tile_routed_moe_kernel(tc, xT, w_words, w_scales, b, gate, offs, out):
                     slots = slice((e - e0) * C, (e - e0 + 1) * C)
                     nc.tensor.matmul_mx(
                         out=sums(n, e),
-                        lhsT=(words_first[:, feats] if e == 0 and n < 2 else words[:, e, feats]).bitcast(FP8X4),
+                        lhsT=(words_first[:, feats] if e == 0 else words[:, e, feats]).bitcast(FP8X4),
                         lhsT_scale=w_scale_rows[e // PER_BANK][4 * (e % PER_BANK) : P, feats],
                         rhs=codes[:, slots].bitcast(FP8X4),
                         rhs_scale=scales[:, slots],
@@ -132,12 +132,11 @@ def tile_routed_moe_kernel(tc, xT, w_words, w_scales, b, gate, offs, out):
         def new_y(name, experts, tag):
             return keep.tile([P, experts * C], F32, name=name, tag=tag, align_bytes=64)[:]
 
-        grouped0 = new_grouped(0, 1, "grouped0")[:]
-        grouped13 = new_grouped(1, 4, "grouped13")
-        grouped12, grouped3 = grouped13[:, 0 : 2 * C], grouped13[:, 2 * C : 3 * C]
+        grouped03 = new_grouped(0, 4, "grouped03")
+        grouped0, grouped12, grouped3 = grouped03[:, 0:C], grouped03[:, C : 3 * C], grouped03[:, 3 * C : 4 * C]
+        grouped13 = grouped03[:, C : 4 * C]
         rounded = {j: keep.tile([P, T], BF16, name=f"rounded{j}") for j in range(PACK) if j != LAST_PLANE}
-        vector_gather(grouped0, 0, 1, 2)
-        vector_gather(grouped12, 1, 3, 2)
+        vector_gather(grouped03[:, 0 : 3 * C], 0, 3, 2)
         nc.scalar.copy(rounded[2][:], planes[2][:])
         scalar_gather(grouped3, 3, 4, 2)
         for j in (0, 1):
@@ -160,10 +159,10 @@ def tile_routed_moe_kernel(tc, xT, w_words, w_scales, b, gate, offs, out):
         quantised = [(1, 3, quantise(1, 3, grouped12)), (3, 4, quantise(3, 4, grouped3))]
         for n in range(BLOCKS):
             scatter(firsts[n], n, 0, 1)
-        for n in (2, 3, 0, 1):
+        for n in range(BLOCKS):
             for e0, e1, operand in quantised:
                 matmuls(e0, e1, operand, (n,))
-        for n in (2, 3, 0):
+        for n in range(BLOCKS - 1):
             finish(new_y(f"y_middle{n}", 3, f"y_middle{n}"), n, 1, 4)
 
         grouped47 = new_grouped(4, 8, "codes3")
@@ -171,7 +170,7 @@ def tile_routed_moe_kernel(tc, xT, w_words, w_scales, b, gate, offs, out):
             scalar_gather(grouped47, 4, 8, j)
         multiply(4, 8, grouped47[:], range(BLOCKS))
 
-        finish(new_y("y_kept", 3, "words_first"), 1, 1, 4)
+        finish(new_y("y_kept", 3, "words_first"), BLOCKS - 1, 1, 4)
 
         for n in range(BLOCKS):
             finish(new_y(f"y_last{n}", 4, f"y_last{n}"), n, 4, 8)

@@ -24,7 +24,8 @@ FLOPS = 2 * K * N * SLOTS
 BYTES = 4 * K * T + E * K * N + E * (K // 32) * N + 4 * N * E + 4 * SLOTS + 2 * 128 * SLOTS // 16 + 4 * N * T
 
 LOAD_ORDER = (2, 0, 1, 3)
-LAST_PLANE = LOAD_ORDER[-1]
+FIRST_PLANE, LAST_PLANE = LOAD_ORDER[0], LOAD_ORDER[-1]
+OVERHANG = 8
 
 
 def tile_routed_moe_kernel(tc, xT, w_words, w_scales, b, gate, offs, out):
@@ -58,12 +59,15 @@ def tile_routed_moe_kernel(tc, xT, w_words, w_scales, b, gate, offs, out):
         def load_words(e0, e1, n0, n1):
             nc.sync.dma_start(words[:, e0:e1, n0 * P : n1 * P].bitcast(I32), w_rows[:, e0:e1, n0 * P : n1 * P])
 
-        nc.sync.dma_start(offsets[:], offs)
-        last_and_first = keep.tile([P, T + C], F32, name="last_and_first", align_bytes=64)
+        last_tile = keep.tile([P, T + C], F32, name="last_tile", align_bytes=64)
+        last_of_3 = last_tile[:, T : T + C]
         planes = {j: keep.tile([P, T], F32, name=f"plane{j}") for j in LOAD_ORDER[:-1]}
-        planes[LAST_PLANE] = last_and_first[:, 0:T]
+        planes[LAST_PLANE] = last_tile[:, 0:T]
+
         for j in LOAD_ORDER:
             nc.sync.dma_start(planes[j][:], x_rows[:, j, :])
+            if j == FIRST_PLANE:
+                nc.sync.dma_start(offsets[:], offs)
         load_scales(0)
         nc.sync.dma_start(bias[:], b.rearrange("(c p) e -> p c e", p=P))
         words_first = keep.tile([P, N], U32, name="words_first", tag="words_first", align_bytes=64)
@@ -83,9 +87,8 @@ def tile_routed_moe_kernel(tc, xT, w_words, w_scales, b, gate, offs, out):
         def sums(n, e):
             return banks[n][e // PER_BANK][:, e % PER_BANK, :]
 
-        def vector_gather(grouped, e0, e1, j, window=None):
-            window = planes[j] if window is None else window
-            nc.vector.tensor_copy(grouped[:, :, j], window[:].indirect(listed(e0, e1)))
+        def vector_gather(grouped, e0, e1, j, source):
+            nc.vector.tensor_copy(grouped[:, :, j], source.indirect(listed(e0, e1)))
 
         def scalar_gather(grouped, e0, e1, j):
             nc.scalar.activation(grouped[:, :, j], rounded[j][:].indirect(listed(e0, e1)), COPY)
@@ -94,26 +97,23 @@ def tile_routed_moe_kernel(tc, xT, w_words, w_scales, b, gate, offs, out):
             codes = keep.tile([P, (e1 - e0) * C], U32, name=f"codes{e0}", tag=f"codes{e0}", align_bytes=64)
             scales = keep.tile([P, (e1 - e0) * C], U8, name=f"scales{e0}", align_bytes=64)
             nc.vector.quantize_mx(out=codes[:].bitcast(FP8X4), scales=scales[:], in_=grouped.rearrange("p s j -> p (s j)"))
-            return codes, scales
+            return e0, e1, codes, scales
 
-        def multiply(e0, e1, grouped, blocks):
-            matmuls(e0, e1, quantise(e0, e1, grouped), blocks)
-
-        def matmuls(e0, e1, operand, blocks):
-            codes, scales = operand
-            for n in blocks:
+        def multiply(groups):
+            for n in range(BLOCKS):
                 feats = slice(n * P, (n + 1) * P)
-                for e in range(e0, e1):
-                    slots = slice((e - e0) * C, (e - e0 + 1) * C)
-                    nc.tensor.matmul_mx(
-                        out=sums(n, e),
-                        lhsT=(words_first[:, feats] if e == 0 else words[:, e, feats]).bitcast(FP8X4),
-                        lhsT_scale=w_scale_rows[e // PER_BANK][4 * (e % PER_BANK) : P, feats],
-                        rhs=codes[:, slots].bitcast(FP8X4),
-                        rhs_scale=scales[:, slots],
-                        start=True,
-                        stop=True,
-                    )
+                for e0, e1, codes, scales in groups:
+                    for e in range(e0, e1):
+                        slots = slice((e - e0) * C, (e - e0 + 1) * C)
+                        nc.tensor.matmul_mx(
+                            out=sums(n, e),
+                            lhsT=(words_first[:, feats] if e == 0 else words[:, e, feats]).bitcast(FP8X4),
+                            lhsT_scale=w_scale_rows[e // PER_BANK][4 * (e % PER_BANK) : P, feats],
+                            rhs=codes[:, slots].bitcast(FP8X4),
+                            rhs_scale=scales[:, slots],
+                            start=True,
+                            stop=True,
+                        )
 
         def activate(y, n, e0, e1):
             for e in range(e0, e1):
@@ -134,41 +134,40 @@ def tile_routed_moe_kernel(tc, xT, w_words, w_scales, b, gate, offs, out):
 
         grouped03 = new_grouped(0, 4, "grouped03")
         grouped0, grouped12, grouped3 = grouped03[:, 0:C], grouped03[:, C : 3 * C], grouped03[:, 3 * C : 4 * C]
-        grouped13 = grouped03[:, C : 4 * C]
         rounded = {j: keep.tile([P, T], BF16, name=f"rounded{j}") for j in range(PACK) if j != LAST_PLANE}
-        vector_gather(grouped03[:, 0 : 3 * C], 0, 3, 2)
-        nc.scalar.copy(rounded[2][:], planes[2][:])
-        scalar_gather(grouped3, 3, 4, 2)
-        for j in (0, 1):
+        vector_gather(grouped03[:, 0 : 3 * C], 0, 3, FIRST_PLANE, planes[FIRST_PLANE][:])
+        nc.scalar.copy(rounded[FIRST_PLANE][:], planes[FIRST_PLANE][:])
+        scalar_gather(grouped3, 3, 4, FIRST_PLANE)
+        for j in LOAD_ORDER[1:-1]:
             nc.vector.tensor_copy(rounded[j][:], planes[j][:])
-            vector_gather(grouped0, 0, 1, j)
-            scalar_gather(grouped13, 1, 4, j)
+            vector_gather(grouped0, 0, 1, j, planes[j][:])
+            scalar_gather(grouped03[:, C : 4 * C], 1, 4, j)
 
-        vector_gather(grouped0, 0, 1, LAST_PLANE)
-        last3 = last_and_first[:, T : T + C]
-        nc.vector.tensor_copy(last3, planes[LAST_PLANE].indirect(listed(3, 4)))
-        nc.scalar.copy(grouped3[:, :, LAST_PLANE], last3)
-        multiply(0, 1, grouped0, range(BLOCKS))
-        vector_gather(grouped12, 1, 3, LAST_PLANE, last_and_first[:, 0 : T + 8])
+        vector_gather(grouped0, 0, 1, LAST_PLANE, planes[LAST_PLANE])
+        nc.vector.tensor_copy(last_of_3, planes[LAST_PLANE].indirect(listed(3, 4)))
+        nc.scalar.copy(grouped3[:, :, LAST_PLANE], last_of_3)
+        multiply([quantise(0, 1, grouped0)])
+
+        vector_gather(grouped12, 1, 3, LAST_PLANE, last_tile[:, 0 : T + OVERHANG])
         windows = [keep.tile([P, T], F32, name=f"window{n}") for n in range(BLOCKS)]
-        firsts = [new_y(f"y_first{n}", 1, f"y_first{n}") for n in range(BLOCKS)]
+        y_first = [new_y(f"y_first{n}", 1, f"y_first{n}") for n in range(BLOCKS)]
         for n in range(BLOCKS):
-            activate(firsts[n], n, 0, 1)
+            activate(y_first[n], n, 0, 1)
+
         rounded[LAST_PLANE] = keep.tile([P, T], BF16, name="rounded_last", tag="words_first", align_bytes=64)
         nc.scalar.copy(rounded[LAST_PLANE][:], planes[LAST_PLANE])
-        quantised = [(1, 3, quantise(1, 3, grouped12)), (3, 4, quantise(3, 4, grouped3))]
+
+        groups13 = [quantise(1, 3, grouped12), quantise(3, 4, grouped3)]
         for n in range(BLOCKS):
-            scatter(firsts[n], n, 0, 1)
-        for n in range(BLOCKS):
-            for e0, e1, operand in quantised:
-                matmuls(e0, e1, operand, (n,))
+            scatter(y_first[n], n, 0, 1)
+        multiply(groups13)
         for n in range(BLOCKS - 1):
             finish(new_y(f"y_middle{n}", 3, f"y_middle{n}"), n, 1, 4)
 
         grouped47 = new_grouped(4, 8, "codes3")
         for j in range(PACK):
             scalar_gather(grouped47, 4, 8, j)
-        multiply(4, 8, grouped47[:], range(BLOCKS))
+        multiply([quantise(4, 8, grouped47[:])])
 
         finish(new_y("y_kept", 3, "words_first"), BLOCKS - 1, 1, 4)
 

@@ -41,7 +41,7 @@ def tile_routed_moe_kernel(tc, xT, w_words, w_scales, b, gate, offs, out):
         w_scale_rows = [keep.tile([P, N], U8, name=f"w_scale_rows{h}", align_bytes=64) for h in range(E // PER_BANK)]
 
         for tile in w_scale_rows:
-            nc.gpsimd.memset(tile[:].bitcast(I32), 0)
+            nc.vector.memset(tile[:].bitcast(I32), 0)
         nc.vector.memset(warm[:], 0.0)
         nc.scalar.activation(warm[:], warm[:], GELU)
 

@@ -73,8 +73,8 @@ def tile_routed_moe_kernel(tc, xT, w_words, w_scales, b, gate, offs, out):
         words_first = keep.tile([P, N], U32, name="words_first", tag="words_first", align_bytes=64)
         nc.sync.dma_start(words_first[:].bitcast(I32), w_rows[:, 0, :])
         nc.sync.dma_start(gates[:, 0:C], gate[0:P, 0:C])
-        load_words(1, 4, 0, 2)
         load_words(1, 4, 2, 4)
+        load_words(1, 4, 0, 2)
         nc.sync.dma_start(gates[:, C:SLOTS], gate[0:P, C:SLOTS])
         load_scales(1)
         load_words(4, 8, 0, 4)
@@ -99,8 +99,8 @@ def tile_routed_moe_kernel(tc, xT, w_words, w_scales, b, gate, offs, out):
             nc.vector.quantize_mx(out=codes[:].bitcast(FP8X4), scales=scales[:], in_=grouped.rearrange("p s j -> p (s j)"))
             return e0, e1, codes, scales
 
-        def multiply(groups):
-            for n in range(BLOCKS):
+        def multiply(groups, blocks=range(BLOCKS)):
+            for n in blocks:
                 feats = slice(n * P, (n + 1) * P)
                 for e0, e1, codes, scales in groups:
                     for e in range(e0, e1):
@@ -150,7 +150,7 @@ def tile_routed_moe_kernel(tc, xT, w_words, w_scales, b, gate, offs, out):
 
         vector_gather(grouped12, 1, 3, LAST_PLANE, last_tile[:, 0 : T + OVERHANG])
         windows = [keep.tile([P, T], F32, name=f"window{n}") for n in range(BLOCKS)]
-        y_first = [new_y(f"y_first{n}", 1, f"y_first{n}") for n in range(BLOCKS)]
+        y_first = [new_y(f"y_first{n}", 4 if n == 3 else 1, f"y_first{n}") for n in range(BLOCKS)]
         for n in range(BLOCKS):
             activate(y_first[n], n, 0, 1)
 
@@ -158,10 +158,12 @@ def tile_routed_moe_kernel(tc, xT, w_words, w_scales, b, gate, offs, out):
         nc.scalar.copy(rounded[LAST_PLANE][:], planes[LAST_PLANE])
 
         groups13 = [quantise(1, 3, grouped12), quantise(3, 4, grouped3)]
-        for n in range(BLOCKS):
-            scatter(y_first[n], n, 0, 1)
-        multiply(groups13)
         for n in range(BLOCKS - 1):
+            scatter(y_first[n], n, 0, 1)
+        multiply(groups13, (3, 2, 0, 1))
+        activate(y_first[3][:, C : 4 * C], 3, 1, 4)
+        scatter(y_first[3], 3, 0, 4)
+        for n in (2, 0):
             finish(new_y(f"y_middle{n}", 3, f"y_middle{n}"), n, 1, 4)
 
         grouped47 = new_grouped(4, 8, "codes3")
@@ -169,7 +171,7 @@ def tile_routed_moe_kernel(tc, xT, w_words, w_scales, b, gate, offs, out):
             scalar_gather(grouped47, 4, 8, j)
         multiply([quantise(4, 8, grouped47[:])])
 
-        finish(new_y("y_kept", 3, "words_first"), BLOCKS - 1, 1, 4)
+        finish(new_y("y_kept", 3, "words_first"), 1, 1, 4)
 
         for n in range(BLOCKS):
             finish(new_y(f"y_last{n}", 4, f"y_last{n}"), n, 4, 8)

@@ -23,9 +23,8 @@ COPY = mybir.ActivationFunctionType.Copy
 FLOPS = 2 * K * N * SLOTS
 BYTES = 4 * K * T + E * K * N + E * (K // 32) * N + 4 * N * E + 4 * SLOTS + 2 * 128 * SLOTS // 16 + 4 * N * T
 
-LOAD_ORDER = (2, 0, 1, 3)
-FIRST_PLANE, LAST_PLANE = LOAD_ORDER[0], LOAD_ORDER[-1]
-OVERHANG = 8
+CHUNKS = ((0, 256, 384), (384, 640, 768), (768, 928, 1024))
+A, B, CC, D = 0, 1, 2, 3
 
 
 def tile_routed_moe_kernel(tc, xT, w_words, w_scales, b, gate, offs, out):
@@ -39,9 +38,12 @@ def tile_routed_moe_kernel(tc, xT, w_words, w_scales, b, gate, offs, out):
         gates = keep.tile([P, SLOTS], F32, name="gates")
         warm = keep.tile([P, 1], F32, name="warm")
         w_scale_rows = [keep.tile([P, N], U8, name=f"w_scale_rows{h}", align_bytes=64) for h in range(E // PER_BANK)]
+        token_codes = keep.tile([P, T], U32, name="token_codes", align_bytes=64)
+        token_scales = keep.tile([P, T], U8, name="token_scales", align_bytes=64)
 
         for tile in w_scale_rows:
             nc.vector.memset(tile[:].bitcast(I32), 0)
+        nc.vector.memset(token_scales[:].bitcast(I32), 0)
         nc.vector.memset(warm[:], 0.0)
         nc.scalar.activation(warm[:], warm[:], GELU)
 
@@ -56,30 +58,40 @@ def tile_routed_moe_kernel(tc, xT, w_words, w_scales, b, gate, offs, out):
                     w_scales[PER_BANK * h : PER_BANK * (h + 1), 0, 4 * quad : 4 * quad + 4, :].bitcast(I32),
                 )
 
-        def load_words(e0, e1, n0, n1):
-            nc.sync.dma_start(words[:, e0:e1, n0 * P : n1 * P].bitcast(I32), w_rows[:, e0:e1, n0 * P : n1 * P])
+        def load_words(e0, e1):
+            nc.sync.dma_start(words[:, e0:e1, :].bitcast(I32), w_rows[:, e0:e1, :])
 
-        last_tile = keep.tile([P, T + C], F32, name="last_tile", align_bytes=64)
-        last_of_3 = last_tile[:, T : T + C]
-        planes = {j: keep.tile([P, T], F32, name=f"plane{j}") for j in LOAD_ORDER[:-1]}
-        planes[LAST_PLANE] = last_tile[:, 0:T]
-
-        for j in LOAD_ORDER:
-            nc.sync.dma_start(planes[j][:], x_rows[:, j, :])
-            if j == FIRST_PLANE:
+        raw = [keep.tile([P, PACK, t1 - t0], F32, name=f"raw{t0}") for t0, ts, t1 in CHUNKS]
+        for c, (t0, ts, t1) in enumerate(CHUNKS):
+            nc.sync.dma_start(raw[c][:], x_rows[:, :, t0:t1])
+            if c == 0:
                 nc.sync.dma_start(offsets[:], offs)
         load_scales(0)
+        load_words(0, 1)
         nc.sync.dma_start(bias[:], b.rearrange("(c p) e -> p c e", p=P))
-        words_first = keep.tile([P, N], U32, name="words_first", tag="words_first", align_bytes=64)
-        nc.sync.dma_start(words_first[:].bitcast(I32), w_rows[:, 0, :])
-        nc.sync.dma_start(gates[:, 0:C], gate[0:P, 0:C])
-        load_words(1, 4, 2, 4)
-        load_words(1, 4, 0, 2)
-        nc.sync.dma_start(gates[:, C:SLOTS], gate[0:P, C:SLOTS])
+        load_words(1, 2)
+        nc.sync.dma_start(gates[:, 0 : 2 * C], gate[0:P, 0 : 2 * C])
+        load_words(2, 4)
+        nc.sync.dma_start(gates[:, 2 * C : SLOTS], gate[0:P, 2 * C : SLOTS])
         load_scales(1)
-        load_words(4, 8, 0, 4)
+        load_words(4, 8)
+
+        for c, (t0, ts, t1) in enumerate(CHUNKS):
+            grouped = keep.tile([P, t1 - t0, PACK], BF16, name=f"grouped{t0}", align_bytes=64)
+            for copy, a0, a1 in ((nc.vector.tensor_copy, 0, ts - t0), (nc.scalar.copy, ts - t0, t1 - t0)):
+                copy(
+                    grouped[:, a0:a1, :].rearrange("p (c i) j -> p c j i", i=4),
+                    raw[c][:, :, a0:a1].rearrange("p j (c i) -> p c j i", i=4),
+                )
+            nc.vector.quantize_mx(
+                out=token_codes[:, t0:t1].bitcast(FP8X4),
+                scales=token_scales[:, t0:t1],
+                in_=grouped[:].rearrange("p t j -> p (t j)"),
+            )
 
         banks = [[psum.tile([P, PER_BANK, C], F32, name=f"bank{n}{h}") for h in range(E // PER_BANK)] for n in range(BLOCKS)]
+        windows = [keep.tile([P, T], F32, name=f"window{n}") for n in range(BLOCKS)]
+        ys = [keep.tile([P, SLOTS], F32, name=f"y{n}") for n in range(BLOCKS)]
 
         def listed(e0, e1):
             return offsets[:, e0 * C // 16 : e1 * C // 16]
@@ -87,92 +99,87 @@ def tile_routed_moe_kernel(tc, xT, w_words, w_scales, b, gate, offs, out):
         def sums(n, e):
             return banks[n][e // PER_BANK][:, e % PER_BANK, :]
 
-        def vector_gather(grouped, e0, e1, j, source):
-            nc.vector.tensor_copy(grouped[:, :, j], source.indirect(listed(e0, e1)))
-
-        def scalar_gather(grouped, e0, e1, j):
-            nc.scalar.activation(grouped[:, :, j], rounded[j][:].indirect(listed(e0, e1)), COPY)
-
-        def quantise(e0, e1, grouped):
-            codes = keep.tile([P, (e1 - e0) * C], U32, name=f"codes{e0}", tag=f"codes{e0}", align_bytes=64)
+        def gather(e0, e1):
+            codes = keep.tile([P, (e1 - e0) * C], U32, name=f"codes{e0}", align_bytes=64)
             scales = keep.tile([P, (e1 - e0) * C], U8, name=f"scales{e0}", align_bytes=64)
-            nc.vector.quantize_mx(out=codes[:].bitcast(FP8X4), scales=scales[:], in_=grouped.rearrange("p s j -> p (s j)"))
+            nc.vector.tensor_copy(codes[:], token_codes[:].indirect(listed(e0, e1)))
+            nc.vector.tensor_copy(scales[:], token_scales[:].indirect(listed(e0, e1)))
             return e0, e1, codes, scales
 
-        def multiply(groups, blocks=range(BLOCKS)):
+        def multiply(group, blocks):
+            e0, e1, codes, scales = group
             for n in blocks:
                 feats = slice(n * P, (n + 1) * P)
-                for e0, e1, codes, scales in groups:
-                    for e in range(e0, e1):
-                        slots = slice((e - e0) * C, (e - e0 + 1) * C)
-                        nc.tensor.matmul_mx(
-                            out=sums(n, e),
-                            lhsT=(words_first[:, feats] if e == 0 else words[:, e, feats]).bitcast(FP8X4),
-                            lhsT_scale=w_scale_rows[e // PER_BANK][4 * (e % PER_BANK) : P, feats],
-                            rhs=codes[:, slots].bitcast(FP8X4),
-                            rhs_scale=scales[:, slots],
-                            start=True,
-                            stop=True,
-                        )
+                for e in range(e0, e1):
+                    slots = slice((e - e0) * C, (e - e0 + 1) * C)
+                    nc.tensor.matmul_mx(
+                        out=sums(n, e),
+                        lhsT=words[:, e, feats].bitcast(FP8X4),
+                        lhsT_scale=w_scale_rows[e // PER_BANK][4 * (e % PER_BANK) : P, feats],
+                        rhs=codes[:, slots].bitcast(FP8X4),
+                        rhs_scale=scales[:, slots],
+                        start=True,
+                        stop=True,
+                    )
 
-        def activate(y, n, e0, e1):
+        def activate(n, e0, e1):
             for e in range(e0, e1):
-                nc.scalar.activation(y[:, (e - e0) * C : (e - e0 + 1) * C], sums(n, e), GELU, bias=bias[:, n, e : e + 1])
+                nc.scalar.activation(ys[n][:, e * C : (e + 1) * C], sums(n, e), GELU, bias=bias[:, n, e : e + 1])
 
-        def scatter(y, n, e0, e1):
-            nc.vector.tensor_tensor(windows[n][:].indirect(listed(e0, e1)), y, gates[:, e0 * C : e1 * C], MULT)
+        def weigh(n, e0, e1):
+            y = ys[n][:, e0 * C : e1 * C]
+            nc.gpsimd.tensor_tensor(y, y, gates[:, e0 * C : e1 * C], MULT)
 
-        def finish(y, n, e0, e1):
-            activate(y, n, e0, e1)
-            scatter(y, n, e0, e1)
+        def vector_scatter(n, e0, e1):
+            nc.vector.tensor_copy(windows[n][:].indirect(listed(e0, e1)), ys[n][:, e0 * C : e1 * C])
 
-        def new_grouped(e0, e1, tag):
-            return keep.tile([P, (e1 - e0) * C, PACK], BF16, name=f"grouped{e0}", tag=tag, align_bytes=64)
+        def scalar_scatter(n, e0, e1):
+            nc.scalar.activation(windows[n][:].indirect(listed(e0, e1)), ys[n][:, e0 * C : e1 * C], COPY)
 
-        def new_y(name, experts, tag):
-            return keep.tile([P, experts * C], F32, name=name, tag=tag, align_bytes=64)[:]
-
-        grouped03 = new_grouped(0, 4, "grouped03")
-        grouped0, grouped12, grouped3 = grouped03[:, 0:C], grouped03[:, C : 3 * C], grouped03[:, 3 * C : 4 * C]
-        rounded = {j: keep.tile([P, T], BF16, name=f"rounded{j}") for j in range(PACK) if j != LAST_PLANE}
-        vector_gather(grouped03[:, 0 : 3 * C], 0, 3, FIRST_PLANE, planes[FIRST_PLANE][:])
-        nc.scalar.copy(rounded[FIRST_PLANE][:], planes[FIRST_PLANE][:])
-        scalar_gather(grouped3, 3, 4, FIRST_PLANE)
-        for j in LOAD_ORDER[1:-1]:
-            nc.vector.tensor_copy(rounded[j][:], planes[j][:])
-            vector_gather(grouped0, 0, 1, j, planes[j][:])
-            scalar_gather(grouped03[:, C : 4 * C], 1, 4, j)
-
-        vector_gather(grouped0, 0, 1, LAST_PLANE, planes[LAST_PLANE])
-        nc.vector.tensor_copy(last_of_3, planes[LAST_PLANE].indirect(listed(3, 4)))
-        nc.scalar.copy(grouped3[:, :, LAST_PLANE], last_of_3)
-        multiply([quantise(0, 1, grouped0)])
-
-        vector_gather(grouped12, 1, 3, LAST_PLANE, last_tile[:, 0 : T + OVERHANG])
-        windows = [keep.tile([P, T], F32, name=f"window{n}") for n in range(BLOCKS)]
-        y_first = [new_y(f"y_first{n}", 4 if n == 3 else 1, f"y_first{n}") for n in range(BLOCKS)]
-        for n in range(BLOCKS):
-            activate(y_first[n], n, 0, 1)
-
-        rounded[LAST_PLANE] = keep.tile([P, T], BF16, name="rounded_last", tag="words_first", align_bytes=64)
-        nc.scalar.copy(rounded[LAST_PLANE][:], planes[LAST_PLANE])
-
-        groups13 = [quantise(1, 3, grouped12), quantise(3, 4, grouped3)]
-        for n in range(BLOCKS - 1):
-            scatter(y_first[n], n, 0, 1)
-        multiply(groups13, (3, 2, 0, 1))
-        activate(y_first[3][:, C : 4 * C], 3, 1, 4)
-        scatter(y_first[3], 3, 0, 4)
-        for n in (2, 0):
-            finish(new_y(f"y_middle{n}", 3, f"y_middle{n}"), n, 1, 4)
-
-        grouped47 = new_grouped(4, 8, "codes3")
-        for j in range(PACK):
-            scalar_gather(grouped47, 4, 8, j)
-        multiply([quantise(4, 8, grouped47[:])])
-
-        finish(new_y("y_kept", 3, "words_first"), 1, 1, 4)
-
-        for n in range(BLOCKS):
-            finish(new_y(f"y_last{n}", 4, f"y_last{n}"), n, 4, 8)
+        def store(n):
             nc.sync.dma_start(out[n * P : (n + 1) * P, :], windows[n][:])
+
+        def ready(n, e0, e1, first=None):
+            activate(n, e0 if first is None else first, e1)
+            weigh(n, e0, e1)
+
+        group0, group1, group23, group47 = gather(0, 1), gather(1, 2), gather(2, 4), gather(4, 8)
+
+        multiply(group0, (CC, D, A, B))
+        ready(CC, 0, 1)
+        ready(D, 0, 1)
+        activate(A, 0, 1)
+        activate(B, 0, 1)
+        scalar_scatter(CC, 0, 1)
+        multiply(group1, (CC, A, D, B))
+        ready(CC, 1, 2)
+        ready(A, 0, 2, 1)
+        scalar_scatter(D, 0, 1)
+        multiply(group23, (A, CC, D, B))
+        ready(A, 2, 4)
+        ready(CC, 2, 4)
+        scalar_scatter(CC, 1, 2)
+        vector_scatter(A, 0, 2)
+        vector_scatter(A, 2, 4)
+        ready(B, 0, 4, 1)
+        ready(D, 1, 4)
+        scalar_scatter(CC, 2, 4)
+        vector_scatter(B, 0, 4)
+        multiply(group47, (CC, A, D, B))
+        ready(CC, 4, 6)
+        ready(A, 4, 8)
+        scalar_scatter(D, 1, 4)
+        vector_scatter(A, 4, 8)
+        store(A)
+        ready(CC, 6, 8)
+        scalar_scatter(CC, 4, 6)
+        ready(B, 4, 8)
+        vector_scatter(B, 4, 8)
+        ready(D, 4, 6)
+        scalar_scatter(CC, 6, 8)
+        store(CC)
+        store(B)
+        ready(D, 6, 8)
+        scalar_scatter(D, 4, 6)
+        scalar_scatter(D, 6, 8)
+        store(D)

@@ -23,7 +23,8 @@ COPY = mybir.ActivationFunctionType.Copy
 FLOPS = 2 * K * N * SLOTS
 BYTES = 4 * K * T + E * K * N + E * (K // 32) * N + 4 * N * E + 4 * SLOTS + 2 * 128 * SLOTS // 16 + 4 * N * T
 
-CHUNKS = ((0, 256, 384), (384, 640, 768), (768, 928, 1024))
+CHUNKS = ((0, 640), (640, 1024))
+PIECES = (((0, 256, True), (256, 512, False), (512, 640, True)), ((640, 896, True), (896, 1024, False)))
 A, B, CC, D = 0, 1, 2, 3
 
 
@@ -61,8 +62,8 @@ def tile_routed_moe_kernel(tc, xT, w_words, w_scales, b, gate, offs, out):
         def load_words(e0, e1):
             nc.sync.dma_start(words[:, e0:e1, :].bitcast(I32), w_rows[:, e0:e1, :])
 
-        raw = [keep.tile([P, PACK, t1 - t0], F32, name=f"raw{t0}") for t0, ts, t1 in CHUNKS]
-        for c, (t0, ts, t1) in enumerate(CHUNKS):
+        raw = [keep.tile([P, PACK, t1 - t0], F32, name=f"raw{t0}") for t0, t1 in CHUNKS]
+        for c, (t0, t1) in enumerate(CHUNKS):
             nc.sync.dma_start(raw[c][:], x_rows[:, :, t0:t1])
             if c == 0:
                 nc.sync.dma_start(offsets[:], offs)
@@ -76,18 +77,29 @@ def tile_routed_moe_kernel(tc, xT, w_words, w_scales, b, gate, offs, out):
         load_scales(1)
         load_words(4, 8)
 
-        for c, (t0, ts, t1) in enumerate(CHUNKS):
+        def rounded(c, t0, t1, on_vector):
             grouped = keep.tile([P, t1 - t0, PACK], BF16, name=f"grouped{t0}", align_bytes=64)
-            for copy, a0, a1 in ((nc.vector.tensor_copy, 0, ts - t0), (nc.scalar.copy, ts - t0, t1 - t0)):
-                copy(
-                    grouped[:, a0:a1, :].rearrange("p (c i) j -> p c j i", i=4),
-                    raw[c][:, :, a0:a1].rearrange("p j (c i) -> p c j i", i=4),
-                )
+            copy = nc.vector.tensor_copy if on_vector else nc.scalar.copy
+            first = CHUNKS[c][0]
+            copy(
+                grouped[:].rearrange("p (c i) j -> p c j i", i=4),
+                raw[c][:, :, t0 - first : t1 - first].rearrange("p j (c i) -> p c j i", i=4),
+            )
+            return t0, t1, grouped
+
+        def quantise(t0, t1, grouped):
             nc.vector.quantize_mx(
                 out=token_codes[:, t0:t1].bitcast(FP8X4),
                 scales=token_scales[:, t0:t1],
                 in_=grouped[:].rearrange("p t j -> p (t j)"),
             )
+
+        first = [rounded(0, *piece) for piece in PIECES[0]]
+        for i in (0, 2, 1):
+            quantise(*first[i])
+        second = [rounded(1, *piece) for piece in PIECES[1]]
+        for i in (1, 0):
+            quantise(*second[i])
 
         banks = [[psum.tile([P, PER_BANK, C], F32, name=f"bank{n}{h}") for h in range(E // PER_BANK)] for n in range(BLOCKS)]
         windows = [keep.tile([P, T], F32, name=f"window{n}") for n in range(BLOCKS)]
@@ -147,39 +159,38 @@ def tile_routed_moe_kernel(tc, xT, w_words, w_scales, b, gate, offs, out):
 
         multiply(group0, (CC, D, A, B))
         ready(CC, 0, 1)
-        ready(D, 0, 1)
+        activate(D, 0, 1)
         activate(A, 0, 1)
-        activate(B, 0, 1)
-        scalar_scatter(CC, 0, 1)
-        multiply(group1, (CC, A, D, B))
+        multiply(group1, (CC, D, A, B))
         ready(CC, 1, 2)
+        ready(D, 0, 2, 1)
+        scalar_scatter(CC, 0, 1)
         ready(A, 0, 2, 1)
-        scalar_scatter(D, 0, 1)
-        multiply(group23, (A, CC, D, B))
-        ready(A, 2, 4)
+        multiply(group23, (CC, A, B, D))
         ready(CC, 2, 4)
         scalar_scatter(CC, 1, 2)
+        vector_scatter(D, 0, 2)
         vector_scatter(A, 0, 2)
+        ready(A, 2, 4)
         vector_scatter(A, 2, 4)
-        ready(B, 0, 4, 1)
-        ready(D, 1, 4)
-        scalar_scatter(CC, 2, 4)
-        vector_scatter(B, 0, 4)
+        activate(B, 0, 4)
         multiply(group47, (CC, A, D, B))
         ready(CC, 4, 6)
+        weigh(B, 0, 4)
+        vector_scatter(B, 0, 4)
+        scalar_scatter(CC, 2, 4)
+        ready(CC, 6, 8)
         ready(A, 4, 8)
-        scalar_scatter(D, 1, 4)
         vector_scatter(A, 4, 8)
         store(A)
-        ready(CC, 6, 8)
         scalar_scatter(CC, 4, 6)
-        ready(B, 4, 8)
-        vector_scatter(B, 4, 8)
-        ready(D, 4, 6)
+        ready(D, 2, 5)
         scalar_scatter(CC, 6, 8)
         store(CC)
-        store(B)
-        ready(D, 6, 8)
-        scalar_scatter(D, 4, 6)
-        scalar_scatter(D, 6, 8)
+        ready(D, 5, 8)
+        ready(B, 4, 8)
+        scalar_scatter(D, 2, 5)
+        scalar_scatter(D, 5, 8)
         store(D)
+        vector_scatter(B, 4, 8)
+        store(B)

@@ -23,8 +23,8 @@ COPY = mybir.ActivationFunctionType.Copy
 FLOPS = 2 * K * N * SLOTS
 BYTES = 4 * K * T + E * K * N + E * (K // 32) * N + 4 * N * E + 4 * SLOTS + 2 * 128 * SLOTS // 16 + 4 * N * T
 
-CHUNKS = ((0, 640), (640, 1024))
-PIECES = (((0, 256, True), (256, 512, False), (512, 640, True)), ((640, 896, True), (896, 1024, False)))
+HALF = E // 2
+SPLIT = 1.5
 A, B, CC, D = 0, 1, 2, 3
 
 
@@ -39,12 +39,9 @@ def tile_routed_moe_kernel(tc, xT, w_words, w_scales, b, gate, offs, out):
         gates = keep.tile([P, SLOTS], F32, name="gates")
         warm = keep.tile([P, 1], F32, name="warm")
         w_scale_rows = [keep.tile([P, N], U8, name=f"w_scale_rows{h}", align_bytes=64) for h in range(E // PER_BANK)]
-        token_codes = keep.tile([P, T], U32, name="token_codes", align_bytes=64)
-        token_scales = keep.tile([P, T], U8, name="token_scales", align_bytes=64)
 
         for tile in w_scale_rows:
             nc.vector.memset(tile[:].bitcast(I32), 0)
-        nc.vector.memset(token_scales[:].bitcast(I32), 0)
         nc.vector.memset(warm[:], 0.0)
         nc.scalar.activation(warm[:], warm[:], GELU)
 
@@ -62,10 +59,10 @@ def tile_routed_moe_kernel(tc, xT, w_words, w_scales, b, gate, offs, out):
         def load_words(e0, e1):
             nc.sync.dma_start(words[:, e0:e1, :].bitcast(I32), w_rows[:, e0:e1, :])
 
-        raw = [keep.tile([P, PACK, t1 - t0], F32, name=f"raw{t0}") for t0, t1 in CHUNKS]
-        for c, (t0, t1) in enumerate(CHUNKS):
-            nc.sync.dma_start(raw[c][:], x_rows[:, :, t0:t1])
-            if c == 0:
+        planes = [keep.tile([P, T], F32, name=f"plane{j}") for j in range(PACK)]
+        for j in range(PACK):
+            nc.sync.dma_start(planes[j][:], x_rows[:, j, :])
+            if j == 0:
                 nc.sync.dma_start(offsets[:], offs)
         load_scales(0)
         load_words(0, 1)
@@ -73,56 +70,55 @@ def tile_routed_moe_kernel(tc, xT, w_words, w_scales, b, gate, offs, out):
         load_words(1, 2)
         nc.sync.dma_start(gates[:, 0 : 2 * C], gate[0:P, 0 : 2 * C])
         load_words(2, 4)
-        nc.sync.dma_start(gates[:, 2 * C : SLOTS], gate[0:P, 2 * C : SLOTS])
+        nc.sync.dma_start(gates[:, 2 * C : 4 * C], gate[0:P, 2 * C : 4 * C])
         load_scales(1)
-        load_words(4, 8)
-
-        def rounded(c, t0, t1, on_vector):
-            grouped = keep.tile([P, t1 - t0, PACK], BF16, name=f"grouped{t0}", align_bytes=64)
-            copy = nc.vector.tensor_copy if on_vector else nc.scalar.copy
-            first = CHUNKS[c][0]
-            copy(
-                grouped[:].rearrange("p (c i) j -> p c j i", i=4),
-                raw[c][:, :, t0 - first : t1 - first].rearrange("p j (c i) -> p c j i", i=4),
-            )
-            return t0, t1, grouped
-
-        def quantise(t0, t1, grouped):
-            nc.vector.quantize_mx(
-                out=token_codes[:, t0:t1].bitcast(FP8X4),
-                scales=token_scales[:, t0:t1],
-                in_=grouped[:].rearrange("p t j -> p (t j)"),
-            )
-
-        first = [rounded(0, *piece) for piece in PIECES[0]]
-        for i in (0, 2, 1):
-            quantise(*first[i])
-        second = [rounded(1, *piece) for piece in PIECES[1]]
-        for i in (1, 0):
-            quantise(*second[i])
+        load_words(4, 6)
+        nc.sync.dma_start(gates[:, 4 * C : SLOTS], gate[0:P, 4 * C : SLOTS])
+        load_words(6, 8)
 
         banks = [[psum.tile([P, PER_BANK, C], F32, name=f"bank{n}{h}") for h in range(E // PER_BANK)] for n in range(BLOCKS)]
         windows = [keep.tile([P, T], F32, name=f"window{n}") for n in range(BLOCKS)]
         ys = [keep.tile([P, SLOTS], F32, name=f"y{n}") for n in range(BLOCKS)]
 
         def listed(e0, e1):
-            return offsets[:, e0 * C // 16 : e1 * C // 16]
+            return offsets[:, int(e0 * C) // 16 : int(e1 * C) // 16]
 
         def sums(n, e):
-            return banks[n][e // PER_BANK][:, e % PER_BANK, :]
+            return banks[n][e % 2][:, e // 2, :]
 
-        def gather(e0, e1):
+        pairs = keep.tile([P, 3, 2 * C, 2], BF16, name="pairs", align_bytes=64)
+        singles = keep.tile([P, PACK, HALF * C], BF16, name="singles", align_bytes=64)
+
+        def vector_gather(j, e0, e1):
+            first = e0 * C if j < 2 else (HALF + e0 % 2) * C
+            into = pairs[:].rearrange("p r s i -> p (r s) i")[:, first : first + (e1 - e0) * C, j % 2]
+            nc.vector.tensor_copy(into, planes[j][:].indirect(listed(e0, e1)))
+
+        def scalar_gather(j):
+            nc.scalar.activation(singles[:, j, :], planes[j][:].indirect(listed(HALF, E)), COPY)
+
+        def interleave(e0, e1):
+            grouped = keep.tile([P, (e1 - e0) * C, PACK], BF16, name=f"grouped{e0}", align_bytes=64)
+            if e0 < HALF:
+                both = pairs[:].bitcast(F32)[:, e0 // 2 : 3 : 2 - e0 // 2, e0 % 2 * C : (e0 % 2 + e1 - e0) * C, :]
+                nc.vector.tensor_copy(grouped[:].bitcast(F32), both.rearrange("p u s o -> p s (u o)"))
+            else:
+                nc.vector.tensor_copy(
+                    grouped[:].rearrange("p (c i) j -> p c j i", i=4),
+                    singles[:, :, (e0 - HALF) * C : (e1 - HALF) * C].rearrange("p j (c i) -> p c j i", i=4),
+                )
+            return e0, e1, grouped
+
+        def quantise(e0, e1, grouped):
             codes = keep.tile([P, (e1 - e0) * C], U32, name=f"codes{e0}", align_bytes=64)
             scales = keep.tile([P, (e1 - e0) * C], U8, name=f"scales{e0}", align_bytes=64)
-            nc.vector.tensor_copy(codes[:], token_codes[:].indirect(listed(e0, e1)))
-            nc.vector.tensor_copy(scales[:], token_scales[:].indirect(listed(e0, e1)))
+            nc.vector.quantize_mx(out=codes[:].bitcast(FP8X4), scales=scales[:], in_=grouped[:].rearrange("p s j -> p (s j)"))
             return e0, e1, codes, scales
 
-        def multiply(group, blocks):
-            e0, e1, codes, scales = group
+        def multiply(blocks, *groups):
             for n in blocks:
                 feats = slice(n * P, (n + 1) * P)
-                for e in range(e0, e1):
+                for e0, e, codes, scales in [(g[0], e, g[2], g[3]) for g in groups for e in range(g[0], g[1])]:
                     slots = slice((e - e0) * C, (e - e0 + 1) * C)
                     nc.tensor.matmul_mx(
                         out=sums(n, e),
@@ -139,14 +135,14 @@ def tile_routed_moe_kernel(tc, xT, w_words, w_scales, b, gate, offs, out):
                 nc.scalar.activation(ys[n][:, e * C : (e + 1) * C], sums(n, e), GELU, bias=bias[:, n, e : e + 1])
 
         def weigh(n, e0, e1):
-            y = ys[n][:, e0 * C : e1 * C]
-            nc.gpsimd.tensor_tensor(y, y, gates[:, e0 * C : e1 * C], MULT)
+            y = ys[n][:, int(e0 * C) : int(e1 * C)]
+            nc.gpsimd.tensor_tensor(y, y, gates[:, int(e0 * C) : int(e1 * C)], MULT)
 
         def vector_scatter(n, e0, e1):
-            nc.vector.tensor_copy(windows[n][:].indirect(listed(e0, e1)), ys[n][:, e0 * C : e1 * C])
+            nc.vector.tensor_copy(windows[n][:].indirect(listed(e0, e1)), ys[n][:, int(e0 * C) : int(e1 * C)])
 
         def scalar_scatter(n, e0, e1):
-            nc.scalar.activation(windows[n][:].indirect(listed(e0, e1)), ys[n][:, e0 * C : e1 * C], COPY)
+            nc.scalar.activation(windows[n][:].indirect(listed(e0, e1)), ys[n][:, int(e0 * C) : int(e1 * C)], COPY)
 
         def store(n):
             nc.sync.dma_start(out[n * P : (n + 1) * P, :], windows[n][:])
@@ -155,42 +151,62 @@ def tile_routed_moe_kernel(tc, xT, w_words, w_scales, b, gate, offs, out):
             activate(n, e0 if first is None else first, e1)
             weigh(n, e0, e1)
 
-        group0, group1, group23, group47 = gather(0, 1), gather(1, 2), gather(2, 4), gather(4, 8)
+        for j in range(PACK):
+            scalar_gather(j)
+        vector_gather(0, 0, HALF)
+        vector_gather(1, 0, HALF)
+        vector_gather(2, 0, 2)
+        vector_gather(3, 0, 1)
+        vector_gather(3, 1, 2)
+        grouped0, grouped1 = interleave(0, 1), interleave(1, 2)
+        group0 = quantise(*grouped0)
+        group1 = quantise(*grouped1)
+        vector_gather(2, 2, 4)
+        vector_gather(3, 2, 4)
+        grouped45, grouped23, grouped67 = interleave(4, 6), interleave(2, 4), interleave(6, 8)
+        group23 = quantise(*grouped23)
+        group45 = quantise(*grouped45)
+        group67 = quantise(*grouped67)
 
-        multiply(group0, (CC, D, A, B))
+        multiply((CC, A, D, B), group0)
+        multiply((D, A, CC, B), group1)
         ready(CC, 0, 1)
-        activate(D, 0, 1)
         activate(A, 0, 1)
-        multiply(group1, (CC, D, A, B))
-        ready(CC, 1, 2)
-        ready(D, 0, 2, 1)
-        scalar_scatter(CC, 0, 1)
+        activate(D, 0, 2)
+        weigh(D, 0, SPLIT)
+        activate(B, 0, 1)
         ready(A, 0, 2, 1)
-        multiply(group23, (CC, A, B, D))
-        ready(CC, 2, 4)
-        scalar_scatter(CC, 1, 2)
-        vector_scatter(D, 0, 2)
+        scalar_scatter(CC, 0, 1)
+        ready(CC, 1, 2)
+        ready(B, 0, 2, 1)
         vector_scatter(A, 0, 2)
+        vector_scatter(B, 0, 2)
+        scalar_scatter(D, 0, SPLIT)
+        multiply((CC, A, B, D), group23)
+        ready(CC, 2, 4)
         ready(A, 2, 4)
         vector_scatter(A, 2, 4)
-        activate(B, 0, 4)
-        multiply(group47, (CC, A, D, B))
-        ready(CC, 4, 6)
-        weigh(B, 0, 4)
-        vector_scatter(B, 0, 4)
+        scalar_scatter(CC, 1, 2)
+        ready(B, 2, 4)
+        vector_scatter(B, 2, 4)
+        activate(D, 2, 4)
+        weigh(D, SPLIT, 4)
+        vector_scatter(D, SPLIT, 4)
         scalar_scatter(CC, 2, 4)
-        ready(CC, 6, 8)
+        multiply((CC, A, D, B), group45, group67)
+        ready(CC, 4, 6)
         ready(A, 4, 8)
         vector_scatter(A, 4, 8)
         store(A)
         scalar_scatter(CC, 4, 6)
-        ready(D, 2, 5)
+        ready(CC, 6, 8)
+        ready(D, 4, 6)
+        ready(B, 4, 8)
+        ready(D, 6, 8)
         scalar_scatter(CC, 6, 8)
         store(CC)
-        ready(D, 5, 8)
-        ready(B, 4, 8)
-        scalar_scatter(D, 2, 5)
-        scalar_scatter(D, 5, 8)
+        scalar_scatter(D, 4, 6)
+        scalar_scatter(D, 6, 8)
         store(D)
         vector_scatter(B, 4, 8)
         store(B)

@@ -24,7 +24,7 @@ FLOPS = 2 * K * N * SLOTS
 BYTES = 4 * K * T + E * K * N + E * (K // 32) * N + 4 * N * E + 4 * SLOTS + 2 * 128 * SLOTS // 16 + 4 * N * T
 
 HALF = E // 2
-SPLIT = 1.5
+SPLIT = 1.75
 A, B, CC, D = 0, 1, 2, 3
 
 
@@ -65,9 +65,8 @@ def tile_routed_moe_kernel(tc, xT, w_words, w_scales, b, gate, offs, out):
             if j == 0:
                 nc.sync.dma_start(offsets[:], offs)
         load_scales(0)
-        load_words(0, 1)
+        load_words(0, 2)
         nc.sync.dma_start(bias[:], b.rearrange("(c p) e -> p c e", p=P))
-        load_words(1, 2)
         nc.sync.dma_start(gates[:, 0 : 2 * C], gate[0:P, 0 : 2 * C])
         load_words(2, 4)
         nc.sync.dma_start(gates[:, 2 * C : 4 * C], gate[0:P, 2 * C : 4 * C])
@@ -77,7 +76,7 @@ def tile_routed_moe_kernel(tc, xT, w_words, w_scales, b, gate, offs, out):
         load_words(6, 8)
 
         banks = [[psum.tile([P, PER_BANK, C], F32, name=f"bank{n}{h}") for h in range(E // PER_BANK)] for n in range(BLOCKS)]
-        windows = [keep.tile([P, T], F32, name=f"window{n}") for n in range(BLOCKS)]
+        windows = {n: keep.tile([P, T], F32, name=f"window{n}") for n in (B, CC, D)}
         ys = [keep.tile([P, SLOTS], F32, name=f"y{n}") for n in range(BLOCKS)]
 
         def listed(e0, e1):
@@ -87,7 +86,7 @@ def tile_routed_moe_kernel(tc, xT, w_words, w_scales, b, gate, offs, out):
             return banks[n][e % 2][:, e // 2, :]
 
         pairs = keep.tile([P, 3, 2 * C, 2], BF16, name="pairs", align_bytes=64)
-        singles = keep.tile([P, PACK, HALF * C], BF16, name="singles", align_bytes=64)
+        singles = keep.tile([P, PACK, HALF * C], BF16, name="singles", tag="singles", align_bytes=64)
 
         def vector_gather(j, e0, e1):
             first = e0 * C if j < 2 else (HALF + e0 % 2) * C
@@ -97,8 +96,8 @@ def tile_routed_moe_kernel(tc, xT, w_words, w_scales, b, gate, offs, out):
         def scalar_gather(j):
             nc.scalar.activation(singles[:, j, :], planes[j][:].indirect(listed(HALF, E)), COPY)
 
-        def interleave(e0, e1):
-            grouped = keep.tile([P, (e1 - e0) * C, PACK], BF16, name=f"grouped{e0}", align_bytes=64)
+        def interleave(e0, e1, tag):
+            grouped = keep.tile([P, (e1 - e0) * C, PACK], BF16, name=f"grouped{e0}", tag=tag, align_bytes=64)
             if e0 < HALF:
                 both = pairs[:].bitcast(F32)[:, e0 // 2 : 3 : 2 - e0 // 2, e0 % 2 * C : (e0 % 2 + e1 - e0) * C, :]
                 nc.vector.tensor_copy(grouped[:].bitcast(F32), both.rearrange("p u s o -> p s (u o)"))
@@ -109,8 +108,8 @@ def tile_routed_moe_kernel(tc, xT, w_words, w_scales, b, gate, offs, out):
                 )
             return e0, e1, grouped
 
-        def quantise(e0, e1, grouped):
-            codes = keep.tile([P, (e1 - e0) * C], U32, name=f"codes{e0}", align_bytes=64)
+        def quantise(e0, e1, grouped, tag=None):
+            codes = keep.tile([P, (e1 - e0) * C], U32, name=f"codes{e0}", tag=tag or f"codes{e0}", align_bytes=64)
             scales = keep.tile([P, (e1 - e0) * C], U8, name=f"scales{e0}", align_bytes=64)
             nc.vector.quantize_mx(out=codes[:].bitcast(FP8X4), scales=scales[:], in_=grouped[:].rearrange("p s j -> p (s j)"))
             return e0, e1, codes, scales
@@ -130,26 +129,31 @@ def tile_routed_moe_kernel(tc, xT, w_words, w_scales, b, gate, offs, out):
                         stop=True,
                     )
 
-        def activate(n, e0, e1):
+        def cols(e0, e1):
+            return slice(int(e0 * C), int(e1 * C))
+
+        def activate(n, e0, e1, into=None):
             for e in range(e0, e1):
-                nc.scalar.activation(ys[n][:, e * C : (e + 1) * C], sums(n, e), GELU, bias=bias[:, n, e : e + 1])
+                nc.scalar.activation((ys[n] if into is None else into)[:, cols(e, e + 1)], sums(n, e), GELU, bias=bias[:, n, e : e + 1])
 
-        def weigh(n, e0, e1):
-            y = ys[n][:, int(e0 * C) : int(e1 * C)]
-            nc.gpsimd.tensor_tensor(y, y, gates[:, int(e0 * C) : int(e1 * C)], MULT)
+        def weigh(engine, n, e0, e1, source=None, into=None):
+            y = ys[n][:, cols(e0, e1)]
+            result = y if into is None else into
+            engine.tensor_tensor(result, y if source is None else source[:, cols(e0, e1)], gates[:, cols(e0, e1)], MULT)
+            return n, e0, e1, result
 
-        def vector_scatter(n, e0, e1):
-            nc.vector.tensor_copy(windows[n][:].indirect(listed(e0, e1)), ys[n][:, int(e0 * C) : int(e1 * C)])
+        def vector_scatter(n, e0, e1, values):
+            nc.vector.tensor_copy(windows[n][:].indirect(listed(e0, e1)), values)
 
-        def scalar_scatter(n, e0, e1):
-            nc.scalar.activation(windows[n][:].indirect(listed(e0, e1)), ys[n][:, int(e0 * C) : int(e1 * C)], COPY)
+        def scalar_scatter(n, e0, e1, values):
+            nc.scalar.activation(windows[n][:].indirect(listed(e0, e1)), values, COPY)
 
         def store(n):
             nc.sync.dma_start(out[n * P : (n + 1) * P, :], windows[n][:])
 
-        def ready(n, e0, e1, first=None):
-            activate(n, e0 if first is None else first, e1)
-            weigh(n, e0, e1)
+        def ready(n, e0, e1):
+            activate(n, e0, e1)
+            return weigh(nc.gpsimd, n, e0, e1)
 
         for j in range(PACK):
             scalar_gather(j)
@@ -158,55 +162,52 @@ def tile_routed_moe_kernel(tc, xT, w_words, w_scales, b, gate, offs, out):
         vector_gather(2, 0, 2)
         vector_gather(3, 0, 1)
         vector_gather(3, 1, 2)
-        grouped0, grouped1 = interleave(0, 1), interleave(1, 2)
+        grouped0, grouped1 = interleave(0, 1, "grouped0"), interleave(1, 2, "grouped1")
         group0 = quantise(*grouped0)
         group1 = quantise(*grouped1)
         vector_gather(2, 2, 4)
         vector_gather(3, 2, 4)
-        grouped45, grouped23, grouped67 = interleave(4, 6), interleave(2, 4), interleave(6, 8)
-        group23 = quantise(*grouped23)
-        group45 = quantise(*grouped45)
-        group67 = quantise(*grouped67)
+        grouped23 = interleave(2, 4, "grouped2")
 
-        multiply((CC, A, D, B), group0)
-        multiply((D, A, CC, B), group1)
-        ready(CC, 0, 1)
-        activate(A, 0, 1)
+        multiply((CC, A, D, B), group0, group1)
+        first = keep.tile([P, 2, 2 * C], F32, name="first", tag="shared", align_bytes=64)
+        weighed = keep.tile([P, 2, 2 * C], F32, name="weighed")
+        activate(CC, 0, 2, first[:, 0, :])
+        activate(A, 0, 2, first[:, 1, :])
+        nc.vector.tensor_tensor(weighed[:], first[:], gates[:, cols(0, 2)].unsqueeze(1).to_broadcast([P, 2, 2 * C]), MULT)
+        grouped47 = interleave(4, 8, "shared")
+        group23 = quantise(*grouped23, "singles")
+        group47 = quantise(*grouped47)
         activate(D, 0, 2)
-        weigh(D, 0, SPLIT)
-        activate(B, 0, 1)
-        ready(A, 0, 2, 1)
-        scalar_scatter(CC, 0, 1)
-        ready(CC, 1, 2)
-        ready(B, 0, 2, 1)
-        vector_scatter(A, 0, 2)
-        vector_scatter(B, 0, 2)
-        scalar_scatter(D, 0, SPLIT)
+        activate(B, 0, 2)
+        scalar_scatter(CC, 0, 2, weighed[:, 0, :])
+        windows[A] = keep.tile([P, T], F32, name="window_a", tag="grouped2", align_bytes=64)
+        vector_scatter(A, 0, 2, weighed[:, 1, :])
+
+        held = keep.tile([P, 12 * C], F32, name="held", tag="shared", align_bytes=64)
+        d0 = weigh(nc.gpsimd, D, 0, SPLIT, into=held[:, cols(0, SPLIT)])
+        vector_scatter(*weigh(nc.gpsimd, B, 0, 2, into=held[:, cols(4, 6)]))
         multiply((CC, A, B, D), group23)
-        ready(CC, 2, 4)
-        ready(A, 2, 4)
-        vector_scatter(A, 2, 4)
-        scalar_scatter(CC, 1, 2)
-        ready(B, 2, 4)
-        vector_scatter(B, 2, 4)
+        activate(CC, 2, 4)
+        c23 = weigh(nc.gpsimd, CC, 2, 4, into=held[:, cols(6, 8)])
+        activate(A, 2, 4)
+        vector_scatter(*weigh(nc.gpsimd, A, 2, 4, into=held[:, cols(8, 10)]))
+        activate(B, 2, 4)
         activate(D, 2, 4)
-        weigh(D, SPLIT, 4)
-        vector_scatter(D, SPLIT, 4)
-        scalar_scatter(CC, 2, 4)
-        multiply((CC, A, D, B), group45, group67)
-        ready(CC, 4, 6)
-        ready(A, 4, 8)
-        vector_scatter(A, 4, 8)
+        scalar_scatter(*d0)
+        multiply((CC, A, D, B), group47)
+        c45 = ready(CC, 4, 6)
+        vector_scatter(*weigh(nc.gpsimd, B, 2, 4, into=held[:, cols(10, 12)]))
+        vector_scatter(*weigh(nc.gpsimd, D, SPLIT, 4, into=held[:, cols(SPLIT, 4)]))
+        scalar_scatter(*c23)
+        vector_scatter(*ready(A, 4, 8))
         store(A)
-        scalar_scatter(CC, 4, 6)
-        ready(CC, 6, 8)
-        ready(D, 4, 6)
-        ready(B, 4, 8)
-        ready(D, 6, 8)
-        scalar_scatter(CC, 6, 8)
+        scalar_scatter(*c45)
+        c67, d45, b47, d67 = ready(CC, 6, 8), ready(D, 4, 6), ready(B, 4, 8), ready(D, 6, 8)
+        scalar_scatter(*c67)
         store(CC)
-        scalar_scatter(D, 4, 6)
-        scalar_scatter(D, 6, 8)
+        scalar_scatter(*d45)
+        scalar_scatter(*d67)
         store(D)
-        vector_scatter(B, 4, 8)
+        vector_scatter(*b47)
         store(B)

@@ -24,7 +24,7 @@ FLOPS = 2 * K * N * SLOTS
 BYTES = 4 * K * T + E * K * N + E * (K // 32) * N + 4 * N * E + 4 * SLOTS + 2 * 128 * SLOTS // 16 + 4 * N * T
 
 HALF = E // 2
-SPLIT = 1.75
+SPLIT = 4
 A, B, CC, D = 0, 1, 2, 3
 
 
@@ -69,11 +69,10 @@ def tile_routed_moe_kernel(tc, xT, w_words, w_scales, b, gate, offs, out):
         nc.sync.dma_start(bias[:], b.rearrange("(c p) e -> p c e", p=P))
         nc.sync.dma_start(gates[:, 0 : 2 * C], gate[0:P, 0 : 2 * C])
         load_words(2, 4)
-        nc.sync.dma_start(gates[:, 2 * C : 4 * C], gate[0:P, 2 * C : 4 * C])
         load_scales(1)
         load_words(4, 6)
-        nc.sync.dma_start(gates[:, 4 * C : SLOTS], gate[0:P, 4 * C : SLOTS])
         load_words(6, 8)
+        nc.sync.dma_start(gates[:, 2 * C : SLOTS], gate[0:P, 2 * C : SLOTS])
 
         banks = [[psum.tile([P, PER_BANK, C], F32, name=f"bank{n}{h}") for h in range(E // PER_BANK)] for n in range(BLOCKS)]
         windows = {n: keep.tile([P, T], F32, name=f"window{n}") for n in (B, CC, D)}
@@ -83,7 +82,7 @@ def tile_routed_moe_kernel(tc, xT, w_words, w_scales, b, gate, offs, out):
             return offsets[:, int(e0 * C) // 16 : int(e1 * C) // 16]
 
         def sums(n, e):
-            return banks[n][e % 2][:, e // 2, :]
+            return banks[n][e // 2 % 2][:, e // 4 * 2 + e % 2, :]
 
         pairs = keep.tile([P, 3, 2 * C, 2], BF16, name="pairs", align_bytes=64)
         singles = keep.tile([P, PACK, HALF * C], BF16, name="singles", tag="singles", align_bytes=64)
@@ -96,14 +95,13 @@ def tile_routed_moe_kernel(tc, xT, w_words, w_scales, b, gate, offs, out):
         def scalar_gather(j):
             nc.scalar.activation(singles[:, j, :], planes[j][:].indirect(listed(HALF, E)), COPY)
 
-        def interleave(e0, e1, tag):
-            grouped = keep.tile([P, (e1 - e0) * C, PACK], BF16, name=f"grouped{e0}", tag=tag, align_bytes=64)
+        def interleave(e0, e1, grouped):
             if e0 < HALF:
                 both = pairs[:].bitcast(F32)[:, e0 // 2 : 3 : 2 - e0 // 2, e0 % 2 * C : (e0 % 2 + e1 - e0) * C, :]
-                nc.vector.tensor_copy(grouped[:].bitcast(F32), both.rearrange("p u s o -> p s (u o)"))
+                nc.vector.tensor_copy(grouped.bitcast(F32), both.rearrange("p u s o -> p s (u o)"))
             else:
                 nc.vector.tensor_copy(
-                    grouped[:].rearrange("p (c i) j -> p c j i", i=4),
+                    grouped.rearrange("p (c i) j -> p c j i", i=4),
                     singles[:, :, (e0 - HALF) * C : (e1 - HALF) * C].rearrange("p j (c i) -> p c j i", i=4),
                 )
             return e0, e1, grouped
@@ -111,7 +109,7 @@ def tile_routed_moe_kernel(tc, xT, w_words, w_scales, b, gate, offs, out):
         def quantise(e0, e1, grouped, tag=None):
             codes = keep.tile([P, (e1 - e0) * C], U32, name=f"codes{e0}", tag=tag or f"codes{e0}", align_bytes=64)
             scales = keep.tile([P, (e1 - e0) * C], U8, name=f"scales{e0}", align_bytes=64)
-            nc.vector.quantize_mx(out=codes[:].bitcast(FP8X4), scales=scales[:], in_=grouped[:].rearrange("p s j -> p (s j)"))
+            nc.vector.quantize_mx(out=codes[:].bitcast(FP8X4), scales=scales[:], in_=grouped.rearrange("p s j -> p (s j)"))
             return e0, e1, codes, scales
 
         def multiply(blocks, *groups):
@@ -162,12 +160,12 @@ def tile_routed_moe_kernel(tc, xT, w_words, w_scales, b, gate, offs, out):
         vector_gather(2, 0, 2)
         vector_gather(3, 0, 1)
         vector_gather(3, 1, 2)
-        grouped0, grouped1 = interleave(0, 1, "grouped0"), interleave(1, 2, "grouped1")
+        early = keep.tile([P, 2 * C, PACK], BF16, name="early", align_bytes=64)
+        grouped0, grouped1 = interleave(0, 1, early[:, cols(0, 1)]), interleave(1, 2, early[:, cols(1, 2)])
         group0 = quantise(*grouped0)
         group1 = quantise(*grouped1)
         vector_gather(2, 2, 4)
         vector_gather(3, 2, 4)
-        grouped23 = interleave(2, 4, "grouped2")
 
         multiply((CC, A, D, B), group0, group1)
         first = keep.tile([P, 2, 2 * C], F32, name="first", tag="shared", align_bytes=64)
@@ -175,39 +173,50 @@ def tile_routed_moe_kernel(tc, xT, w_words, w_scales, b, gate, offs, out):
         activate(CC, 0, 2, first[:, 0, :])
         activate(A, 0, 2, first[:, 1, :])
         nc.vector.tensor_tensor(weighed[:], first[:], gates[:, cols(0, 2)].unsqueeze(1).to_broadcast([P, 2, 2 * C]), MULT)
-        grouped47 = interleave(4, 8, "shared")
-        group23 = quantise(*grouped23, "singles")
-        group47 = quantise(*grouped47)
+        late = keep.tile([P, 6 * C, PACK], BF16, name="late", tag="shared", align_bytes=64)
+        grouped23 = interleave(2, 4, late[:, cols(0, 2)])
+        grouped45 = interleave(4, 6, late[:, cols(2, 4)])
+        group23 = quantise(*grouped23)
         activate(D, 0, 2)
+        d01 = weigh(nc.vector, D, 0, 2)
+        grouped67 = interleave(6, 8, late[:, cols(4, 6)])
+        group45 = quantise(*grouped45)
+        group67 = quantise(*grouped67)
         activate(B, 0, 2)
         scalar_scatter(CC, 0, 2, weighed[:, 0, :])
-        windows[A] = keep.tile([P, T], F32, name="window_a", tag="grouped2", align_bytes=64)
+        scalar_scatter(*d01)
+        windows[A] = keep.tile([P, T], F32, name="window_a", tag="singles", align_bytes=64)
         vector_scatter(A, 0, 2, weighed[:, 1, :])
 
-        held = keep.tile([P, 12 * C], F32, name="held", tag="shared", align_bytes=64)
-        d0 = weigh(nc.gpsimd, D, 0, SPLIT, into=held[:, cols(0, SPLIT)])
-        vector_scatter(*weigh(nc.gpsimd, B, 0, 2, into=held[:, cols(4, 6)]))
-        multiply((CC, A, B, D), group23)
+        held = keep.tile([P, 10 * C], F32, name="held", tag="shared", align_bytes=64)
+        vector_scatter(*weigh(nc.gpsimd, B, 0, 2, into=held[:, cols(0, 2)]))
+
+        multiply((CC, A, D, B), group23)
         activate(CC, 2, 4)
-        c23 = weigh(nc.gpsimd, CC, 2, 4, into=held[:, cols(6, 8)])
+        scalar_scatter(*weigh(nc.gpsimd, CC, 2, 4, into=held[:, cols(2, 4)]))
         activate(A, 2, 4)
-        vector_scatter(*weigh(nc.gpsimd, A, 2, 4, into=held[:, cols(8, 10)]))
-        activate(B, 2, 4)
+        vector_scatter(*weigh(nc.gpsimd, A, 2, 4, into=held[:, cols(4, 6)]))
         activate(D, 2, 4)
-        scalar_scatter(*d0)
-        multiply((CC, A, D, B), group47)
+        vector_scatter(*weigh(nc.gpsimd, D, 2, SPLIT, into=held[:, cols(6, 4 + SPLIT)]))
+        activate(B, 2, 4)
+        b23 = weigh(nc.gpsimd, B, 2, 4, into=held[:, cols(8, 10)])
+
+        multiply((CC, D, A, B), group45)
+        multiply((A, CC, D, B), group67)
         c45 = ready(CC, 4, 6)
-        vector_scatter(*weigh(nc.gpsimd, B, 2, 4, into=held[:, cols(10, 12)]))
-        vector_scatter(*weigh(nc.gpsimd, D, SPLIT, 4, into=held[:, cols(SPLIT, 4)]))
-        scalar_scatter(*c23)
-        vector_scatter(*ready(A, 4, 8))
-        store(A)
+        vector_scatter(*b23)
         scalar_scatter(*c45)
-        c67, d45, b47, d67 = ready(CC, 6, 8), ready(D, 4, 6), ready(B, 4, 8), ready(D, 6, 8)
-        scalar_scatter(*c67)
+        ready(A, 4, 6)
+        ready(A, 6, 8)
+        vector_scatter(A, 4, 8, ys[A][:, cols(4, 8)])
+        store(A)
+        scalar_scatter(*ready(CC, 6, 8))
         store(CC)
-        scalar_scatter(*d45)
-        scalar_scatter(*d67)
+        activate(D, 4, 6)
+        scalar_scatter(*weigh(nc.gpsimd, D, SPLIT, 6))
+        scalar_scatter(*ready(D, 6, 8))
         store(D)
-        vector_scatter(*b47)
+        ready(B, 4, 6)
+        ready(B, 6, 8)
+        vector_scatter(B, 4, 8, ys[B][:, cols(4, 8)])
         store(B)

@@ -2,12 +2,17 @@ from contextlib import ExitStack
 
 import concourse.mybir as mybir
 
-K, T, E, C, N = 512, 1024, 8, 128, 512
+K, T, E, N = 512, 1024, 8, 512
+CAP = 128
 P = 128
 PACK = 4
-SLOTS = E * C
-BLOCKS = N // P
-PER_BANK = 4
+SLOTS = E * CAP
+GROUPS = N // P
+PER_TILE = 4
+HALF = E // 2
+PAIR = 2 * CAP
+A, B, C, D = range(GROUPS)
+SPLIT = 480
 
 F32 = mybir.dt.float32
 BF16 = mybir.dt.bfloat16
@@ -23,10 +28,6 @@ COPY = mybir.ActivationFunctionType.Copy
 FLOPS = 2 * K * N * SLOTS
 BYTES = 4 * K * T + E * K * N + E * (K // 32) * N + 4 * N * E + 4 * SLOTS + 2 * 128 * SLOTS // 16 + 4 * N * T
 
-HALF = E // 2
-SPLIT = 4
-A, B, CC, D = 0, 1, 2, 3
-
 
 def tile_routed_moe_kernel(tc, xT, w_words, w_scales, b, gate, offs, out):
     nc = tc.nc
@@ -35,10 +36,10 @@ def tile_routed_moe_kernel(tc, xT, w_words, w_scales, b, gate, offs, out):
         psum = ctx.enter_context(tc.psum_pool(name="psum", bufs=1))
 
         offsets = keep.tile([P, SLOTS // 16], U16, name="offsets")
-        bias = keep.tile([P, BLOCKS, E], F32, name="bias")
+        bias = keep.tile([P, GROUPS, E], F32, name="bias")
         gates = keep.tile([P, SLOTS], F32, name="gates")
         warm = keep.tile([P, 1], F32, name="warm")
-        w_scale_rows = [keep.tile([P, N], U8, name=f"w_scale_rows{h}", align_bytes=64) for h in range(E // PER_BANK)]
+        w_scale_rows = [keep.tile([P, N], U8, name=f"w_scale_rows{h}", align_bytes=64) for h in range(E // PER_TILE)]
 
         for tile in w_scale_rows:
             nc.vector.memset(tile[:].bitcast(I32), 0)
@@ -53,7 +54,7 @@ def tile_routed_moe_kernel(tc, xT, w_words, w_scales, b, gate, offs, out):
             for quad in range(4):
                 nc.sync.dma_start(
                     w_scale_rows[h][32 * quad : 32 * quad + 16, :].bitcast(I32),
-                    w_scales[PER_BANK * h : PER_BANK * (h + 1), 0, 4 * quad : 4 * quad + 4, :].bitcast(I32),
+                    w_scales[PER_TILE * h : PER_TILE * (h + 1), 0, 4 * quad : 4 * quad + 4, :].bitcast(I32),
                 )
 
         def load_words(e0, e1):
@@ -67,91 +68,92 @@ def tile_routed_moe_kernel(tc, xT, w_words, w_scales, b, gate, offs, out):
         load_scales(0)
         load_words(0, 2)
         nc.sync.dma_start(bias[:], b.rearrange("(c p) e -> p c e", p=P))
-        nc.sync.dma_start(gates[:, 0 : 2 * C], gate[0:P, 0 : 2 * C])
+        nc.sync.dma_start(gates[:, 0:PAIR], gate[0:P, 0:PAIR])
         load_words(2, 4)
         load_scales(1)
         load_words(4, 6)
         load_words(6, 8)
-        nc.sync.dma_start(gates[:, 2 * C : SLOTS], gate[0:P, 2 * C : SLOTS])
+        nc.sync.dma_start(gates[:, PAIR:SLOTS], gate[0:P, PAIR:SLOTS])
 
-        banks = [[psum.tile([P, PER_BANK, C], F32, name=f"bank{n}{h}") for h in range(E // PER_BANK)] for n in range(BLOCKS)]
-        windows = {n: keep.tile([P, T], F32, name=f"window{n}") for n in (B, CC, D)}
-        ys = [keep.tile([P, SLOTS], F32, name=f"y{n}") for n in range(BLOCKS)]
+        banks = [[psum.tile([P, PER_TILE, CAP], F32, name=f"bank{n}{h}") for h in range(E // PER_TILE)] for n in range(GROUPS)]
+        windows = {n: keep.tile([P, T], F32, name=f"window{n}") for n in (B, C, D)}
+        ys = [keep.tile([P, SLOTS], F32, name=f"y{n}") for n in range(GROUPS)]
 
-        def listed(e0, e1):
-            return offsets[:, int(e0 * C) // 16 : int(e1 * C) // 16]
+        def slots(e0, e1):
+            return slice(e0 * CAP, e1 * CAP)
+
+        def listed(cols):
+            return offsets[:, cols.start // 16 : cols.stop // 16]
 
         def sums(n, e):
             return banks[n][e // 2 % 2][:, e // 4 * 2 + e % 2, :]
 
-        pairs = keep.tile([P, 3, 2 * C, 2], BF16, name="pairs", align_bytes=64)
-        singles = keep.tile([P, PACK, HALF * C], BF16, name="singles", tag="singles", align_bytes=64)
+        pairs = keep.tile([P, 3, PAIR, 2], BF16, name="pairs", align_bytes=64)
+        singles = keep.tile([P, PACK, HALF * CAP], BF16, name="singles", tag="singles", align_bytes=64)
 
         def vector_gather(j, e0, e1):
-            first = e0 * C if j < 2 else (HALF + e0 % 2) * C
-            into = pairs[:].rearrange("p r s i -> p (r s) i")[:, first : first + (e1 - e0) * C, j % 2]
-            nc.vector.tensor_copy(into, planes[j][:].indirect(listed(e0, e1)))
+            start = e0 * CAP if j < 2 else (HALF + e0 % 2) * CAP
+            into = pairs[:].rearrange("p r s i -> p (r s) i")[:, start : start + (e1 - e0) * CAP, j % 2]
+            nc.vector.tensor_copy(into, planes[j][:].indirect(listed(slots(e0, e1))))
 
         def scalar_gather(j):
-            nc.scalar.activation(singles[:, j, :], planes[j][:].indirect(listed(HALF, E)), COPY)
+            nc.scalar.activation(singles[:, j, :], planes[j][:].indirect(listed(slots(HALF, E))), COPY)
 
-        def interleave(e0, e1, grouped):
-            if e0 < HALF:
-                both = pairs[:].bitcast(F32)[:, e0 // 2 : 3 : 2 - e0 // 2, e0 % 2 * C : (e0 % 2 + e1 - e0) * C, :]
-                nc.vector.tensor_copy(grouped.bitcast(F32), both.rearrange("p u s o -> p s (u o)"))
-            else:
-                nc.vector.tensor_copy(
-                    grouped.rearrange("p (c i) j -> p c j i", i=4),
-                    singles[:, :, (e0 - HALF) * C : (e1 - HALF) * C].rearrange("p j (c i) -> p c j i", i=4),
-                )
+        def interleave_pairs(e0, e1, grouped):
+            part = e0 // 2
+            halves = pairs[:].bitcast(F32)[:, part : 3 : 2 - part, slots(e0 % 2, e0 % 2 + e1 - e0), :]
+            nc.vector.tensor_copy(grouped.bitcast(F32), halves.rearrange("p u s o -> p s (u o)"))
             return e0, e1, grouped
 
-        def quantise(e0, e1, grouped, tag=None):
-            codes = keep.tile([P, (e1 - e0) * C], U32, name=f"codes{e0}", tag=tag or f"codes{e0}", align_bytes=64)
-            scales = keep.tile([P, (e1 - e0) * C], U8, name=f"scales{e0}", align_bytes=64)
+        def interleave_singles(e0, e1, grouped):
+            nc.vector.tensor_copy(
+                grouped.rearrange("p (c i) j -> p c j i", i=4),
+                singles[:, :, slots(e0 - HALF, e1 - HALF)].rearrange("p j (c i) -> p c j i", i=4),
+            )
+            return e0, e1, grouped
+
+        def quantise(e0, e1, grouped):
+            codes = keep.tile([P, (e1 - e0) * CAP], U32, name=f"codes{e0}", align_bytes=64)
+            scales = keep.tile([P, (e1 - e0) * CAP], U8, name=f"scales{e0}", align_bytes=64)
             nc.vector.quantize_mx(out=codes[:].bitcast(FP8X4), scales=scales[:], in_=grouped.rearrange("p s j -> p (s j)"))
             return e0, e1, codes, scales
 
-        def multiply(blocks, *groups):
-            for n in blocks:
+        def multiply(*quantised):
+            for n in (C, A, D, B):
                 feats = slice(n * P, (n + 1) * P)
-                for e0, e, codes, scales in [(g[0], e, g[2], g[3]) for g in groups for e in range(g[0], g[1])]:
-                    slots = slice((e - e0) * C, (e - e0 + 1) * C)
-                    nc.tensor.matmul_mx(
-                        out=sums(n, e),
-                        lhsT=words[:, e, feats].bitcast(FP8X4),
-                        lhsT_scale=w_scale_rows[e // PER_BANK][4 * (e % PER_BANK) : P, feats],
-                        rhs=codes[:, slots].bitcast(FP8X4),
-                        rhs_scale=scales[:, slots],
-                        start=True,
-                        stop=True,
-                    )
+                for e0, e1, codes, scales in quantised:
+                    for e in range(e0, e1):
+                        own = slots(e - e0, e - e0 + 1)
+                        nc.tensor.matmul_mx(
+                            out=sums(n, e),
+                            lhsT=words[:, e, feats].bitcast(FP8X4),
+                            lhsT_scale=w_scale_rows[e // PER_TILE][4 * (e % PER_TILE) : P, feats],
+                            rhs=codes[:, own].bitcast(FP8X4),
+                            rhs_scale=scales[:, own],
+                            start=True,
+                            stop=True,
+                        )
 
-        def cols(e0, e1):
-            return slice(int(e0 * C), int(e1 * C))
-
-        def activate(n, e0, e1, into=None):
+        def activate(n, e0, e1, into):
             for e in range(e0, e1):
-                nc.scalar.activation((ys[n] if into is None else into)[:, cols(e, e + 1)], sums(n, e), GELU, bias=bias[:, n, e : e + 1])
+                nc.scalar.activation(into[:, slots(e, e + 1)], sums(n, e), GELU, bias=bias[:, n, e : e + 1])
 
-        def weigh(engine, n, e0, e1, source=None, into=None):
-            y = ys[n][:, cols(e0, e1)]
-            result = y if into is None else into
-            engine.tensor_tensor(result, y if source is None else source[:, cols(e0, e1)], gates[:, cols(e0, e1)], MULT)
-            return n, e0, e1, result
+        def weigh(n, cols, into):
+            nc.gpsimd.tensor_tensor(into, ys[n][:, cols], gates[:, cols], MULT)
+            return n, cols, into
 
-        def vector_scatter(n, e0, e1, values):
-            nc.vector.tensor_copy(windows[n][:].indirect(listed(e0, e1)), values)
+        def ready(n, e0, e1, into=None):
+            activate(n, e0, e1, ys[n])
+            return weigh(n, slots(e0, e1), ys[n][:, slots(e0, e1)] if into is None else into)
 
-        def scalar_scatter(n, e0, e1, values):
-            nc.scalar.activation(windows[n][:].indirect(listed(e0, e1)), values, COPY)
+        def vector_scatter(n, cols, values):
+            nc.vector.tensor_copy(windows[n][:].indirect(listed(cols)), values)
+
+        def scalar_scatter(n, cols, values):
+            nc.scalar.activation(windows[n][:].indirect(listed(cols)), values, COPY)
 
         def store(n):
             nc.sync.dma_start(out[n * P : (n + 1) * P, :], windows[n][:])
-
-        def ready(n, e0, e1):
-            activate(n, e0, e1)
-            return weigh(nc.gpsimd, n, e0, e1)
 
         for j in range(PACK):
             scalar_gather(j)
@@ -160,63 +162,62 @@ def tile_routed_moe_kernel(tc, xT, w_words, w_scales, b, gate, offs, out):
         vector_gather(2, 0, 2)
         vector_gather(3, 0, 1)
         vector_gather(3, 1, 2)
-        early = keep.tile([P, 2 * C, PACK], BF16, name="early", align_bytes=64)
-        grouped0, grouped1 = interleave(0, 1, early[:, cols(0, 1)]), interleave(1, 2, early[:, cols(1, 2)])
-        group0 = quantise(*grouped0)
-        group1 = quantise(*grouped1)
+        early = keep.tile([P, PAIR, PACK], BF16, name="early", align_bytes=64)
+        grouped0, grouped1 = interleave_pairs(0, 1, early[:, slots(0, 1)]), interleave_pairs(1, 2, early[:, slots(1, 2)])
+        quantised0 = quantise(*grouped0)
+        quantised1 = quantise(*grouped1)
         vector_gather(2, 2, 4)
-        vector_gather(3, 2, 4)
+        vector_gather(3, 2, 3)
 
-        multiply((CC, A, D, B), group0, group1)
-        first = keep.tile([P, 2, 2 * C], F32, name="first", tag="shared", align_bytes=64)
-        weighed = keep.tile([P, 2, 2 * C], F32, name="weighed")
-        activate(CC, 0, 2, first[:, 0, :])
-        activate(A, 0, 2, first[:, 1, :])
-        nc.vector.tensor_tensor(weighed[:], first[:], gates[:, cols(0, 2)].unsqueeze(1).to_broadcast([P, 2, 2 * C]), MULT)
-        late = keep.tile([P, 6 * C, PACK], BF16, name="late", tag="shared", align_bytes=64)
-        grouped23 = interleave(2, 4, late[:, cols(0, 2)])
-        grouped45 = interleave(4, 6, late[:, cols(2, 4)])
-        group23 = quantise(*grouped23)
-        activate(D, 0, 2)
-        d01 = weigh(nc.vector, D, 0, 2)
-        grouped67 = interleave(6, 8, late[:, cols(4, 6)])
-        group45 = quantise(*grouped45)
-        group67 = quantise(*grouped67)
-        activate(B, 0, 2)
-        scalar_scatter(CC, 0, 2, weighed[:, 0, :])
-        scalar_scatter(*d01)
+        multiply(quantised0, quantised1)
+        first = keep.tile([P, PAIR], F32, name="first", tag="shared", align_bytes=64)
+        both = keep.tile([P, 2, PAIR], F32, name="both")
+        activate(C, 0, 2, first)
+        nc.vector.tensor_tensor(ys[C][:, 0:PAIR], first[:], gates[:, 0:PAIR], MULT)
+        vector_gather(3, 3, 4)
+
+        late = keep.tile([P, 6 * CAP, PACK], BF16, name="late", tag="shared", align_bytes=64)
+        grouped23 = interleave_pairs(2, 4, late[:, slots(0, 2)])
+        grouped45 = interleave_singles(4, 6, late[:, slots(2, 4)])
+        quantised23 = quantise(*grouped23)
+        activate(D, 0, 2, both[:, 0, :])
+        activate(A, 0, 2, both[:, 1, :])
+        nc.vector.tensor_tensor(both[:], both[:], gates[:, 0:PAIR].unsqueeze(1).to_broadcast([P, 2, PAIR]), MULT)
+        grouped67 = interleave_singles(6, 8, late[:, slots(4, 6)])
+        quantised45 = quantise(*grouped45)
+        quantised67 = quantise(*grouped67)
+        activate(B, 0, 2, ys[B])
+        scalar_scatter(C, slots(0, 2), ys[C][:, 0:PAIR])
+        scalar_scatter(D, slots(0, 2), both[:, 0, :])
         windows[A] = keep.tile([P, T], F32, name="window_a", tag="singles", align_bytes=64)
-        vector_scatter(A, 0, 2, weighed[:, 1, :])
+        vector_scatter(A, slots(0, 2), both[:, 1, :])
 
-        held = keep.tile([P, 10 * C], F32, name="held", tag="shared", align_bytes=64)
-        vector_scatter(*weigh(nc.gpsimd, B, 0, 2, into=held[:, cols(0, 2)]))
+        held = keep.tile([P, 5 * PAIR], F32, name="held", tag="shared", align_bytes=64)
+        vector_scatter(*weigh(B, slots(0, 2), held[:, 0:PAIR]))
 
-        multiply((CC, A, D, B), group23)
-        activate(CC, 2, 4)
-        scalar_scatter(*weigh(nc.gpsimd, CC, 2, 4, into=held[:, cols(2, 4)]))
-        activate(A, 2, 4)
-        vector_scatter(*weigh(nc.gpsimd, A, 2, 4, into=held[:, cols(4, 6)]))
-        activate(D, 2, 4)
-        vector_scatter(*weigh(nc.gpsimd, D, 2, SPLIT, into=held[:, cols(6, 4 + SPLIT)]))
-        activate(B, 2, 4)
-        b23 = weigh(nc.gpsimd, B, 2, 4, into=held[:, cols(8, 10)])
+        multiply(quantised23)
+        scalar_scatter(*ready(C, 2, 4, held[:, PAIR : 2 * PAIR]))
+        vector_scatter(*ready(A, 2, 4, held[:, 2 * PAIR : 3 * PAIR]))
+        activate(D, 2, 4, ys[D])
+        vector_scatter(*weigh(D, slice(PAIR, SPLIT), held[:, 3 * PAIR : 2 * PAIR + SPLIT]))
+        b23 = ready(B, 2, 4, held[:, 4 * PAIR : 5 * PAIR])
 
-        multiply((CC, D, A, B), group45)
-        multiply((A, CC, D, B), group67)
-        c45 = ready(CC, 4, 6)
+        multiply(quantised45)
+        multiply(quantised67)
+        c45 = ready(C, 4, 6)
         vector_scatter(*b23)
         scalar_scatter(*c45)
+        scalar_scatter(*ready(C, 6, 8))
+        store(C)
         ready(A, 4, 6)
         ready(A, 6, 8)
-        vector_scatter(A, 4, 8, ys[A][:, cols(4, 8)])
+        vector_scatter(A, slots(4, 8), ys[A][:, slots(4, 8)])
         store(A)
-        scalar_scatter(*ready(CC, 6, 8))
-        store(CC)
-        activate(D, 4, 6)
-        scalar_scatter(*weigh(nc.gpsimd, D, SPLIT, 6))
+        activate(D, 4, 6, ys[D])
+        scalar_scatter(*weigh(D, slice(SPLIT, 3 * PAIR), ys[D][:, SPLIT : 3 * PAIR]))
         scalar_scatter(*ready(D, 6, 8))
         store(D)
         ready(B, 4, 6)
         ready(B, 6, 8)
-        vector_scatter(B, 4, 8, ys[B][:, cols(4, 8)])
+        vector_scatter(B, slots(4, 8), ys[B][:, slots(4, 8)])
         store(B)

@@ -12,7 +12,7 @@ PER_TILE = 4
 HALF = E // 2
 PAIR = 2 * CAP
 A, B, C, D = range(GROUPS)
-SPLIT = 480
+SPLIT = 448
 
 F32 = mybir.dt.float32
 BF16 = mybir.dt.bfloat16
@@ -70,10 +70,10 @@ def tile_routed_moe_kernel(tc, xT, w_words, w_scales, b, gate, offs, out):
         nc.sync.dma_start(bias[:], b.rearrange("(c p) e -> p c e", p=P))
         nc.sync.dma_start(gates[:, 0:PAIR], gate[0:P, 0:PAIR])
         load_words(2, 4)
+        nc.sync.dma_start(gates[:, PAIR : 2 * PAIR], gate[0:P, PAIR : 2 * PAIR])
         load_scales(1)
-        load_words(4, 6)
-        load_words(6, 8)
-        nc.sync.dma_start(gates[:, PAIR:SLOTS], gate[0:P, PAIR:SLOTS])
+        load_words(4, 8)
+        nc.sync.dma_start(gates[:, 2 * PAIR : SLOTS], gate[0:P, 2 * PAIR : SLOTS])
 
         banks = [[psum.tile([P, PER_TILE, CAP], F32, name=f"bank{n}{h}") for h in range(E // PER_TILE)] for n in range(GROUPS)]
         windows = {n: keep.tile([P, T], F32, name=f"window{n}") for n in (B, C, D)}
@@ -138,13 +138,14 @@ def tile_routed_moe_kernel(tc, xT, w_words, w_scales, b, gate, offs, out):
             for e in range(e0, e1):
                 nc.scalar.activation(into[:, slots(e, e + 1)], sums(n, e), GELU, bias=bias[:, n, e : e + 1])
 
-        def weigh(n, cols, into):
+        def weigh(n, cols, into=None):
+            into = ys[n][:, cols] if into is None else into
             nc.gpsimd.tensor_tensor(into, ys[n][:, cols], gates[:, cols], MULT)
             return n, cols, into
 
-        def ready(n, e0, e1, into=None):
+        def ready(n, e0, e1, into):
             activate(n, e0, e1, ys[n])
-            return weigh(n, slots(e0, e1), ys[n][:, slots(e0, e1)] if into is None else into)
+            return weigh(n, slots(e0, e1), into)
 
         def vector_scatter(n, cols, values):
             nc.vector.tensor_copy(windows[n][:].indirect(listed(cols)), values)
@@ -152,8 +153,8 @@ def tile_routed_moe_kernel(tc, xT, w_words, w_scales, b, gate, offs, out):
         def scalar_scatter(n, cols, values):
             nc.scalar.activation(windows[n][:].indirect(listed(cols)), values, COPY)
 
-        def store(n):
-            nc.sync.dma_start(out[n * P : (n + 1) * P, :], windows[n][:])
+        def store(n, queue=nc.sync):
+            queue.dma_start(out[n * P : (n + 1) * P, :], windows[n][:])
 
         for j in range(PACK):
             scalar_gather(j)
@@ -204,20 +205,20 @@ def tile_routed_moe_kernel(tc, xT, w_words, w_scales, b, gate, offs, out):
 
         multiply(quantised45)
         multiply(quantised67)
-        c45 = ready(C, 4, 6)
+        for n in (C, A, D, B):
+            activate(n, 4, 8, ys[n])
         vector_scatter(*b23)
-        scalar_scatter(*c45)
-        scalar_scatter(*ready(C, 6, 8))
+        scalar_scatter(*weigh(C, slots(4, 6)))
+        scalar_scatter(*weigh(C, slots(6, 8)))
         store(C)
-        ready(A, 4, 6)
-        ready(A, 6, 8)
+        weigh(A, slots(4, 6))
+        weigh(A, slots(6, 8))
         vector_scatter(A, slots(4, 8), ys[A][:, slots(4, 8)])
         store(A)
-        activate(D, 4, 6, ys[D])
-        scalar_scatter(*weigh(D, slice(SPLIT, 3 * PAIR), ys[D][:, SPLIT : 3 * PAIR]))
-        scalar_scatter(*ready(D, 6, 8))
-        store(D)
-        ready(B, 4, 6)
-        ready(B, 6, 8)
+        scalar_scatter(*weigh(D, slice(SPLIT, 3 * PAIR)))
+        scalar_scatter(*weigh(D, slots(6, 8)))
+        store(D, nc.scalar)
+        weigh(B, slots(4, 6))
+        weigh(B, slots(6, 8))
         vector_scatter(B, slots(4, 8), ys[B][:, slots(4, 8)])
         store(B)

@@ -12,7 +12,7 @@ PER_TILE = 4
 HALF = E // 2
 PAIR = 2 * CAP
 A, B, C, D = range(GROUPS)
-SPLIT = 448
+SPLIT = 224
 
 F32 = mybir.dt.float32
 BF16 = mybir.dt.bfloat16
@@ -22,6 +22,7 @@ U16 = mybir.dt.uint16
 U8 = mybir.dt.uint8
 FP8X4 = mybir.dt.float8_e4m3fn_x4
 MULT = mybir.AluOpType.mult
+ADD = mybir.AluOpType.add
 GELU = mybir.ActivationFunctionType.Gelu_apprx_tanh
 COPY = mybir.ActivationFunctionType.Copy
 
@@ -48,7 +49,7 @@ def tile_routed_moe_kernel(tc, xT, w_words, w_scales, b, gate, offs, out):
 
         x_rows = xT.rearrange("(p j) t -> p j t", j=PACK)
         w_rows = w_words.rearrange("e a p n r -> p (e a) (n r)").bitcast(I32)
-        words = keep.tile([P, E, N], U32, name="words", align_bytes=64)
+        words = [keep.tile([P, 2, N], U32, name=f"words{h}", tag=f"words{h}", align_bytes=64) for h in range(E // 2)]
 
         def load_scales(h):
             for quad in range(4):
@@ -58,7 +59,7 @@ def tile_routed_moe_kernel(tc, xT, w_words, w_scales, b, gate, offs, out):
                 )
 
         def load_words(e0, e1):
-            nc.sync.dma_start(words[:, e0:e1, :].bitcast(I32), w_rows[:, e0:e1, :])
+            nc.sync.dma_start(words[e0 // 2][:].bitcast(I32), w_rows[:, e0:e1, :])
 
         planes = [keep.tile([P, T], F32, name=f"plane{j}") for j in range(PACK)]
         for j in range(PACK):
@@ -70,14 +71,13 @@ def tile_routed_moe_kernel(tc, xT, w_words, w_scales, b, gate, offs, out):
         nc.sync.dma_start(bias[:], b.rearrange("(c p) e -> p c e", p=P))
         nc.sync.dma_start(gates[:, 0:PAIR], gate[0:P, 0:PAIR])
         load_words(2, 4)
-        nc.sync.dma_start(gates[:, PAIR : 2 * PAIR], gate[0:P, PAIR : 2 * PAIR])
         load_scales(1)
-        load_words(4, 8)
-        nc.sync.dma_start(gates[:, 2 * PAIR : SLOTS], gate[0:P, 2 * PAIR : SLOTS])
+        nc.sync.dma_start(gates[:, PAIR:SLOTS], gate[0:P, PAIR:SLOTS])
+        load_words(4, 6)
+        load_words(6, 8)
 
         banks = [[psum.tile([P, PER_TILE, CAP], F32, name=f"bank{n}{h}") for h in range(E // PER_TILE)] for n in range(GROUPS)]
-        windows = {n: keep.tile([P, T], F32, name=f"window{n}") for n in (B, C, D)}
-        ys = [keep.tile([P, SLOTS], F32, name=f"y{n}") for n in range(GROUPS)]
+        windows = {n: keep.tile([P, T], F32, name=f"window{n}") for n in (A, B, C)}
 
         def slots(e0, e1):
             return slice(e0 * CAP, e1 * CAP)
@@ -89,7 +89,14 @@ def tile_routed_moe_kernel(tc, xT, w_words, w_scales, b, gate, offs, out):
             return banks[n][e // 2 % 2][:, e // 4 * 2 + e % 2, :]
 
         pairs = keep.tile([P, 3, PAIR, 2], BF16, name="pairs", align_bytes=64)
-        singles = keep.tile([P, PACK, HALF * CAP], BF16, name="singles", tag="singles", align_bytes=64)
+        singles = keep.tile([P, PACK, HALF * CAP], BF16, name="singles", align_bytes=64)
+        grouped = {}
+
+        def group_tile(e0, e1, tag):
+            tile = keep.tile([P, (e1 - e0) * CAP, PACK], BF16, name=f"grouped{e0}", tag=tag, align_bytes=64)
+            for a in range(e0, e1):
+                for z in range(a + 1, e1 + 1):
+                    grouped[a, z] = tile[:, slots(a - e0, z - e0), :]
 
         def vector_gather(j, e0, e1):
             start = e0 * CAP if j < 2 else (HALF + e0 % 2) * CAP
@@ -99,53 +106,53 @@ def tile_routed_moe_kernel(tc, xT, w_words, w_scales, b, gate, offs, out):
         def scalar_gather(j):
             nc.scalar.activation(singles[:, j, :], planes[j][:].indirect(listed(slots(HALF, E))), COPY)
 
-        def interleave_pairs(e0, e1, grouped):
+        def interleave_pairs(e0, e1):
             part = e0 // 2
             halves = pairs[:].bitcast(F32)[:, part : 3 : 2 - part, slots(e0 % 2, e0 % 2 + e1 - e0), :]
-            nc.vector.tensor_copy(grouped.bitcast(F32), halves.rearrange("p u s o -> p s (u o)"))
-            return e0, e1, grouped
+            nc.vector.tensor_copy(grouped[e0, e1].bitcast(F32), halves.rearrange("p u s o -> p s (u o)"))
 
-        def interleave_singles(e0, e1, grouped):
+        def interleave_singles(e0, e1):
             nc.vector.tensor_copy(
-                grouped.rearrange("p (c i) j -> p c j i", i=4),
+                grouped[e0, e1].rearrange("p (c i) j -> p c j i", i=4),
                 singles[:, :, slots(e0 - HALF, e1 - HALF)].rearrange("p j (c i) -> p c j i", i=4),
             )
-            return e0, e1, grouped
 
-        def quantise(e0, e1, grouped):
-            codes = keep.tile([P, (e1 - e0) * CAP], U32, name=f"codes{e0}", align_bytes=64)
+        def some_planes(e, j0, j1):
+            source = singles[:, j0:j1, slots(e - HALF, e + 1 - HALF)].rearrange("p j s -> p s j")
+            return grouped[e, e + 1][:, :, j0:j1], source
+
+        quantised = {}
+
+        def quantise(e0, e1):
+            codes = keep.tile([P, (e1 - e0) * CAP], U32, name=f"codes{e0}", tag=f"codes{e0}", align_bytes=64)
             scales = keep.tile([P, (e1 - e0) * CAP], U8, name=f"scales{e0}", align_bytes=64)
-            nc.vector.quantize_mx(out=codes[:].bitcast(FP8X4), scales=scales[:], in_=grouped.rearrange("p s j -> p (s j)"))
-            return e0, e1, codes, scales
+            nc.vector.quantize_mx(
+                out=codes[:].bitcast(FP8X4), scales=scales[:], in_=grouped[e0, e1].rearrange("p s j -> p (s j)")
+            )
+            for e in range(e0, e1):
+                own = slots(e - e0, e - e0 + 1)
+                quantised[e] = codes[:, own].bitcast(FP8X4), scales[:, own]
 
-        def multiply(*quantised):
-            for n in (C, A, D, B):
+        def multiply(e0, e1, order):
+            for n in order:
                 feats = slice(n * P, (n + 1) * P)
-                for e0, e1, codes, scales in quantised:
-                    for e in range(e0, e1):
-                        own = slots(e - e0, e - e0 + 1)
-                        nc.tensor.matmul_mx(
-                            out=sums(n, e),
-                            lhsT=words[:, e, feats].bitcast(FP8X4),
-                            lhsT_scale=w_scale_rows[e // PER_TILE][4 * (e % PER_TILE) : P, feats],
-                            rhs=codes[:, own].bitcast(FP8X4),
-                            rhs_scale=scales[:, own],
-                            start=True,
-                            stop=True,
-                        )
+                for e in range(e0, e1):
+                    nc.tensor.matmul_mx(
+                        out=sums(n, e),
+                        lhsT=words[e // 2][:, e % 2, feats].bitcast(FP8X4),
+                        lhsT_scale=w_scale_rows[e // PER_TILE][4 * (e % PER_TILE) : P, feats],
+                        rhs=quantised[e][0],
+                        rhs_scale=quantised[e][1],
+                        start=True,
+                        stop=True,
+                    )
 
         def activate(n, e0, e1, into):
             for e in range(e0, e1):
-                nc.scalar.activation(into[:, slots(e, e + 1)], sums(n, e), GELU, bias=bias[:, n, e : e + 1])
+                nc.scalar.activation(into[:, slots(e - e0, e - e0 + 1)], sums(n, e), GELU, bias=bias[:, n, e : e + 1])
 
-        def weigh(n, cols, into=None):
-            into = ys[n][:, cols] if into is None else into
-            nc.gpsimd.tensor_tensor(into, ys[n][:, cols], gates[:, cols], MULT)
-            return n, cols, into
-
-        def ready(n, e0, e1, into):
-            activate(n, e0, e1, ys[n])
-            return weigh(n, slots(e0, e1), into)
+        def both_gates(e0, e1):
+            return gates[:, slots(e0, e1)].unsqueeze(1).to_broadcast([P, 2, (e1 - e0) * CAP])
 
         def vector_scatter(n, cols, values):
             nc.vector.tensor_copy(windows[n][:].indirect(listed(cols)), values)
@@ -156,69 +163,90 @@ def tile_routed_moe_kernel(tc, xT, w_words, w_scales, b, gate, offs, out):
         def store(n, queue=nc.sync):
             queue.dma_start(out[n * P : (n + 1) * P, :], windows[n][:])
 
+        group_tile(0, 1, "first")
+        group_tile(1, 2, "second")
+        group_tile(6, 7, "sixth")
         for j in range(PACK):
             scalar_gather(j)
+            if j == 1:
+                nc.gpsimd.tensor_scalar(*some_planes(6, 0, 2), 1.0, 0.0, MULT, ADD)
+        nc.scalar.copy(*some_planes(6, 2, 4))
         vector_gather(0, 0, HALF)
         vector_gather(1, 0, HALF)
         vector_gather(2, 0, 2)
         vector_gather(3, 0, 1)
         vector_gather(3, 1, 2)
-        early = keep.tile([P, PAIR, PACK], BF16, name="early", align_bytes=64)
-        grouped0, grouped1 = interleave_pairs(0, 1, early[:, slots(0, 1)]), interleave_pairs(1, 2, early[:, slots(1, 2)])
-        quantised0 = quantise(*grouped0)
-        quantised1 = quantise(*grouped1)
+        interleave_pairs(0, 1)
+        interleave_pairs(1, 2)
+        quantise(0, 1)
+        quantise(1, 2)
         vector_gather(2, 2, 4)
-        vector_gather(3, 2, 3)
+        vector_gather(3, 2, 4)
+        group_tile(7, 8, "second")
+        nc.gpsimd.tensor_scalar(*some_planes(7, 0, 4), 1.0, 0.0, MULT, ADD)
 
-        multiply(quantised0, quantised1)
-        first = keep.tile([P, PAIR], F32, name="first", tag="shared", align_bytes=64)
-        both = keep.tile([P, 2, PAIR], F32, name="both")
-        activate(C, 0, 2, first)
-        nc.vector.tensor_tensor(ys[C][:, 0:PAIR], first[:], gates[:, 0:PAIR], MULT)
-        vector_gather(3, 3, 4)
+        raw01 = keep.tile([P, 2, PAIR], F32, name="raw01", tag="late", align_bytes=64)
+        ac01 = keep.tile([P, 2, PAIR], F32, name="ac01")
+        bd01 = keep.tile([P, 2, PAIR], F32, name="bd01")
+        ad23 = keep.tile([P, 2, PAIR], F32, name="ad23")
+        bc23 = keep.tile([P, 2, PAIR], F32, name="bc23")
+        multiply(0, 2, (A, C, B, D))
+        for n, tile in ((A, raw01), (C, raw01), (B, bd01), (D, bd01)):
+            activate(n, 0, 2, tile[:, n // 2, :])
+        nc.vector.tensor_tensor(ac01[:], raw01[:], both_gates(0, 2), MULT)
+        group_tile(2, 6, "late")
+        interleave_pairs(2, 4)
+        interleave_singles(4, 6)
+        quantise(6, 7)
+        quantise(7, 8)
+        quantise(2, 4)
+        quantise(4, 6)
+        scalar_scatter(C, slots(0, 2), ac01[:, 1, :])
+        vector_scatter(A, slots(0, 2), ac01[:, 0, :])
 
-        late = keep.tile([P, 6 * CAP, PACK], BF16, name="late", tag="shared", align_bytes=64)
-        grouped23 = interleave_pairs(2, 4, late[:, slots(0, 2)])
-        grouped45 = interleave_singles(4, 6, late[:, slots(2, 4)])
-        quantised23 = quantise(*grouped23)
-        activate(D, 0, 2, both[:, 0, :])
-        activate(A, 0, 2, both[:, 1, :])
-        nc.vector.tensor_tensor(both[:], both[:], gates[:, 0:PAIR].unsqueeze(1).to_broadcast([P, 2, PAIR]), MULT)
-        grouped67 = interleave_singles(6, 8, late[:, slots(4, 6)])
-        quantised45 = quantise(*grouped45)
-        quantised67 = quantise(*grouped67)
-        activate(B, 0, 2, ys[B])
-        scalar_scatter(C, slots(0, 2), ys[C][:, 0:PAIR])
-        scalar_scatter(D, slots(0, 2), both[:, 0, :])
-        windows[A] = keep.tile([P, T], F32, name="window_a", tag="singles", align_bytes=64)
-        vector_scatter(A, slots(0, 2), both[:, 1, :])
+        bd03 = keep.tile([P, 2, 2 * PAIR], F32, name="bd03", tag="late", align_bytes=64)
+        nc.gpsimd.tensor_tensor(bd03[:, :, 0:PAIR], bd01[:], both_gates(0, 2), MULT)
+        vector_scatter(B, slots(0, 2), bd03[:, 0, 0:PAIR])
 
-        held = keep.tile([P, 5 * PAIR], F32, name="held", tag="shared", align_bytes=64)
-        vector_scatter(*weigh(B, slots(0, 2), held[:, 0:PAIR]))
+        ac47 = keep.tile([P, 2, 2 * PAIR], F32, name="ac47")
+        bd47 = keep.tile([P, 2, 2 * PAIR], F32, name="bd47")
 
-        multiply(quantised23)
-        scalar_scatter(*ready(C, 2, 4, held[:, PAIR : 2 * PAIR]))
-        vector_scatter(*ready(A, 2, 4, held[:, 2 * PAIR : 3 * PAIR]))
-        activate(D, 2, 4, ys[D])
-        vector_scatter(*weigh(D, slice(PAIR, SPLIT), held[:, 3 * PAIR : 2 * PAIR + SPLIT]))
-        b23 = ready(B, 2, 4, held[:, 4 * PAIR : 5 * PAIR])
+        def late(e0, e1):
+            cols = slots(e0 - HALF, e1 - HALF)
+            multiply(e0, e1, (C, A, D, B))
+            for n, tile in ((C, ac47), (A, ac47), (D, bd47), (B, bd47)):
+                activate(n, e0, e1, tile[:, n // 2, cols])
 
-        multiply(quantised45)
-        multiply(quantised67)
-        for n in (C, A, D, B):
-            activate(n, 4, 8, ys[n])
-        vector_scatter(*b23)
-        scalar_scatter(*weigh(C, slots(4, 6)))
-        scalar_scatter(*weigh(C, slots(6, 8)))
+        def weigh(tile, e0, e1):
+            cols = slots(e0 - HALF, e1 - HALF)
+            nc.gpsimd.tensor_tensor(tile[:, :, cols], tile[:, :, cols], both_gates(e0, e1), MULT)
+
+        multiply(2, 4, (A, D, B, C))
+        for n, tile in ((A, ad23), (D, ad23), (B, bc23), (C, bc23)):
+            activate(n, 2, 4, tile[:, n // 2, :])
+        late(4, 6)
+        weighed = keep.tile([P, 2, PAIR], F32, name="weighed", tag="words2", align_bytes=64)
+        windows[D] = keep.tile([P, T], F32, name="window_d", tag="codes4", align_bytes=64)
+        nc.gpsimd.tensor_tensor(bd03[:, :, PAIR : 2 * PAIR], ad23[:], both_gates(2, 4), MULT)
+        nc.gpsimd.tensor_tensor(weighed[:], bc23[:], both_gates(2, 4), MULT)
+        scalar_scatter(D, slice(0, SPLIT), bd03[:, 1, 0:SPLIT])
+        vector_scatter(A, slots(2, 4), bd03[:, 0, PAIR : 2 * PAIR])
+        scalar_scatter(C, slots(2, 4), weighed[:, 1, :])
+        vector_scatter(B, slots(2, 4), weighed[:, 0, :])
+        vector_scatter(D, slice(SPLIT, 2 * PAIR), bd03[:, 1, SPLIT : 2 * PAIR])
+        late(6, 8)
+        weigh(ac47, 4, 6)
+        weigh(bd47, 4, 6)
+        weigh(ac47, 6, 8)
+        weigh(bd47, 6, 8)
+        ys = [ac47[:, 0, :], bd47[:, 0, :], ac47[:, 1, :], bd47[:, 1, :]]
+        scalar_scatter(C, slots(4, 6), ys[C][:, 0:PAIR])
+        scalar_scatter(D, slots(4, 5), ys[D][:, 0:CAP])
+        scalar_scatter(C, slots(6, 8), ys[C][:, PAIR : 2 * PAIR])
         store(C)
-        weigh(A, slots(4, 6))
-        weigh(A, slots(6, 8))
-        vector_scatter(A, slots(4, 8), ys[A][:, slots(4, 8)])
+        vector_scatter(A, slots(4, 8), ys[A])
         store(A)
-        scalar_scatter(*weigh(D, slice(SPLIT, 3 * PAIR)))
-        scalar_scatter(*weigh(D, slots(6, 8)))
+        scalar_scatter(D, slots(5, 8), ys[D][:, CAP : 2 * PAIR])
         store(D, nc.scalar)
-        weigh(B, slots(4, 6))
-        weigh(B, slots(6, 8))
-        vector_scatter(B, slots(4, 8), ys[B][:, slots(4, 8)])
+        vector_scatter(B, slots(4, 8), ys[B])
         store(B)

@@ -88,7 +88,8 @@ def tile_routed_moe_kernel(tc, xT, w_words, w_scales, b, gate, offs, out):
         def sums(n, e):
             return banks[n][e // 2 % 2][:, e // 4 * 2 + e % 2, :]
 
-        pairs = keep.tile([P, 3, PAIR, 2], BF16, name="pairs", align_bytes=64)
+        pairs = keep.tile([P, 8 * CAP, 2], BF16, name="pairs", align_bytes=64)
+        place = {0: 5, 2: 6, 1: 7, 3: 7}
         singles = keep.tile([P, PACK, HALF * CAP], BF16, name="singles", align_bytes=64)
         grouped = {}
 
@@ -99,17 +100,23 @@ def tile_routed_moe_kernel(tc, xT, w_words, w_scales, b, gate, offs, out):
                     grouped[a, z] = tile[:, slots(a - e0, z - e0), :]
 
         def vector_gather(j, e0, e1):
-            start = e0 * CAP if j < 2 else (HALF + e0 % 2) * CAP
-            into = pairs[:].rearrange("p r s i -> p (r s) i")[:, start : start + (e1 - e0) * CAP, j % 2]
+            if j < 2:
+                into = pairs[:, slots(e0, e1), j]
+            elif (e0, e1) == (0, 2):
+                into = pairs[:].rearrange("p (r s) i -> p r s i", s=CAP)[:, place[0] : place[1] + 1 : 2, :, j % 2]
+            else:
+                into = pairs[:, slots(place[e0], place[e0] + e1 - e0), j % 2]
             nc.vector.tensor_copy(into, planes[j][:].indirect(listed(slots(e0, e1))))
 
         def scalar_gather(j):
             nc.scalar.activation(singles[:, j, :], planes[j][:].indirect(listed(slots(HALF, E))), COPY)
 
         def interleave_pairs(e0, e1):
-            part = e0 // 2
-            halves = pairs[:].bitcast(F32)[:, part : 3 : 2 - part, slots(e0 % 2, e0 % 2 + e1 - e0), :]
-            nc.vector.tensor_copy(grouped[e0, e1].bitcast(F32), halves.rearrange("p u s o -> p s (u o)"))
+            count = e1 - e0
+            rows = pairs[:].bitcast(F32).rearrange("p (r s) o -> p r (s o)", s=count * CAP)
+            low, high = e0 // count, place[e0] // count
+            halves = rows[:, low : high + 1 : high - low, :]
+            nc.vector.tensor_copy(grouped[e0, e1].bitcast(F32), halves.rearrange("p u s -> p s u"))
 
         def interleave_singles(e0, e1):
             nc.vector.tensor_copy(
@@ -174,15 +181,16 @@ def tile_routed_moe_kernel(tc, xT, w_words, w_scales, b, gate, offs, out):
         vector_gather(0, 0, HALF)
         vector_gather(1, 0, HALF)
         vector_gather(2, 0, 2)
+        vector_gather(2, 2, 3)
         vector_gather(3, 0, 1)
         vector_gather(3, 1, 2)
         interleave_pairs(0, 1)
         interleave_pairs(1, 2)
         quantise(0, 1)
         quantise(1, 2)
-        vector_gather(2, 2, 4)
+        vector_gather(2, 3, 4)
         vector_gather(3, 2, 4)
-        group_tile(7, 8, "second")
+        group_tile(7, 8, "first")
         nc.gpsimd.tensor_scalar(*some_planes(7, 0, 4), 1.0, 0.0, MULT, ADD)
 
         raw01 = keep.tile([P, 2, PAIR], F32, name="raw01", tag="late", align_bytes=64)
@@ -190,12 +198,13 @@ def tile_routed_moe_kernel(tc, xT, w_words, w_scales, b, gate, offs, out):
         bd01 = keep.tile([P, 2, PAIR], F32, name="bd01")
         ad23 = keep.tile([P, 2, PAIR], F32, name="ad23")
         bc23 = keep.tile([P, 2, PAIR], F32, name="bc23")
-        multiply(0, 2, (A, C, B, D))
-        for n, tile in ((A, raw01), (C, raw01), (B, bd01), (D, bd01)):
-            activate(n, 0, 2, tile[:, n // 2, :])
-        nc.vector.tensor_tensor(ac01[:], raw01[:], both_gates(0, 2), MULT)
+        multiply(0, 2, (C, A, B, D))
+        for n, tile in ((C, raw01[:, 1, :]), (A, ac01[:, 0, :]), (B, bd01[:, 0, :]), (D, bd01[:, 1, :])):
+            activate(n, 0, 2, tile)
+        nc.vector.tensor_tensor(ac01[:, 1, :], raw01[:, 1, :], gates[:, 0:PAIR], MULT)
         group_tile(2, 6, "late")
         interleave_pairs(2, 4)
+        nc.vector.tensor_tensor(ac01[:, 0, :], ac01[:, 0, :], gates[:, 0:PAIR], MULT)
         interleave_singles(4, 6)
         quantise(6, 7)
         quantise(7, 8)

@@ -195,16 +195,18 @@ def tile_routed_moe_kernel(tc, xT, w_words, w_scales, b, gate, offs, out):
 
         raw01 = keep.tile([P, 2, PAIR], F32, name="raw01", tag="late", align_bytes=64)
         ac01 = keep.tile([P, 2, PAIR], F32, name="ac01")
+        raw_a = keep.tile([P, PAIR], F32, name="raw_a", tag="codes2", align_bytes=64)
         bd01 = keep.tile([P, 2, PAIR], F32, name="bd01")
         ad23 = keep.tile([P, 2, PAIR], F32, name="ad23")
         bc23 = keep.tile([P, 2, PAIR], F32, name="bc23")
+        group_tile(2, 4, "third")
+        interleave_pairs(2, 4)
         multiply(0, 2, (C, A, B, D))
-        for n, tile in ((C, raw01[:, 1, :]), (A, ac01[:, 0, :]), (B, bd01[:, 0, :]), (D, bd01[:, 1, :])):
+        for n, tile in ((C, raw01[:, 1, :]), (A, raw_a[:]), (B, bd01[:, 0, :]), (D, bd01[:, 1, :])):
             activate(n, 0, 2, tile)
         nc.vector.tensor_tensor(ac01[:, 1, :], raw01[:, 1, :], gates[:, 0:PAIR], MULT)
-        group_tile(2, 6, "late")
-        interleave_pairs(2, 4)
-        nc.vector.tensor_tensor(ac01[:, 0, :], ac01[:, 0, :], gates[:, 0:PAIR], MULT)
+        group_tile(4, 6, "late")
+        nc.vector.tensor_tensor(ac01[:, 0, :], raw_a[:], gates[:, 0:PAIR], MULT)
         interleave_singles(4, 6)
         quantise(6, 7)
         quantise(7, 8)

@@ -12,6 +12,7 @@ PER_TILE = 4
 HALF = E // 2
 PAIR = 2 * CAP
 A, B, C, D = range(GROUPS)
+LANDING = (2, 3, 0, 1)
 SPLIT = 224
 
 F32 = mybir.dt.float32
@@ -62,9 +63,9 @@ def tile_routed_moe_kernel(tc, xT, w_words, w_scales, b, gate, offs, out):
             nc.sync.dma_start(words[e0 // 2][:].bitcast(I32), w_rows[:, e0:e1, :])
 
         planes = [keep.tile([P, T], F32, name=f"plane{j}") for j in range(PACK)]
-        for j in range(PACK):
+        for j in LANDING:
             nc.sync.dma_start(planes[j][:], x_rows[:, j, :])
-            if j == 0:
+            if j == LANDING[0]:
                 nc.sync.dma_start(offsets[:], offs)
         load_scales(0)
         load_words(0, 2)
@@ -88,8 +89,7 @@ def tile_routed_moe_kernel(tc, xT, w_words, w_scales, b, gate, offs, out):
         def sums(n, e):
             return banks[n][e // 2 % 2][:, e // 4 * 2 + e % 2, :]
 
-        pairs = keep.tile([P, 8 * CAP, 2], BF16, name="pairs", align_bytes=64)
-        place = {0: 5, 2: 6, 1: 7, 3: 7}
+        pairs = keep.tile([P, 7 * CAP, 2], BF16, name="pairs", align_bytes=64)
         singles = keep.tile([P, PACK, HALF * CAP], BF16, name="singles", align_bytes=64)
         grouped = {}
 
@@ -100,22 +100,16 @@ def tile_routed_moe_kernel(tc, xT, w_words, w_scales, b, gate, offs, out):
                     grouped[a, z] = tile[:, slots(a - e0, z - e0), :]
 
         def vector_gather(j, e0, e1):
-            if j < 2:
-                into = pairs[:, slots(e0, e1), j]
-            elif (e0, e1) == (0, 2):
-                into = pairs[:].rearrange("p (r s) i -> p r s i", s=CAP)[:, place[0] : place[1] + 1 : 2, :, j % 2]
-            else:
-                into = pairs[:, slots(place[e0], place[e0] + e1 - e0), j % 2]
+            first = 3 * (j // 2)
+            into = pairs[:, slots(first + e0, first + e1), j % 2]
             nc.vector.tensor_copy(into, planes[j][:].indirect(listed(slots(e0, e1))))
 
         def scalar_gather(j):
             nc.scalar.activation(singles[:, j, :], planes[j][:].indirect(listed(slots(HALF, E))), COPY)
 
         def interleave_pairs(e0, e1):
-            count = e1 - e0
-            rows = pairs[:].bitcast(F32).rearrange("p (r s) o -> p r (s o)", s=count * CAP)
-            low, high = e0 // count, place[e0] // count
-            halves = rows[:, low : high + 1 : high - low, :]
+            rows = pairs[:].bitcast(F32).rearrange("p s o -> p (s o)")[:, slots(e0 // 2, e0 // 2 + 6)]
+            halves = rows.rearrange("p (u s) -> p u s", u=2)[:, :, slots(e0 - e0 // 2, e1 - e0 // 2)]
             nc.vector.tensor_copy(grouped[e0, e1].bitcast(F32), halves.rearrange("p u s -> p s u"))
 
         def interleave_singles(e0, e1):
@@ -143,7 +137,7 @@ def tile_routed_moe_kernel(tc, xT, w_words, w_scales, b, gate, offs, out):
         def multiply(e0, e1, order):
             for n in order:
                 feats = slice(n * P, (n + 1) * P)
-                for e in range(e0, e1):
+                for e in (1, 0) if e0 == 0 else range(e0, e1):
                     nc.tensor.matmul_mx(
                         out=sums(n, e),
                         lhsT=words[e // 2][:, e % 2, feats].bitcast(FP8X4),
@@ -155,7 +149,7 @@ def tile_routed_moe_kernel(tc, xT, w_words, w_scales, b, gate, offs, out):
                     )
 
         def activate(n, e0, e1, into):
-            for e in range(e0, e1):
+            for e in (1, 0) if e0 == 0 else range(e0, e1):
                 nc.scalar.activation(into[:, slots(e - e0, e - e0 + 1)], sums(n, e), GELU, bias=bias[:, n, e : e + 1])
 
         def both_gates(e0, e1):
@@ -170,26 +164,25 @@ def tile_routed_moe_kernel(tc, xT, w_words, w_scales, b, gate, offs, out):
         def store(n, queue=nc.sync):
             queue.dma_start(out[n * P : (n + 1) * P, :], windows[n][:])
 
-        group_tile(0, 1, "first")
-        group_tile(1, 2, "second")
+        group_tile(0, 1, "second")
+        group_tile(1, 2, "first")
         group_tile(6, 7, "sixth")
-        for j in range(PACK):
+        for j in LANDING:
             scalar_gather(j)
-            if j == 1:
-                nc.gpsimd.tensor_scalar(*some_planes(6, 0, 2), 1.0, 0.0, MULT, ADD)
-        nc.scalar.copy(*some_planes(6, 2, 4))
-        vector_gather(0, 0, HALF)
-        vector_gather(1, 0, HALF)
-        vector_gather(2, 0, 2)
-        vector_gather(2, 2, 3)
-        vector_gather(3, 0, 1)
-        vector_gather(3, 1, 2)
-        interleave_pairs(0, 1)
+            if j == 3:
+                nc.gpsimd.tensor_scalar(*some_planes(6, 2, 4), 1.0, 0.0, MULT, ADD)
+        nc.scalar.copy(*some_planes(6, 0, 2))
+        vector_gather(2, 0, HALF)
+        vector_gather(3, 0, HALF)
+        vector_gather(0, 0, 3)
+        vector_gather(1, 1, 2)
+        vector_gather(1, 0, 1)
         interleave_pairs(1, 2)
-        quantise(0, 1)
+        interleave_pairs(0, 1)
         quantise(1, 2)
-        vector_gather(2, 3, 4)
-        vector_gather(3, 2, 4)
+        quantise(0, 1)
+        vector_gather(0, 3, 4)
+        vector_gather(1, 2, 4)
         group_tile(7, 8, "first")
         nc.gpsimd.tensor_scalar(*some_planes(7, 0, 4), 1.0, 0.0, MULT, ADD)
 

@@ -87,7 +87,8 @@ def tile_routed_moe_kernel(tc, xT, w_words, w_scales, b, gate, offs, out):
             return offsets[:, cols.start // 16 : cols.stop // 16]
 
         def sums(n, e):
-            return banks[n][e // 2 % 2][:, e // 4 * 2 + e % 2, :]
+            bank = {C: D, D: C}.get(n, n) if e == 1 else n
+            return banks[bank][e // 2 % 2][:, e // 4 * 2 + e % 2, :]
 
         pairs = keep.tile([P, 7 * CAP, 2], BF16, name="pairs", align_bytes=64)
         singles = keep.tile([P, PACK, HALF * CAP], BF16, name="singles", align_bytes=64)
@@ -194,8 +195,10 @@ def tile_routed_moe_kernel(tc, xT, w_words, w_scales, b, gate, offs, out):
         bc23 = keep.tile([P, 2, PAIR], F32, name="bc23")
         group_tile(2, 4, "third")
         interleave_pairs(2, 4)
-        multiply(0, 2, (C, A, B, D))
-        for n, tile in ((C, raw01[:, 1, :]), (A, raw_a[:]), (B, bd01[:, 0, :]), (D, bd01[:, 1, :])):
+        multiply(0, 2, (C, A, B))
+        activate(C, 0, 2, raw01[:, 1, :])
+        multiply(0, 2, (D,))
+        for n, tile in ((A, raw_a[:]), (B, bd01[:, 0, :]), (D, bd01[:, 1, :])):
             activate(n, 0, 2, tile)
         nc.vector.tensor_tensor(ac01[:, 1, :], raw01[:, 1, :], gates[:, 0:PAIR], MULT)
         group_tile(4, 6, "late")

from contextlib import ExitStack

import concourse.mybir as mybir

K, T, E, N = 512, 1024, 8, 512
CAP = 128
P = 128
PACK = 4
SLOTS = E * CAP
GROUPS = N // P
PER_TILE = 4
HALF = E // 2
PAIR = 2 * CAP
A, B, C, D = range(GROUPS)
LANDING = (2, 3, 0, 1)
SPLIT = 224

F32 = mybir.dt.float32
BF16 = mybir.dt.bfloat16
U32 = mybir.dt.uint32
I32 = mybir.dt.int32
U16 = mybir.dt.uint16
U8 = mybir.dt.uint8
FP8X4 = mybir.dt.float8_e4m3fn_x4
MULT = mybir.AluOpType.mult
ADD = mybir.AluOpType.add
GELU = mybir.ActivationFunctionType.Gelu_apprx_tanh
COPY = mybir.ActivationFunctionType.Copy

FLOPS = 2 * K * N * SLOTS
BYTES = 4 * K * T + E * K * N + E * (K // 32) * N + 4 * N * E + 4 * SLOTS + 2 * 128 * SLOTS // 16 + 4 * N * T


def tile_routed_moe_kernel(tc, xT, w_words, w_scales, b, gate, offs, out):
    nc = tc.nc
    with ExitStack() as ctx:
        keep = ctx.enter_context(tc.tile_pool(name="keep", bufs=1))
        psum = ctx.enter_context(tc.psum_pool(name="psum", bufs=1))

        offsets = keep.tile([P, SLOTS // 16], U16, name="offsets")
        bias = keep.tile([P, GROUPS, E], F32, name="bias")
        gates = keep.tile([P, SLOTS], F32, name="gates")
        warm = keep.tile([P, 1], F32, name="warm")
        w_scale_rows = [keep.tile([P, N], U8, name=f"w_scale_rows{h}", align_bytes=64) for h in range(E // PER_TILE)]

        for tile in w_scale_rows:
            nc.vector.memset(tile[:].bitcast(I32), 0)
        nc.vector.memset(warm[:], 0.0)
        nc.scalar.activation(warm[:], warm[:], GELU)

        x_rows = xT.rearrange("(p j) t -> p j t", j=PACK)
        w_rows = w_words.rearrange("e a p n r -> p (e a) (n r)").bitcast(I32)
        words = [keep.tile([P, 2, N], U32, name=f"words{h}", tag=f"words{h}", align_bytes=64) for h in range(E // 2)]

        def load_scales(h):
            for quad in range(4):
                nc.sync.dma_start(
                    w_scale_rows[h][32 * quad : 32 * quad + 16, :].bitcast(I32),
                    w_scales[PER_TILE * h : PER_TILE * (h + 1), 0, 4 * quad : 4 * quad + 4, :].bitcast(I32),
                )

        def load_words(e0, e1):
            nc.sync.dma_start(words[e0 // 2][:].bitcast(I32), w_rows[:, e0:e1, :])

        planes = [keep.tile([P, T], F32, name=f"plane{j}") for j in range(PACK)]
        for j in LANDING:
            nc.sync.dma_start(planes[j][:], x_rows[:, j, :])
            if j == LANDING[0]:
                nc.sync.dma_start(offsets[:], offs)
        load_scales(0)
        load_words(0, 2)
        nc.sync.dma_start(bias[:], b.rearrange("(c p) e -> p c e", p=P))
        nc.sync.dma_start(gates[:, 0:PAIR], gate[0:P, 0:PAIR])
        load_words(2, 4)
        load_scales(1)
        nc.sync.dma_start(gates[:, PAIR:SLOTS], gate[0:P, PAIR:SLOTS])
        load_words(4, 6)
        load_words(6, 8)

        banks = [[psum.tile([P, PER_TILE, CAP], F32, name=f"bank{n}{h}") for h in range(E // PER_TILE)] for n in range(GROUPS)]
        windows = {n: keep.tile([P, T], F32, name=f"window{n}") for n in (A, B, C)}

        def slots(e0, e1):
            return slice(e0 * CAP, e1 * CAP)

        def listed(cols):
            return offsets[:, cols.start // 16 : cols.stop // 16]

        def sums(n, e):
            bank = {C: D, D: C}.get(n, n) if e == 1 else n
            return banks[bank][e // 2 % 2][:, e // 4 * 2 + e % 2, :]

        pairs = keep.tile([P, 7 * CAP, 2], BF16, name="pairs", align_bytes=64)
        singles = keep.tile([P, PACK, HALF * CAP], BF16, name="singles", align_bytes=64)
        grouped = {}

        def group_tile(e0, e1, tag):
            tile = keep.tile([P, (e1 - e0) * CAP, PACK], BF16, name=f"grouped{e0}", tag=tag, align_bytes=64)
            for a in range(e0, e1):
                for z in range(a + 1, e1 + 1):
                    grouped[a, z] = tile[:, slots(a - e0, z - e0), :]

        def vector_gather(j, e0, e1):
            first = 3 * (j // 2)
            into = pairs[:, slots(first + e0, first + e1), j % 2]
            nc.vector.tensor_copy(into, planes[j][:].indirect(listed(slots(e0, e1))))

        def scalar_gather(j):
            nc.scalar.activation(singles[:, j, :], planes[j][:].indirect(listed(slots(HALF, E))), COPY)

        def interleave_pairs(e0, e1):
            rows = pairs[:].bitcast(F32).rearrange("p s o -> p (s o)")[:, slots(e0 // 2, e0 // 2 + 6)]
            halves = rows.rearrange("p (u s) -> p u s", u=2)[:, :, slots(e0 - e0 // 2, e1 - e0 // 2)]
            nc.vector.tensor_copy(grouped[e0, e1].bitcast(F32), halves.rearrange("p u s -> p s u"))

        def interleave_singles(e0, e1):
            nc.vector.tensor_copy(
                grouped[e0, e1].rearrange("p (c i) j -> p c j i", i=4),
                singles[:, :, slots(e0 - HALF, e1 - HALF)].rearrange("p j (c i) -> p c j i", i=4),
            )

        def some_planes(e, j0, j1):
            source = singles[:, j0:j1, slots(e - HALF, e + 1 - HALF)].rearrange("p j s -> p s j")
            return grouped[e, e + 1][:, :, j0:j1], source

        quantised = {}

        def quantise(e0, e1):
            codes = keep.tile([P, (e1 - e0) * CAP], U32, name=f"codes{e0}", tag=f"codes{e0}", align_bytes=64)
            scales = keep.tile([P, (e1 - e0) * CAP], U8, name=f"scales{e0}", align_bytes=64)
            nc.vector.quantize_mx(
                out=codes[:].bitcast(FP8X4), scales=scales[:], in_=grouped[e0, e1].rearrange("p s j -> p (s j)")
            )
            for e in range(e0, e1):
                own = slots(e - e0, e - e0 + 1)
                quantised[e] = codes[:, own].bitcast(FP8X4), scales[:, own]

        def multiply(e0, e1, order):
            for n in order:
                feats = slice(n * P, (n + 1) * P)
                for e in (1, 0) if e0 == 0 else range(e0, e1):
                    nc.tensor.matmul_mx(
                        out=sums(n, e),
                        lhsT=words[e // 2][:, e % 2, feats].bitcast(FP8X4),
                        lhsT_scale=w_scale_rows[e // PER_TILE][4 * (e % PER_TILE) : P, feats],
                        rhs=quantised[e][0],
                        rhs_scale=quantised[e][1],
                        start=True,
                        stop=True,
                    )

        def activate(n, e0, e1, into):
            for e in (1, 0) if e0 == 0 else range(e0, e1):
                nc.scalar.activation(into[:, slots(e - e0, e - e0 + 1)], sums(n, e), GELU, bias=bias[:, n, e : e + 1])

        def both_gates(e0, e1):
            return gates[:, slots(e0, e1)].unsqueeze(1).to_broadcast([P, 2, (e1 - e0) * CAP])

        def vector_scatter(n, cols, values):
            nc.vector.tensor_copy(windows[n][:].indirect(listed(cols)), values)

        def scalar_scatter(n, cols, values):
            nc.scalar.activation(windows[n][:].indirect(listed(cols)), values, COPY)

        def store(n, queue=nc.sync):
            queue.dma_start(out[n * P : (n + 1) * P, :], windows[n][:])

        group_tile(0, 1, "second")
        group_tile(1, 2, "first")
        group_tile(6, 7, "sixth")
        for j in LANDING:
            scalar_gather(j)
            if j == 3:
                nc.gpsimd.tensor_scalar(*some_planes(6, 2, 4), 1.0, 0.0, MULT, ADD)
        nc.scalar.copy(*some_planes(6, 0, 2))
        vector_gather(2, 0, HALF)
        vector_gather(3, 0, HALF)
        vector_gather(0, 0, 3)
        vector_gather(1, 1, 2)
        vector_gather(1, 0, 1)
        interleave_pairs(1, 2)
        interleave_pairs(0, 1)
        quantise(1, 2)
        quantise(0, 1)
        vector_gather(0, 3, 4)
        vector_gather(1, 2, 4)
        group_tile(7, 8, "first")
        nc.gpsimd.tensor_scalar(*some_planes(7, 0, 4), 1.0, 0.0, MULT, ADD)

        raw01 = keep.tile([P, 2, PAIR], F32, name="raw01", tag="late", align_bytes=64)
        ac01 = keep.tile([P, 2, PAIR], F32, name="ac01")
        raw_a = keep.tile([P, PAIR], F32, name="raw_a", tag="codes2", align_bytes=64)
        bd01 = keep.tile([P, 2, PAIR], F32, name="bd01")
        ad23 = keep.tile([P, 2, PAIR], F32, name="ad23")
        bc23 = keep.tile([P, 2, PAIR], F32, name="bc23")
        group_tile(2, 4, "third")
        interleave_pairs(2, 4)
        multiply(0, 2, (C, A, B))
        activate(C, 0, 2, raw01[:, 1, :])
        multiply(0, 2, (D,))
        for n, tile in ((A, raw_a[:]), (B, bd01[:, 0, :]), (D, bd01[:, 1, :])):
            activate(n, 0, 2, tile)
        nc.vector.tensor_tensor(ac01[:, 1, :], raw01[:, 1, :], gates[:, 0:PAIR], MULT)
        group_tile(4, 6, "late")
        nc.vector.tensor_tensor(ac01[:, 0, :], raw_a[:], gates[:, 0:PAIR], MULT)
        interleave_singles(4, 6)
        quantise(6, 7)
        quantise(7, 8)
        quantise(2, 4)
        quantise(4, 6)
        scalar_scatter(C, slots(0, 2), ac01[:, 1, :])
        vector_scatter(A, slots(0, 2), ac01[:, 0, :])

        bd03 = keep.tile([P, 2, 2 * PAIR], F32, name="bd03", tag="late", align_bytes=64)
        nc.gpsimd.tensor_tensor(bd03[:, :, 0:PAIR], bd01[:], both_gates(0, 2), MULT)
        vector_scatter(B, slots(0, 2), bd03[:, 0, 0:PAIR])

        ac47 = keep.tile([P, 2, 2 * PAIR], F32, name="ac47")
        bd47 = keep.tile([P, 2, 2 * PAIR], F32, name="bd47")

        def late(e0, e1):
            cols = slots(e0 - HALF, e1 - HALF)
            multiply(e0, e1, (C, A, D, B))
            for n, tile in ((C, ac47), (A, ac47), (D, bd47), (B, bd47)):
                activate(n, e0, e1, tile[:, n // 2, cols])

        def weigh(tile, e0, e1):
            cols = slots(e0 - HALF, e1 - HALF)
            nc.gpsimd.tensor_tensor(tile[:, :, cols], tile[:, :, cols], both_gates(e0, e1), MULT)

        multiply(2, 4, (A, D, B, C))
        for n, tile in ((A, ad23), (D, ad23), (B, bc23), (C, bc23)):
            activate(n, 2, 4, tile[:, n // 2, :])
        late(4, 6)
        weighed = keep.tile([P, 2, PAIR], F32, name="weighed", tag="words2", align_bytes=64)
        windows[D] = keep.tile([P, T], F32, name="window_d", tag="codes4", align_bytes=64)
        nc.gpsimd.tensor_tensor(bd03[:, :, PAIR : 2 * PAIR], ad23[:], both_gates(2, 4), MULT)
        nc.gpsimd.tensor_tensor(weighed[:], bc23[:], both_gates(2, 4), MULT)
        scalar_scatter(D, slice(0, SPLIT), bd03[:, 1, 0:SPLIT])
        vector_scatter(A, slots(2, 4), bd03[:, 0, PAIR : 2 * PAIR])
        scalar_scatter(C, slots(2, 4), weighed[:, 1, :])
        vector_scatter(B, slots(2, 4), weighed[:, 0, :])
        vector_scatter(D, slice(SPLIT, 2 * PAIR), bd03[:, 1, SPLIT : 2 * PAIR])
        late(6, 8)
        weigh(ac47, 4, 6)
        weigh(bd47, 4, 6)
        weigh(ac47, 6, 8)
        weigh(bd47, 6, 8)
        ys = [ac47[:, 0, :], bd47[:, 0, :], ac47[:, 1, :], bd47[:, 1, :]]
        scalar_scatter(C, slots(4, 6), ys[C][:, 0:PAIR])
        scalar_scatter(D, slots(4, 5), ys[D][:, 0:CAP])
        scalar_scatter(C, slots(6, 8), ys[C][:, PAIR : 2 * PAIR])
        store(C)
        vector_scatter(A, slots(4, 8), ys[A])
        store(A)
        scalar_scatter(D, slots(5, 8), ys[D][:, CAP : 2 * PAIR])
        store(D, nc.scalar)
        vector_scatter(B, slots(4, 8), ys[B])
        store(B)
